import numpy as np, ml_dtypes
CORES = [113,118,241,246]
N = 4
BF = ml_dtypes.bfloat16
V, M, W, TR, RO, CAP = 448, 224, 4096, 3, 3, 44
def spot(a, b, p, q):
    return ((a * (2 * b + 1) >> 4) + a + p * (2 * b + 613) + q * (2 * a + 37)) & (W - 1)
def look(X, a, b, p, q):
    return np.take_along_axis(X, spot(a, b, p, q).reshape(N, 8, 1, 16 * M), 3).reshape(N, 8, 16, 16, M)
def excess(R, z):
    return np.add.reduce(np.maximum(R - z[:, :, :, None, :], 0), axis=2)
def scan(X, G, B, d, z, t):
    ra = np.arange(N)[:, None, None, None]; ga = np.arange(8)[None, :, None, None]; z = z.astype(np.int32)
    n = np.add.reduce((G >= 0).astype(np.int64), axis=2)
    s = np.where((G >= 0) & ((G & 1) == (t & 1)), n[ra, ga, np.maximum(G, 0)], -1)
    e = np.take_along_axis(G, np.argmax(s, axis=2)[:, :, None, :], 2)[:, :, 0]
    e = np.where(np.max(s, axis=2) >= 0, e, -1)
    v = 2 * np.arange(M) + (t & 1); L = G[..., v]; on = L >= 0; a = np.maximum(L, 0)
    old = d[ra, ga, a]; mine = on & (e[ra, ga, a] == v); dv = d[:, :, v][:, :, None, :]
    new = old; pick = look(X, a, v, old, dv); low = excess(pick, z)
    for j in range(1, TR):
        p = (old + j) & 15; R = look(X, a, v, p, dv); x = excess(R, z); w = mine & (x < low)
        low = np.where(w, x, low); new = np.where(w, p, new); pick = np.where(w[:, :, None], R, pick)
    up = np.max(np.where(on[:, :, None], pick, 0), axis=3)
    o = np.take_along_axis(B, a, 3); both = np.concatenate([d, np.roll(d, -1, axis=0)], axis=2); do = both[ra, ga, o]
    dmg = np.where(on, excess(look(X, o, a, do, new), z) - excess(look(X, o, a, do, old), z), -99999)
    k = np.argmax(dmg, axis=2)[:, :, None, :]
    return n[:, :, v], v, L, a, mine, new, up, np.take_along_axis(dmg, k, 2)[:, :, 0], np.take_along_axis(o, k, 2)[:, :, 0]
def graph(rng, S, share):
    m = np.argsort(rng.random((S, V)), axis=1); i = np.arange(S)[:, None]; mate = np.zeros((S, V), np.int64)
    mate[i, m[:, :M]] = m[:, M:]; mate[i, m[:, M:]] = m[:, :M]
    act = 0.3 + 0.7 * rng.random(V); act[rng.random(V) < 0.04] = 0.0
    r = rng.random((S, V))[i, np.minimum(mate, np.arange(V))]
    return np.where(r < share * act * act[mate], mate, -1)
def tidy(tab):
    tab = np.array(tab, np.int64)
    for k in range(1, len(tab)): tab[k] = np.where(np.any(tab[:k] == tab[k], axis=0), -1, tab[k])
    tab = np.take_along_axis(tab, np.argsort(tab < 0, axis=0, kind="stable"), 0)[:16]
    return np.concatenate([tab, np.full((16 - len(tab), V), -1, np.int64)])
def plain(rng, share):
    return tidy(np.concatenate([np.where(rng.random((1, V)) < 0.15, np.arange(V), -1), graph(rng, 16, share)]))
def blocks(rng, own):
    p = rng.permutation(V).reshape(-1, 16); tab = np.zeros((16, V), np.int64)
    o = np.argsort(rng.random((len(p), 16, 16)), axis=2)
    tab[:, p.reshape(-1)] = p[np.arange(len(p))[:, None, None], o].reshape(-1, 16).T
    return tab if own else tidy(np.where(tab == np.arange(V), -1, tab))
def edges():
    return np.concatenate([np.arange(8), np.arange(V - 8, V)])
def corner(rng):
    c = edges(); tab = c[np.argsort(rng.random((16, V)), axis=0)]
    size = rng.choice(np.array([16, 16, 15, 14, 2, 0]), V); size[c] = rng.choice(np.array([16, 16, 15, 14]), 16)
    tab[:2, size == 2] = np.array([[0], [V - 1]])
    for u in (0, V - 1): tab[:, u] = np.concatenate([[V - 2], rng.permutation(c[c != V - 2])])
    tab[:, V - 2] = np.concatenate([[0], rng.permutation(c[1:15]), [V - 1]]); size[[0, V - 2, V - 1]] = 16
    return np.where(np.arange(16)[:, None] < size, tab, -1)
def lift(rng, rec, z, a, v, dv, o, do):
    def ex(x): return np.add.reduce(np.maximum(rec[:, x] - z.reshape((16,) + (1,) * (x.ndim - 1) + (-1,)), 0), axis=0)
    p = np.arange(16)[:, None]; E = ex(spot(a, v, p, dv))
    new = (p + np.argmin(np.stack([np.roll(E, -j, axis=0) for j in range(TR)]), axis=0)) & 15
    F = ex(spot(o[:, None], a, do[:, None], p))
    D = np.take_along_axis(F, np.broadcast_to(new, F.shape), 1) - F
    s = np.where(D > 0, 1 + rng.random(D.shape) + 2 * (np.arange(len(o))[:, None, None] == 0), 0)
    b = np.argmax(s.reshape(-1, s.shape[-1]), axis=0)
    return b & 15, b >> 4
def parts(rng):
    gl = np.stack([np.stack([plain(rng, float(rng.choice(np.array([0.7, 1.0, 1.5, 2.5])))) for g in range(8)]) for r in range(N)])
    rec = (256 * rng.random((N, 8, 16, W)) * (0.4 + 0.6 * rng.random((N, 8, 1, W)))).astype(np.int64)
    val = rng.integers(0, 16, (N, 8, V)); zl = (256 * rng.random((N, 8, 16, M)) ** 1.5).astype(np.int64)
    th = (rng.choice(np.array([4, 40, 200, 1000]), (N, 8, M)) * rng.random((N, 8, M))).astype(np.int64)
    gs = rng.choice(np.array([0.3, 0.5, 0.8]), (N, 8, 1, 1)); full = rng.integers(0, 8, N); gs[np.arange(N), full] = 1.0; th[np.arange(N), full] = rng.integers(0, 8, (N, M))
    nb = rng.integers(0, V, (N, 8, 16, V)) + V * (rng.random((N, 8, 16, V)) < gs)
    return rec, gl, nb, val, zl, th
def pack(rec, gl, nb, val, zl, th):
    return {"rec": rec.reshape(N, 128, W).astype(np.float32).astype(BF), "gl": np.ascontiguousarray(gl.reshape(N, 128, V)).astype(np.int32), "nb": np.ascontiguousarray(nb.reshape(N, 128, V)).astype(np.int32),
            "val": val.astype(np.int32), "zl": zl.reshape(N, 128, M).astype(np.float32).astype(BF), "th": th.astype(np.int32)}
def largest(rec, gl, nb, val, zl):
    return scan(rec.astype(np.int32), gl, nb, val, zl, 0)[7]
def tune(rng, top, want):
    pos = np.argsort(np.argsort(np.where(top > 0, rng.random(top.shape), 2.0), axis=2), axis=2); sel = (pos < want) & (top > 0); coin = rng.random(top.shape)
    low = np.where(coin < 0.5, top - 1, (rng.random(top.shape) * top).astype(np.int64))
    return np.where(sel, low, np.where(coin < 0.1, 4080, np.maximum(top, 0)))
def setup_inputs(rng):
    return pack(*parts(rng))
def setup_inputs_spread(rng):
    rec, gl, nb, val, zl, th = parts(rng)
    rec = (np.exp2(8 * rng.random((N, 8, 1, W))) * rng.random((N, 8, 16, W))).astype(np.int64)
    zl = (np.exp2(8 * rng.random((N, 8, 1, M))) * rng.random((N, 8, 16, M))).astype(np.int64)
    th = np.minimum((np.exp2(12 * rng.random((N, 8, M)) ** 1.5) - 1).astype(np.int64), 4080)
    nb = (2 * V * rng.random((N, 8, 16, V)) ** 1.5).astype(np.int64); val = (16 * rng.random((N, 8, V)) ** 2).astype(np.int64)
    return pack(rec, gl, nb, val, zl, th)
def setup_inputs_ends(rng):
    rec, gl, nb, val, zl, th = parts(rng)
    rec = 255 * np.where(rng.random((N, 8, 1, W)) < 0.8, rng.integers(0, 2, (N, 8, 1, W)), rng.integers(0, 2, (N, 8, 16, W)))
    val = 15 * rng.integers(0, 2, (N, 8, V)); th = 4080 * (rng.random((N, 8, M)) < 0.4).astype(np.int64)
    zl = 255 * np.where(rng.random((N, 8, 1, M)) < 0.6, rng.random((N, 8, 1, M)) < 0.35, rng.random((N, 8, 16, M)) < 0.35).astype(np.int64)
    e = rng.random((N, 8, 16, V)); nb = np.where(e < 0.4, 0, np.where(e < 0.85, 2 * V - 1, nb))
    for r in range(N):
        few = [6, 7] + [int(g) for g in rng.permutation(6)[:2]]
        for g in range(8):
            gl[r, g] = corner(rng) if g in few else tidy(np.concatenate([graph(rng, 14, 1.5), np.zeros((1, V), np.int64), np.full((1, V), V - 1, np.int64)]))
    for g in (6, 7):
        val[:, g, 0] = 15; val[:, g, V - 2] = 0; val[:, g, V - 1] = 0; zl[:, g, :, M - 1] = 0
        th[:, g, M - 1] = np.where(np.arange(N) % 2 == 1, 0, 4080)
        nb[:, g, 15, V - 1] = 2 * V - 1; nb[:, g, 0, 0] = 0 if g == 7 else 2 * V - 1
        hi = [spot(0, V - 2, 15, 0), spot(V - 1, V - 2, 0, 0), spot(2 * V - 1, V - 1, 0, 1), spot(0, 0, 15, 0) if g == 7 else spot(2 * V - 1, 0, 0, 15)]
        lo = [spot(0, V - 2, 0, 0), spot(V - 1, V - 2, 1, 0), spot(2 * V - 1, V - 1, 0, 0), spot(0, 0, 15, 15) if g == 7 else spot(2 * V - 1, 0, 0, 0)]
        for x in lo: rec[:, g, :, x] = 0
        for x in hi: rec[:, g, :, x] = 255
    return pack(rec, gl, nb, val, zl, th)
def setup_inputs_corners(rng):
    rec, gl, nb, val, zl, th = parts(rng); c = edges(); late = []
    for r in range(N):
        for g, k in enumerate(rng.permutation(8)):
            if k == 0:
                ev = np.concatenate([[V - 2], 2 * rng.permutation(M - 1)]); od = 2 * rng.permutation(M) + 1; h = M // 2
                tab = np.full((16, V), -1, np.int64)
                tab[0, ev[:h]] = od[:h]; tab[0, od[:h]] = ev[:h]; tab[0, od[h:]] = ev[:h]; tab[1, od[h:]] = ev[h:]; tab[0, ev[h:]] = od[h:]
                late.append((r, g, ev[:h], od[:h], od[h:]))
            elif k == 1: tab = blocks(rng, True)
            elif k == 2: tab = blocks(rng, False)
            elif k == 3:
                tab = graph(rng, 16, 2.0); tab = tidy(np.where((tab & 1 == 1) & (np.arange(V) & 1 == 1), tab, -1))
            elif k == 4:
                tab = graph(rng, 16, 2.0); off = rng.random(V) < 0.5; tab = tidy(np.where(off | off[tab], -1, tab))
            elif k == 5:
                tab = np.argsort(rng.random((V, V)), axis=1)[:, :16].T; tab = np.where(np.arange(16)[:, None] < rng.integers(0, 17, V), tab, -1)
            elif k == 6:
                tab = c[np.argsort(rng.random((16, V)), axis=0)]; tab[:, c] = np.argsort(rng.random((16, V)), axis=1)[:, :16].T
            else: tab = plain(rng, 1.5)
            gl[r, g] = tab
    m = np.arange(V); e = rng.integers(0, 10, (N, 8, 16, V))
    for k, x in enumerate((0, V - 1, V, 2 * V - 1, m, m + V)): nb = np.where(e == k, x, nb)
    e = rng.integers(0, 4, (N, 8, V)); val = np.where(e == 0, 0, np.where(e == 1, 15, val))
    e = rng.integers(0, 6, (N, 8, 1, M)); zl = np.where(e == 0, 0, np.where(e == 1, 255, zl >> 1))
    want = rng.choice(np.array([0, 1, CAP - 1, CAP, CAP + 1, M]), (N, 8, 1))
    for r, g, v, a, o in late:
        zl[r, g, :, M - 1] = 0; dv = val[r, g, v]; do = val[r, g, o]; q = (np.arange(16) + 1) & 15
        x = spot(a[0], v[0], np.arange(16), dv[0]); y = spot(o[0], a[0], do[0], np.arange(16))
        s = int(np.argmax((x != y) & (x[q] != y[q]))); u = int(q[s])
        rec[r, g, :, int(x[s])] = 255; rec[r, g, :, int(y[u])] = 255; rec[r, g, :, int(x[u])] = 0; rec[r, g, :, int(y[s])] = 0
        p = lift(rng, rec[r, g], zl[r, g][:, v >> 1], a, v, dv, o[None], do[None])[0]
        val[r, g, a] = p; val[r, g, a[0]] = s; nb[r, g][:, a] = o; want[r, g, 0] = M
    th = tune(rng, largest(rec, gl, nb, val, zl), want)
    for r, g, v, a, o in late: th[r, g, M - 1] = 4079
    return pack(rec, gl, nb, val, zl, th)
def setup_inputs_crowd(rng):
    rec, gl, nb, val, zl, th = parts(rng); zl = zl >> 1; ev = 2 * np.arange(M)
    spots = np.array([V, 2 * V - 1, V + M]); cnt = np.array([CAP, CAP + 1, CAP - 1, M, CAP + 1]); want = np.zeros((N, 8, 1), np.int64)
    for r in range(N):
        most = ((2, 3), (4, 5), (3, 2), (5, 4))[r % 4]
        left = [g for g in range(1, 8) if g not in most]
        want[r, left, 0] = cnt if r == 0 else rng.permutation(cnt)
        want[r, most[0], 0] = M; want[r, most[1], 0] = M - 1
        for g in range(8):
            gl[r, g] = plain(rng, 1.5); s = int(rng.choice(spots))
            if g in most:
                od = 2 * rng.permutation(M) + 1; tab = np.full((16, V), -1, np.int64); tab[0, ev] = od; tab[0, od] = ev; gl[r, g] = tab
                o = np.tile(rng.permutation(spots)[:, None], (1, M))
                p, k = lift(rng, rec[r, g], zl[r, g], od, ev, val[r, g, ev], o, val[(r + 1) % N, g][o - V])
                val[r, g, od] = p; nb[r, g] = o[0, 0]; nb[r, g][:, od] = o[k, np.arange(M)]
            elif g == 0: nb[r, g] = (0, V - 1)[r % 2]
            elif g < 5: nb[r, g] = s
            elif g == 5: nb[r, g] = rng.choice(spots, (16, V))
            else: nb[r, g] = np.where(rng.random((16, V)) * CAP < 1, 2 * V - 1 if s == V else V, s)
    top = largest(rec, gl, nb, val, zl); got = np.minimum(np.add.reduce((top > 0).astype(np.int64), axis=2), want[:, :, 0])
    for r in range(N): want[r, 0, 0] = ((31, 0)[r % 2] - int(np.add.reduce(got[r, 1:]))) & 31
    return pack(rec, gl, nb, val, zl, tune(rng, top, want))
def check_inputs(d):
    bad = []
    for k, lo, hi in (("rec", 0, 255), ("gl", -1, V - 1), ("nb", 0, 2 * V - 1), ("val", 0, 15), ("zl", 0, 255), ("th", 0, 4080)):
        x = np.asarray(d[k]).astype(np.float64)
        if not (np.min(x) >= lo and np.max(x) <= hi): bad.append("range of " + k)
        if np.any(x != np.floor(x)): bad.append("whole numbers in " + k)
    g = np.asarray(d["gl"]).reshape(N, 8, 16, V); on = g >= 0; s = np.sort(g, axis=2)
    if np.any(on[:, :, 1:] & ~on[:, :, :-1]): bad.append("gl: a name after an empty slot")
    if np.any((s[:, :, 1:] == s[:, :, :-1]) & (s[:, :, 1:] >= 0)): bad.append("gl: a name twice in one list")
    return bad
def reference(rec, gl, nb, val, zl, th):
    X = rec.astype(np.float32).astype(np.int32).reshape(N, 8, 16, W); G = gl.astype(np.int64).reshape(N, 8, 16, V); B = nb.astype(np.int64).reshape(N, 8, 16, V)
    d = val.astype(np.int64); z = zl.astype(np.float32).astype(np.int32).reshape(N, 8, 16, M); h = th.astype(np.int64); c = np.zeros((N, 1, 1), np.int64)
    for t in range(RO):
        n, v, L, a, mine, new, up, top, who = scan(X, G, B, d, z, t)
        hurt = top > h + (c & 31)
        c = np.add.reduce(hurt.astype(np.int64).reshape(N, 8 * M), axis=1).reshape(N, 1, 1)
        z = np.roll((z + up) >> 1, 1 + t, axis=0)
        w = np.nonzero(mine); d = d + 0; d[w[0], w[1], a[w]] = new[w]
        gh = (hurt & (who >= V)).astype(np.int64); told = (gh == 1) & (np.add.accumulate(gh, axis=2) - gh < CAP)
        w = np.nonzero(told); np.add.at(d, ((w[0] + 1) % N, w[1], who[w] - V), 1); d = d & 15
        w = np.nonzero(hurt & (who < V) & (n < 16) & ~np.any(L == who[:, :, None, :], axis=2))
        G[w[0], w[1], n[w], v[w[2]]] = who[w]
    return {"yl": G.reshape(N, 128, V).astype(np.float32), "yd": d.astype(np.float32), "yz": z.reshape(N, 128, M).astype(np.float32).astype(BF)}

@@ -1,0 +1,876 @@
+from concourse.mybir import AluOpType, AxisListType, ActivationFunctionType
+
+V, M, W, RO, CAP = 448, 224, 4096, 3, 44
+CELLS = 16 * M
+WIN = CELLS + V
+CH = 1792
+
+
+def bf(n): return ("sbuf", [128, n], "bfloat16")
+def f4(n): return ("sbuf", [128, n], "float32")
+def i4(n): return ("sbuf", [128, n], "int32")
+def u2(n): return ("sbuf", [128, n], "uint16")
+
+
+SCRATCH = {
+    "GI": i4(V), "NBI": i4(V), "VI": ("sbuf", [8, V], "int32"), "THI": ("sbuf", [8, M], "int32"), "Z0": bf(M),
+    "REC": bf(W + 16), "NW": bf(2 * CELLS), "KW": bf(2 * CELLS), "KC": bf(464), "KT": bf(2 * CH), "WR": bf(WIN), "WP": bf(WIN),
+    "GF": f4(464), "GU": u2(V), "G0": bf(V), "NBD": bf(2 * V), "NBT": i4(2 * V),
+    "VB": ("sbuf", [8, V], "bfloat16"), "THT": ("sbuf", [8, 2 * M], "int32"), "THB": ("sbuf", [8, 2 * M], "bfloat16"),
+    "TN": bf(464), "X34": bf(1024), "TE": bf(912), "ID": bf(912),
+    "IOQ": i4(8), "COL": f4(32), "IOM": f4(128), "IOX": f4(464), "IOC": f4(28), "S1": f4(4 * M), "IO8": f4(16),
+    "RA": bf(CH), "RM": bf(CH), "CK": bf(512), "J84": bf(84), "PATP": f4(256), "PATC": f4(V), "LPI": i4(16),
+    "LPC": u2(44), "SELS": bf(64), "ONE": bf(128), "UPR": bf(128), "IDN": bf(128), "E8": ("sbuf", [8, 128], "bfloat16"),
+    "EJ": ("sbuf", [32, 128], "bfloat16"), "EE0": ("sbuf", [32, 128], "bfloat16"), "EE": ("sbuf", [32, 2048], "bfloat16"),
+    "BD": bf(128), "MM": bf(1024),
+    "LW": bf(2048), "LW4": bf(2048), "LWE0": bf(2048), "LWE1": bf(2048), "LWD": bf(2048), "LWN": bf(2048),
+    "LWK": bf(2048), "LWO": bf(2048), "DA2": bf(2048), "W32": f4(32), "B32": f4(32), "TH0": f4(32), "THC": f4(32),
+    "MAT": bf(V), "NG": bf(V), "INL": bf(V), "MSK": bf(2 * V), "OG": bf(V), "OA": f4(V), "NVO": bf(2 * V), "KV": bf(V),
+    "PAY": bf(V), "GD": bf(2 * V), "ZE": bf(V), "MT": bf(3 * V), "RP": bf(V), "MN": bf(V), "MO": bf(V), "NMO": bf(V),
+    "SI": i4(M), "SF": f4(6 * M), "ISL": u2(M), "OHN": f4(M), "UPD": f4(M), "ZH": f4(M), "ZI": i4(M),
+    "SC": f4(512), "IT": f4(14 * 32), "II": i4(4 * 32), "IBC": bf(64), "XX": bf(64), "XT": ("sbuf", [32, M], "bfloat16"),
+    "OHP": bf(256), "OHC": bf(V), "DT": bf(64), "CF": f4(4), "CI": i4(4),
+    "DF": f4(28 * 104), "DN": i4(28 * 72), "DU": u2(28 * 64), "DB": bf(32 * 12),
+    "PA": ("psum", [128, 512], "float32"), "PB": ("psum", [128, 512], "float32"), "PC": ("psum", [128, 512], "float32"),
+    "PD": ("psum", [128, 512], "float32"), "PK": ("psum", [128, 512], "float32"), "PN": ("psum", [128, 512], "float32"),
+    "PS": ("psum", [128, 512], "float32"), "PJ": ("psum", [128, 512], "float32"),
+}
+for _t in range(3):
+    SCRATCH["WD%d" % _t] = bf(WIN)
+    SCRATCH["LG%d" % _t] = bf(32)
+    SCRATCH["LN%d" % _t] = bf(32)
+    SCRATCH["LZ%d" % _t] = bf(M)
+    SCRATCH["ZB%d" % _t] = bf(M)
+SEMAPHORES = ["cv", "cs", "ct", "cg"] + ["dma%d" % k for k in range(40)] + ["rg%d" % k for k in range(3)] + \
+    ["rn%d" % k for k in range(3)] + ["rz%d" % k for k in range(3)] + ["ls%d" % k for k in range(9)]
+ALIAS = {"SELD": ("SELS", 0), "SELP": ("SELS", 16), "SELT": ("SELS", 32), "SELU": ("SELS", 48), "IB": ("IBC", 0), "CB": ("IBC", 32),
+         "LP": ("LPC", 0), "LC": ("LPC", 16), "R2B": ("MM", 0), "LOA": ("MM", 128), "IP": ("MM", 256), "N0W": ("MM", 384),
+         "N1W": ("MM", 512), "I3": ("MM", 640), "I4": ("MM", 768), "YD": ("SF", 0), "YL": ("SF", 448)}
+PSUM = {"PA", "PB", "PC", "PD", "PK", "PN", "PS", "PJ"}
+
+
+def builder(g, T):
+    eng = {"v": g.vector, "s": g.scalar, "t": g.tensor, "g": g, "y": g.sync}
+    cnt = {"v": 0, "s": 0, "t": 0, "g": 0, "dma": 0, "ls": 0}
+    known = {q: {} for q in eng}
+    log = {}
+    total = {}
+
+    def wait(q, evs):
+        k = known[q]
+        top = {}
+        for e in evs:
+            if k.get(e[0], 0) < e[1] and (e[0] not in top or top[e[0]][1] < e[1]): top[e[0]] = e
+        for e in sorted(top.values(), key=lambda e: -sum(e[2].values())):
+            if k.get(e[0], 0) >= e[1]: continue
+            eng[q].wait_ge(T.sem[e[0]], e[1])
+            k[e[0]] = e[1]
+            for s, n in e[2].items():
+                if k.get(s, 0) < n: k[s] = n
+
+    def deps(q, outs, ins, comp):
+        evs = []
+        for regs, w in ((ins, False), (outs, True)):
+            for b, lo, hi in regs:
+                for r in log.get(b, []):
+                    same = comp and r[3] == q
+                    if b in PSUM:
+                        if not same or (q != "t" and (w or r[2])): evs.append(r[4])
+                    elif r[0] < hi and lo < r[1] and (w or r[2]):
+                        if same and (q == "t" or not r[2]): continue
+                        evs.append(r[4])
+        return evs
+
+    def note(q, outs, ins, ev):
+        for regs, w in ((ins, False), (outs, True)):
+            for b, lo, hi in regs:
+                L = log.setdefault(b, [])
+                if b in PSUM: L[:] = [r for r in L if r[3] != q or r[2] != w]
+                else: L[:] = [r for r in L if not (lo <= r[0] and r[1] <= hi and (w or (not r[2] and r[3] == q and q in "vstg")))]
+                L.append((lo, hi, w, q, ev))
+
+    def emit(q, outs, ins, call):
+        wait(q, deps(q, outs, ins, True))
+        cnt[q] += 1
+        s = "c" + q
+        call().then_inc(T.sem[s], 1)
+        total[s] = cnt[q]
+        note(q, outs, ins, (s, cnt[q], dict(known[q])))
+
+    def dma(q, out, in_):
+        wait(q, deps("d" + q, out[1], in_[1], False))
+        s = "dma%d" % cnt["dma"]
+        cnt["dma"] += 1
+        eng[q].dma_start(out[0], in_[0]).then_inc(T.sem[s], 16)
+        total[s] = 16
+        note("d" + s, out[1], in_[1], (s, 16, dict(known[q])))
+
+    def send(out, in_, sem, to):
+        wait("g", deps("r", [], in_[1], False))
+        s = "ls%d" % cnt["ls"]
+        cnt["ls"] += 1
+        g.remote_dma(out[0], in_[0], T.sem[sem], T.sem[s], to[1], to[0], to[2])
+        total[s] = to[3]
+        note("r" + s, [], in_[1], (s, to[3], dict(known["g"])))
+
+    def arrive(view, sem, n):
+        total[sem] = n
+        for b, lo, hi in view[1]: log.setdefault(b, []).append((lo, hi, True, "x" + sem, (sem, n, {})))
+
+    def finish():
+        wait("y", [(s, n, {}) for s, n in sorted(total.items())])
+
+    return emit, dma, send, arrive, finish
+
+
+def rank_program(g, core, T, topo):
+    rank = T.rank_of(core)
+    if rank is None: return
+    N = len(T.cores)
+    A, F = AluOpType, ActivationFunctionType
+    emit, dma, send, arrive, finish = builder(g, T)
+
+    def B(n, lo, hi, st=1, p=128):
+        if n in ALIAS: n, lo, hi = ALIAS[n][0], lo + ALIAS[n][1], hi + ALIAS[n][1]
+        ap = T[n][0:p, lo:hi] if st == 1 else T[n][0:p, lo:hi:st]
+        return (ap, [(n, lo, hi)])
+
+    def P4(n, p0, p1, lo, hi): return (T[n][p0:p1, lo:hi], [(n, lo, hi)])
+    def ind(win, off): return (win[0].indirect(off[0]), win[1] + off[1])
+    def num(s): return (s, []) if s is None or isinstance(s, (int, float)) else s
+    def tt(o, a, b, op): emit("v", o[1], a[1] + b[1], lambda: g.vector.tensor_tensor(o[0], a[0], b[0], op))
+    def cp(o, a): emit("v", o[1], a[1], lambda: g.vector.tensor_copy(o[0], a[0]))
+
+    def ts(o, a, s1, op0, s2=None, op1=None):
+        x, y = num(s1), num(s2)
+        if op1 is None: emit("v", o[1], a[1] + x[1], lambda: g.vector.tensor_scalar(o[0], a[0], x[0], None, op0))
+        else: emit("v", o[1], a[1] + x[1] + y[1], lambda: g.vector.tensor_scalar(o[0], a[0], x[0], y[0], op0, op1))
+
+    def scan(o, a, b, op0, op1): emit("v", o[1], a[1] + b[1], lambda: g.vector.tensor_tensor_scan(o[0], a[0], b[0], 0.0, op0, op1))
+    def fill(o, c): emit("v", o[1], [], lambda: g.vector.memset(o[0], c))
+
+    def act(o, a, scale=1.0, bias=0.0, relu=False):
+        x, y = num(scale), num(bias)
+        fn = F.Relu if relu else F.Copy if y[0] == 0.0 and not y[1] else F.Identity
+        emit("s", o[1], a[1] + x[1] + y[1], lambda: g.scalar.activation(o[0], a[0], fn, bias=y[0], scale=x[0]))
+
+    def mm(o, l, r, start, stop): emit("t", o[1], l[1] + r[1], lambda: g.tensor.matmul(o[0], l[0], r[0], start, stop))
+    def iota(o, pat, base, cm): emit("g", o[1], [], lambda: g.iota(o[0], pat, base, cm, allow_small_or_imprecise_dtypes=True))
+    def asel(o, a, pat, op, base, cm): emit("g", o[1], a[1], lambda: g.affine_select(o[0], a[0], pat, op, 0.0, base, cm))
+    def mat(n, p, k=128): return (T[n][0:k, p * 128:p * 128 + 128], [(n, p * 128, p * 128 + 128)])
+
+    def dist(o, n, src, base, st, cols, first=True):
+        for p in range(16):
+            lo = base + p
+            mm(o, mat(n, p), B(src, lo, lo + (cols - 1) * st + 1, st), first and p == 0, p == 15)
+
+    def spread(src, first):
+        for p in range(16): mm(B("PA", p, p + 433, 16), mat("DA2", p), src, first, first or p == 15)
+
+    slots = {}
+
+    def slot(buf, width):
+        def f(name):
+            k = (buf, name[:-1] + "0" if name[-1] == "2" and buf != "DB" else name)
+            if k not in slots: slots[k] = sum(1 for x in slots if x[0] == buf)
+            return B(buf, slots[k] * width, slots[k] * width + 28)
+        return f
+
+    DF, DN, DU, DB = slot("DF", 28), slot("DN", 28), slot("DU", 28), slot("DB", 32)
+
+    def wide(f, n, s):
+        vs = [f("%s%d%s" % (n, j, s)) for j in range(3)]
+        return B(vs[0][1][0][0], vs[0][1][0][1], vs[2][1][0][2])
+
+    def out32(name):
+        b, lo, hi = DB(name)[1][0]
+        return B(b, lo, lo + 32)
+
+    def lanes(src, dst): return topo.engines(src, dst)[:8]
+
+    def route(dst):
+        c = T.cores[dst % N]
+        rid, pid = topo.addr(c, core)
+        return (rid, pid, sum(1 << e for e in lanes(core, c)), len(lanes(core, c)))
+
+    def came(src, view, sem): arrive(view, sem, len(lanes(T.cores[src % N], core)))
+
+    col = lambda j, p=128: B("COL", j, j + 1, 1, p)
+    dma("y", B("GI", 0, V), (T.gl[:, :], []))
+    dma("y", B("VI", 0, V, 1, 8), (T.val[:, :], []))
+    dma("y", B("NBI", 0, V), (T.nb[:, :], []))
+    dma("y", B("Z0", 0, M), (T.zl[:, :], []))
+    dma("y", B("REC", 0, W), (T.rec[:, :], []))
+    dma("y", B("THI", 0, M, 1, 8), (T.th[:, :], []))
+    for t in range(3):
+        came(rank + 1, B("LG%d" % t, 0, 32), "rg%d" % t)
+        came(rank - 1, B("LN%d" % t, 0, 32), "rn%d" % t)
+        came(rank - 1 - t, B("LZ%d" % t, 0, M), "rz%d" % t)
+    iota(B("IOQ", 0, 1), [[0, 1]], 0, 1)
+    iota(B("IOM", 0, 128), [[1, 8], [0, 16]], 0, 0)
+    fill(B("ONE", 0, 128), 1.0)
+    fill(B("WD0", 0, CH), 0.0)
+    asel(B("IDN", 0, 128), B("ONE", 0, 128), [[1, 128]], A.is_equal, 0, -1)
+    iota(B("X34", 0, 512), [[256, 2], [0, 256]], 0, 0)
+    iota(B("X34", 512, 1024), [[0, 2], [1, 256]], 0, 0)
+    iota(B("IOX", 0, 464), [[1, 464]], 0, 0)
+    asel(B("E8", 0, 128, 1, 8), B("ONE", 0, 128, 1, 8), [[1, 128]], A.is_equal, -2, -16)
+    iota(B("IOC", 0, 28), [[16, 28]], 0, 0)
+    ts(B("IOQ", 1, 2), B("IOQ", 0, 1), 15, A.bitwise_and)
+    ts(B("IOQ", 2, 3), B("IOQ", 0, 1), 4, A.arith_shift_right)
+    cp(col(0), B("IOQ", 1, 2))
+    cp(col(1), B("IOQ", 2, 3))
+    ts(B("BD", 0, 128), B("IOM", 0, 128), col(1), A.is_equal)
+    for j in range(5): ts(col(4 + j), col(0), float(j), A.is_equal)
+    ts(col(9), col(4), -128.0, A.mult)
+    ts(col(11), col(5), -256.0, A.mult, col(9), A.add)
+    ts(col(10), col(4), -256.0, A.mult)
+    ts(col(14), col(5), -128.0, A.mult, col(10), A.add)
+    ts(col(17), col(4), col(5), A.add)
+    ts(B("TN", 0, 1), col(17), -256.0, A.mult)
+    fill(B("TN", V + 1, 464), 0.0)
+    fill(B("N0W", 0, 256), 0.0)
+    ts(B("N0W", 0, 113, 16), B("BD", 0, 113, 16), 16.0, A.mult)
+    ts(B("N1W", 1, 114, 16), B("BD", 0, 113, 16), 16.0, A.mult)
+    ts(B("R2B", 0, 128), B("BD", 0, 128), col(6), A.mult)
+    ts(B("I3", 0, 128), B("IDN", 0, 128), col(7), A.mult)
+    ts(B("I4", 0, 128), B("IDN", 0, 128), col(8), A.mult)
+    ts(B("G0", 0, V), B("GI", 0, V), 0.0, A.is_ge)
+    ts(B("GU", 0, M), B("GI", 0, V - 1, 2), 1.0, A.add)
+    ts(B("GU", M, V), B("GI", 1, V, 2), 1.0, A.add)
+    cp(B("VB", 0, V, 1, 8), B("VI", 0, V, 1, 8))
+
+    def sizes(last):
+        mm(B("PA", 0, V), B("I3", 0, 128), B("X34", 1, V + 1), True, False)
+        mm(B("PA", 0, V), B("I4", 0, 128), B("X34", 513, 513 + V), False, False)
+        mm(B("PA", 0, V - 1, 2), B("N0W", 0, 128), B("G0", 0, V - 1, 2), False, False)
+        mm(B("PA", 1, V, 2), B("N1W", 0, 128), B("G0", 1, V, 2), False, last)
+
+    sizes(False)
+    mm(B("PA", 0, V), B("E8", 0, 128, 1, 8), B("VB", 0, V, 1, 8), False, True)
+    ts(B("TN", 1, V, 2), B("PA", 0, V - 1, 2), col(11), A.add)
+    ts(B("TN", 2, V + 1, 2), B("PA", 1, V, 2), col(14), A.add)
+    TNW = B("TN", 0, 464)
+
+    def table(values, alone=False):
+        if alone:
+            spread(B("DT", 0, 28), True)
+            act(B("TN", 1, V + 1), B("PA", 0, V))
+            return
+        sizes(not values)
+        if values: spread(B("DT", 0, 28), False)
+        act(B("TN", 1, V, 2), B("PA", 0, V - 1, 2), bias=col(11))
+        act(B("TN", 2, V + 1, 2), B("PA", 1, V, 2), bias=col(14))
+
+    def sgather(c0, c1): act(B("KW", 16 * c0, 16 * c1), ind(TNW, B("GU", c0, c1)))
+    def vgather(c0, c1): cp(B("KW", 16 * c0, 16 * c1), ind(TNW, B("GU", c0, c1)))
+    turn = [0]
+
+    def half():
+        turn[0] ^= 1
+        return turn[0] * CH
+
+    def scans(lo, hi):
+        while lo < hi:
+            n, b = min(CH, hi - lo), half()
+            scan(B("KT", b, b + n), B("RA", 0, n), B("KW", lo, lo + n), A.add, A.max)
+            cp(B("KC", lo // 16, (lo + n) // 16), B("KT", b + 15, b + n, 16))
+            lo += n
+
+    CUT = 320
+    for c in range(0, CUT, 80): sgather(c, c + 80)
+    fill(B("LW", 0, 2048), 0.0)
+    for a in range(8): cp(B("LW", 16 * a, 16 * a + 129 * 15 + 1, 129), B("BD", 16 * a, 16 * a + 16))
+    for n, op, b in (("LWD", A.is_equal, -2), ("LWN", A.is_ge, -3)):
+        asel(B(n, 0, 2048), B("LW", 0, 2048), [[0, 16], [-16, 8], [0, 16]], op, b, 1)
+    iota(B("SF", 0, 912), [[0, 57], [1, 16]], 0, 0)
+    asel(B("LWE1", 0, 2048), B("LW", 0, 2048), [[0, 16], [-16, 8], [0, 16]], A.is_equal, -1, 1)
+    for j, b in enumerate((1, 3, 613, 615)): iota(B("S1", j * M, j * M + M), [[4, M]], b, 0)
+    fill(B("RA", 0, CH), 1.0)
+    fill(B("RA", 0, CH - 15, 16), -512.0)
+    fill(B("KC", V, 464), 0.0)
+    vgather(CUT, 448)
+    for n, m in (("NW", 4), ("WP", 2), ("WD1", 2), ("WD2", 2)):
+        for j in range(m): dma("y", B(n, j * CH, j * CH + CH), B("WD0", 0, CH))
+    dma("y", B("WD0", CH, 2 * CH), B("WP", CH, 2 * CH))
+    scans(16 * CUT, 7168)
+    aD = DF("aD")
+    ts(aD, B("IOC", 0, 28), col(0), A.add)
+    ts(DF("A37"), aD, 2.0, A.mult, 37.0, A.add)
+    ts(DF("A1"), aD, 2.0, A.mult, 1.0, A.add)
+    ts(DF("A613"), aD, 2.0, A.mult, 613.0, A.add)
+    ts(DF("CNB"), aD, -448.0, A.add)
+    ts(DF("CPOS"), aD, float(CELLS), A.add)
+    ts(B("IOQ", 5, 6), B("IOQ", 0, 1), 1, A.bitwise_and)
+    ts(col(3), B("IOQ", 5, 6), 3576.0, A.mult, 15.0, A.add)
+    ts(DF("CM"), aD, 8.0, A.mult, col(3), A.add)
+    ts(col(2), col(0), 1.0, A.add)
+    for j, x in ((28, -1.0), (29, 35.0), (30, 8192.0)): fill(col(j), x)
+    ts(col(9), col(4), 16.0, A.mult, col(5), A.add)
+    act(B("LWE0", 0, 2048), B("LW", 0, 2048), scale=col(4))
+    act(B("LWK", 0, 2048), B("LW", 0, 2048), scale=col(2))
+    scans(0, 16 * CUT)
+
+    def base1(rows):
+        for p in range(16):
+            lo = (p & 1) * M + (p >> 1)
+            mm(B("PB", 0, 28), mat(rows, p), B("KC", lo, lo + 27 * 8 + 1, 8), p == 0, p == 15)
+
+    def base2(nm):
+        ts(DN("kI" + nm), B("PB", 0, 28), 128.0, A.add)
+        ts(DF("val" + nm), B("PB", 0, 28), -200.0, A.is_gt)
+        ts(DN("r" + nm), DN("kI" + nm), 15, A.bitwise_and)
+        tt(DN("ce" + nm), DF("CM"), DN("r" + nm), A.subtract)
+        cp(DU("ce" + nm), DN("ce" + nm))
+        act(B("NG", 0, V), ind(B("KW", 0, 7168), DU("ce" + nm)))
+        dist(B("PB", 32, 60), "LWN", "NG", 0, 16, 28)
+
+    def base3(nm, e): tt(e, B("PB", 32, 60), DF("val" + nm), A.mult)
+
+    def send_moved(t): send(B("LG%d" % t, 0, 32), out32("mv%d" % t), "rg%d" % t, route(rank + N - 1))
+    def zin(t): return B("Z0", 0, M) if t == 0 else B("LZ%d" % (t - 1), 0, M)
+    def rec(u): return ind(B("REC", 0, W + 16), DU(u))
+
+    def E1(t):
+        s = str(t)
+        e1, em, ei = DF("e" + s), DN("em" + s), DN("ei" + s)
+        cp(DU("e" + s), e1)
+        act(B("MSK", 0, V), ind(B("ID", 0, 912), DU("e" + s)))
+        ts(em, e1, -1.0, A.add)
+        ts(DN("ec" + s), em, 4, A.arith_shift_right)
+        cp(DU("ec" + s), DN("ec" + s))
+        ts(ei, em, 1, A.arith_shift_right)
+        cp(DU("ei" + s), ei)
+
+    def E2(t):
+        s = str(t)
+        tt(B("MAT", 0, V), ind(B("GF", 0, 464), DU("e" + s)), B("IOX", 1, V + 1), A.is_equal)
+        dist(B("PB", 64, 92), "LWK", "MAT", 0, 16, 28)
+        ts(DF("s1" + s), DF("e" + s), 2.0, A.mult, -1.0, A.add)
+        tt(DN("m1" + s), DF("s1" + s), aD, A.mult)
+        ts(DN("m2" + s), DN("m1" + s), 4, A.arith_shift_right)
+        tt(DF("c1" + s), DN("m2" + s), aD, A.add)
+        ts(DF("sl0" + s), DF("s1" + s), 612.0, A.add)
+
+    def E3(t):
+        s = str(t)
+        ts(DF("nk" + s), B("PB", 64, 92), 448.0, A.mult)
+        cp(DF("kk" + s), B("PB", 64, 92))
+        tt(DF("nk" + s), DF("nk" + s), DF("CNB"), A.add)
+        cp(DU("nk" + s), DF("nk" + s))
+        act(B("OG", 0, V), ind(B("NW", 0, 7168), DU("nk" + s)))
+        dist(B("PB", 96, 124), "LWO", "OG", 0, 16, 28)
+
+    def E4(t):
+        s = str(t)
+        ts(DF("mi" + s), DF("kk" + s), 0.5, A.is_gt)
+        t1 = DF("ps" + s)
+        ts(t1, DN("ei" + s), 16.0, A.mult, -1.0 - CELLS, A.add)
+        tt(t1, t1, DF("kk" + s), A.add)
+        tt(t1, t1, aD, A.subtract)
+        tt(t1, t1, DF("mi" + s), A.mult)
+        tt(t1, t1, DF("CPOS"), A.add)
+        cp(DU("ps" + s), t1)
+
+    def E5a(t):
+        s = str(t)
+        ts(DU("o" + s), B("PB", 96, 124), 1.0, A.add)
+        act(B("MSK", V, 2 * V), ind(B("ID", 0, 912), DU("o" + s)))
+
+    def E5b(t):
+        s = str(t)
+        cp(DN("o" + s), B("PB", 96, 124))
+        ts(DN("oc" + s), DN("o" + s), 4, A.arith_shift_right)
+        cp(DU("oc" + s), DN("oc" + s))
+        tt(DN("om" + s), DN("o" + s), DF("A1"), A.mult)
+        ts(DN("om" + s), DN("om" + s), 4, A.arith_shift_right)
+        tt(DF("ob" + s), DN("om" + s), DN("o" + s), A.add)
+        ts(DF("s37" + s), DN("o" + s), 2.0, A.mult, 37.0, A.add)
+
+    def D1(t):
+        s = str(t)
+        tt(B("GD", 0, V), ind(B("DT", 0, 64), DU("ec" + s)), B("MSK", 0, V), A.mult)
+        dist(B("PD", 0, 28), "LW", "GD", 0, 16, 28)
+        for j in range(3): ts(DN("pj%d%s" % (j, s)), DN("d" + s), float(j), A.add)
+        pj = wide(DN, "pj", s)
+        ts(pj, pj, 15, A.bitwise_and)
+
+    def D2(t):
+        s = str(t)
+        for j in range(3): tt(DF("bs%d%s" % (j, s)), DN("pj%d%s" % (j, s)), DF("sl0" + s), A.mult)
+        tt(DF("qt" + s), B("PD", 0, 28), DF("A37"), A.mult)
+        tt(DF("c0" + s), DF("c1" + s), DF("qt" + s), A.add)
+        for j in range(3): tt(DN("ix%d%s" % (j, s)), DF("bs%d%s" % (j, s)), DF("c0" + s), A.add)
+        ix = wide(DN, "ix", s)
+        ts(ix, ix, 4095, A.bitwise_and)
+        cp(wide(DU, "ix", s), ix)
+
+    def D3(t):
+        tt(B("GD", V, 2 * V), ind(B("DT", 0, 64), DU("oc%d" % t)), B("MSK", V, 2 * V), A.mult)
+        dist(B("PC", 128, 156), "LW", "GD", V, 16, 28)
+
+    def ze(t): act(B("ZE", 0, V), ind(zin(t), DU("ei" + str(t))))
+    def R1(t, j): tt(B("MT", j * V, j * V + V), rec("ix%d%d" % (j, t)), B("ZE", 0, V), A.max)
+
+    def R1x(t):
+        mm(B("PC", 0, 84), B("IDN", 0, 128), B("J84", 0, 84), True, False)
+        dist(B("PC", 0, 84), "LW4", "MT", 0, 16, 84, first=False)
+
+    def D4(t):
+        s = str(t)
+        tt(DF("od" + s), B("PC", 128, 156), DF("A613"), A.mult)
+        tt(DF("co" + s), DF("ob" + s), DF("od" + s), A.add)
+        tt(DF("ot" + s), DN("d" + s), DF("s37" + s), A.mult)
+        tt(DN("io" + s), DF("ot" + s), DF("co" + s), A.add)
+        ts(DN("io" + s), DN("io" + s), 4095, A.bitwise_and)
+        cp(DU("io" + s), DN("io" + s))
+
+    def R2(t):
+        tt(B("MO", 0, V), rec("io%d" % t), B("ZE", 0, V), A.max)
+        act(B("NMO", 0, V), B("MO", 0, V), scale=-1.0)
+
+    def R3(t):
+        s = str(t)
+        cp(DF("x" + s), B("PC", 0, 28))
+        tt(DF("x" + s), B("PC", 28, 56), DF("x" + s), A.min)
+        tt(DN("x" + s), B("PC", 56, 84), DF("x" + s), A.min)
+        ts(DN("x" + s), DN("x" + s), 3, A.bitwise_and)
+        tt(DF("jm" + s), DN("x" + s), DF("mi" + s), A.mult)
+        tt(DN("np" + s), DF("jm" + s), DN("d" + s), A.add)
+        nd = DN("nd" + s)
+        ts(nd, DN("np" + s), 15, A.bitwise_and)
+        for a, b, c, d in (("nt", "s37", "co", "in"), ("pt", "sl0", "c0", "ip")):
+            tt(DF(a + s), nd, DF(b + s), A.mult)
+            tt(DN(d + s), DF(a + s), DF(c + s), A.add)
+            ts(DN(d + s), DN(d + s), 4095, A.bitwise_and)
+            cp(DU(d + s), DN(d + s))
+            if d == "in": tt(B("MN", 0, V), rec("in" + s), B("ZE", 0, V), A.max)
+        act(B("RP", 0, V), rec("ip" + s), scale=0.5)
+        wd = "WD" + s
+        emit("v", [(wd, 0, WIN)], [("MN", 0, V), ("NMO", 0, V)] + DU("ps" + s)[1],
+             lambda: g.vector.tensor_tensor(T[wd][:, 0:WIN].indirect(DU("ps" + s)[0]), T["MN"][:, 0:V], T["NMO"][:, 0:V], A.add))
+        if t < 2:
+            cp(DB("mv%d" % (t + 1)), nd)
+            send_moved(t + 1)
+
+    def open_keys(): mm(B("PK", 0, 512), B("IDN", 0, 128), B("CK", 0, 512), True, False)
+
+    def keys(w, sel, stop):
+        for h in range(2):
+            for k in range(16):
+                lo = h * 112 * 16 + k
+                o = (T["PK"][0:112, h * 256 + k:h * 256 + 241 + k:16], [("PK", 0, 512)])
+                mm(o, B(w, lo, lo + 111 * 16 + 1, 16), B(sel, 0, 16), False, stop and h == 1 and k == 15)
+
+    def F1(t):
+        s, par = str(t), t & 1
+        if t == 2: return
+        mm(B("PA", 0, V), B("N0W", 0, 128), B("G0", 0, V), True, True)
+        act(B("TE", 1, V + 1), B("PA", 0, V))
+        act(B("NVO", 0, V), ind(B("TE", 0, 912), DU("e" + s)))
+        ts(DU("kc" + s), DN("ei" + s), float(par * M), A.add)
+
+    def F1b(t):
+        if t < 2: act(B("NVO", V, 2 * V), ind(B("TE", 0, 912), DU("o%d" % t)))
+        mm(B("PA", 0, V), B("LOA", 0, 128), B("OG", 0, V), True, True)
+        act(B("OA", 0, V), B("PA", 0, V), bias=1.0)
+
+    def F1c(t):
+        s = str(t)
+        if t < 2: dist(B("PJ", 0, 56), "LWE0", "NVO", 0, 16, 56)
+        tt(B("INL", 0, V), ind(B("GF", 0, 464), DU("e" + s)), B("OA", 0, V), A.is_equal)
+        dist(B("PJ", 64, 92), "LW", "INL", 0, 16, 28)
+
+    def F1k(t):
+        act(B("KV", 0, V), ind(B("KC", 0, 464), DU("kc%d" % t)))
+        dist(B("PJ", 128, 156), "LWE1" if t == 0 else "LWE0", "KV", 0, 16, 28)
+
+    def F2(t):
+        s, par = str(t), t & 1
+        jo, pa, kv = DF("jo" + s), DF("pa" + s), DF("kv" + s)
+        ts(DF("ow" + s), DN("o" + s), 448.0, A.is_lt)
+        ts(jo, B("PJ", 64, 92), 0.5, A.is_lt)
+        tt(jo, jo, DF("ow" + s), A.mult)
+        if t < 2:
+            ts(DN("pa" + s), DN("o" + s), 1, A.bitwise_and)
+            ts(pa, DN("pa" + s), float(1 - par), A.is_equal)
+            tt(pa, pa, jo, A.mult)
+            ts(DF("nf" + s), B("PJ", 0, 28), 255.0, A.is_lt)
+            tt(pa, pa, DF("nf" + s), A.mult)
+            ts(kv, B("PJ", 128, 156), 128.0, A.add)
+            tt(kv, B("PJ", 28, 56), kv, A.is_gt)
+            tt(pa, pa, kv, A.mult)
+            ts(pa, pa, 128.0, A.mult)
+            ts(jo, jo, 64.0, A.mult)
+            tt(DB("fl"), jo, pa, A.add)
+        else: ts(DB("fl"), jo, 64.0, A.mult)
+        mm(B("PA", 0, V), B("IP", 0, 128), B("OG", 0, V), True, False)
+        spread(DB("fl"), False)
+        act(B("PAY", 0, V), B("PA", 0, V))
+
+    def F3(t):
+        u = DU("ps%d" % t)
+        emit("v", [("WP", 0, WIN)], [("PAY", 0, V)] + u[1], lambda: g.vector.tensor_copy(T["WP"][:, 0:WIN].indirect(u[0]), T["PAY"][:, 0:V]))
+
+    it = lambda k, n=32: B("IT", 32 * k, 32 * k + n, 1, 112)
+    ii = lambda k: B("II", 32 * k, 32 * k + 32, 1, 112)
+
+    def injuries(t):
+        s = str(t)
+        scan(B("SC", 0, 512, 1, 112), B("RM", 0, 512, 1, 112), B("PK", 0, 512, 1, 112), A.mult, A.max)
+        top = B("SC", 15, 512, 16, 112)
+        cp(ii(0), top)
+        tt(it(0), top, B("TH0" if t == 0 else "THC", 0, 32, 1, 112), A.is_gt)
+        ts(ii(1), ii(0), 63, A.bitwise_and)
+        ts(it(2), ii(1), 28.0, A.is_ge)
+        ib, ib0, ib1 = B("IB", 0, 32, 1, 112), B("IB", 0, 16, 1, 112), B("IB", 16, 32, 1, 112)
+        tt(ib, it(2), it(0), A.mult)
+        up, on = B("UPR", 0, 112, 1, 112), B("ONE", 0, 112, 1, 112)
+        mm(P4("PN", 0, 112, 0, 16), up, ib0, True, True)
+        mm(P4("PN", 0, 112, 16, 32), up, ib1, True, False)
+        mm(P4("PN", 0, 112, 16, 32), on, ib0, False, True)
+        tt(B("OHP", 0, 256), ind(B("II", 32, 64), B("LP", 0, 16)), B("PATP", 0, 256), A.is_equal)
+        tt(it(3), ib, ii(1), A.mult)
+        ts(it(4), P4("PN", 0, 112, 0, 32), float(CAP), A.is_lt)
+        tt(it(5), it(4), it(3), A.mult)
+        tt(B("OHC", 0, V), ind(B("IT", 160, 192), B("LC", 0, 28)), B("PATC", 0, V), A.is_equal)
+        for q in range(4):
+            for h in range(2):
+                b = h * 8 + 2 * q
+                mm(P4("PN", 32 * q, 32 * q + 32, 64, 120), B("OHP", b * 16, b * 16 + 32), B("OHC", b * 28, b * 28 + 56), h == 0, h == 1)
+        joins(t)
+        ts(DF("n0" + s), B("PN", 64, 92), col(20), A.mult)
+        ts(DF("n1" + s), B("PN", 92, 120), col(21), A.mult)
+        tt(DB("cn" + s), DF("n0" + s), DF("n1" + s), A.add)
+        send(B("LN" + s, 0, 32), out32("cn" + s), "rn" + s, route(rank + 1))
+
+    def joins(t):
+        par = t & 1
+        tt(it(8), ii(1), B("W32", 0, 32, 1, 112), A.mult)
+        tt(it(8), it(8), B("B32", 0, 32, 1, 112), A.add)
+        for j in range(2 if t < 2 else 1):
+            ts(ii(2 + j), ii(0), 64 << j, A.bitwise_and)
+            ts(it(6 + j), ii(2 + j), 1.0, A.is_ge)
+            tt(it(6 + j), it(6 + j), it(0), A.mult)
+            for h in range(2):
+                tt(B("XX", 32 * h + 16 * j, 32 * h + 16 * j + 16, 1, 112), B("IT", 192 + 32 * j + 16 * h, 208 + 32 * j + 16 * h, 1, 112),
+                   B("IT", 256 + 16 * h, 272 + 16 * h, 1, 112), A.mult)
+        for h in range(2):
+            mm(P4("PJ", 0, 32, 112 * h, 112 * h + 112), B("XX", 32 * h, 32 * h + 32, 1, 112), B("IDN", 0, 112, 1, 112), True, True)
+        act(P4("XT", 0, 32, 0, M), P4("PJ", 0, 32, 0, M))
+        if t < 2:
+            for a in range(8):
+                mm(B("PJ", 480, 508), mat("EE", 2 * a + par, 32), B("XT", a, a + 217, 8, 32), a == 0, a == 7)
+        mm(B("PJ", 224, 448), B("EJ", 0, 128, 1, 32), B("XT", 0, M, 1, 32), True, True)
+
+    def next_e(t):
+        s, n = str(t), str(t + 1)
+        ts(DF("cq" + s), B("PJ", 480, 508), 0.0, A.is_equal)
+        tt(DF("cq" + s), DF("cq" + s), DF("eb" + n), A.mult)
+        tt(DF("e" + n), B("PJ", 480, 508), DF("cq" + s), A.add)
+
+    def ghosts(t):
+        s = str(t)
+        tt(DN("gd" + s), B("LG%d" % (t + 1), 0, 28), DB("cn" + s), A.add)
+        ts(DN("gd" + s), DN("gd" + s), 15, A.bitwise_and)
+        cp(B("DT", 28, 56), DN("gd" + s))
+
+    def own(t):
+        s, n = str(t), str(t + 1)
+        tt(DN("dd" + s), DN("nd" + s), B("LN" + s, 0, 28), A.add)
+        ts(DN("d" + n), DN("dd" + s), 15, A.bitwise_and)
+        cp(B("DT", 0, 28), DN("d" + n))
+
+    def lists(t):
+        par = t & 1
+        gf = B("GF", 1 + par, 448 + par, 2)
+        tt(B("UPD", 0, M), B("PJ", 224, 448), B("OHN", 0, M), A.mult)
+        tt(gf, gf, B("UPD", 0, M), A.add)
+        if t < 2: ts(B("G0", par, V - 1 + par, 2), gf, 0.5, A.is_gt)
+        if t == 0: cp(B("GU", 0, M), gf)
+
+    def count1(t):
+        cp(B("CB", 0, 32, 1, 112), it(0))
+        mm(B("PN", 128, 160), B("ONE", 0, 128, 1, 112), B("CB", 0, 32, 1, 112), True, True)
+
+    def count2(t):
+        for j in range(2):
+            lo = 128 + 16 * j
+            emit("v", [("CF", 0, 2)], [("PN", 0, 512)], lambda: g.vector.tensor_reduce(T["CF"][:, j:j + 1], T["PN"][:, lo:lo + 8], AxisListType.X, A.add))
+        tt(B("CI", 0, 1), B("CF", 0, 1), B("CF", 1, 2), A.add)
+        ts(B("CI", 1, 2), B("CI", 0, 1), 31, A.bitwise_and)
+        ts(B("CF", 2, 3), B("CI", 1, 2), 4096.0, A.mult)
+        ts(B("THC", 0, 32, 1, 112), B("TH0", 0, 32, 1, 112), B("CF", 2, 3, 1, 112), A.add)
+
+    SF = lambda k: B("SF", k * M, k * M + M)
+    SI = B("SI", 0, M)
+
+    def sp0(t):
+        mm(B("PN", 256, 480), B("BD", 0, 128), B("G0", t & 1, V - 1 + (t & 1), 2), True, True)
+        ts(B("OHN", 0, M), B("PN", 256, 480), col(0), A.is_equal)
+
+    def spS(t):
+        gf = B("GF", 1 + (t & 1), 448 + (t & 1), 2)
+        act(SF(0), gf, bias=col(28))
+        act(SF(3), gf, scale=2.0, bias=col(29))
+        act(SF(4), gf, scale=-8192.0, bias=col(30), relu=True)
+
+    def spV(t):
+        par = t & 1
+        tt(SI, SF(0), B("S1", par * M, par * M + M), A.mult)
+        ts(SI, SI, 4, A.arith_shift_right)
+        tt(SF(1), SI, SF(0), A.add)
+
+    def slots1(t, j):
+        par = t & 1
+        dist(B("PS", 112 * j, 112 * j + 112), "LWD", "KW", par * CELLS + j * CH, 16, 112)
+        if j: mm(B("PS", 256, 480), B("R2B", 0, 128), B("TN", 1 + par, 448 + par, 2), True, True)
+
+    def slots2(t):
+        par = t & 1
+        tt(SF(2), B("PS", 0, M), B("S1", (2 + par) * M, (3 + par) * M), A.mult)
+        tt(SF(3), B("PS", 256, 480), SF(3), A.mult)
+        tt(SF(1), SF(1), SF(2), A.add)
+        tt(SI, SF(1), SF(3), A.add)
+        ts(SI, SI, 4095, A.bitwise_and)
+        tt(SF(1), SI, SF(4), A.add)
+        ts(B("ISL", 0, M), SF(1), float(W), A.min)
+
+    def slots3(a, b):
+        act(B("WR", 16 * a, 16 * b), ind(B("REC", 0, W + 16), B("ISL", a, b)), scale=0.5)
+
+    def L1(t):
+        u = DU("ps%d" % t)
+        ts(B("ZH", 0, M), zin(t), 0.5, A.mult, -0.25, A.add)
+        emit("v", [("WR", 0, WIN)], [("RP", 0, V)] + u[1], lambda: g.vector.tensor_copy(T["WR"][:, 0:WIN].indirect(u[0]), T["RP"][:, 0:V]))
+
+    def L2(t, j):
+        s = str(t)
+        b, z = half(), j * CH // 16
+        scan(B("KT", b, b + CH), B("RM", 0, CH), B("WR", j * CH, j * CH + CH), A.mult, A.max)
+        tt(B("ZI", z, z + 112), B("KT", b + 15, b + CH, 16), B("ZH", z, z + 112), A.add)
+        if j == 0: return
+        cp(B("ZB" + s, 0, M), B("ZI", 0, M))
+        send(B("LZ" + s, 0, M), B("ZB" + s, 0, M), "rz" + s, route(rank + 1 + t))
+
+    def thresholds1():
+        ts(B("IOQ", 3, 4), B("IOQ", 0, 1), 7, A.bitwise_and)
+        ts(B("IOQ", 4, 5), B("IOQ", 2, 3), 1, A.bitwise_and)
+        cp(col(21), B("IOQ", 4, 5))
+        ts(col(20), col(21), -1.0, A.mult, 1.0, A.add)
+        cp(col(22), B("IOQ", 0, 1))
+        cp(col(23), B("IOQ", 3, 4))
+        ts(B("THT", 0, M, 1, 8), B("THI", 0, M, 1, 8), 4, A.arith_shift_right)
+        ts(B("THT", M, 2 * M, 1, 8), B("THI", 0, M, 1, 8), 15, A.bitwise_and)
+        cp(B("THB", 0, 2 * M, 1, 8), B("THT", 0, 2 * M, 1, 8))
+        ts(B("SELT", 0, 16), B("IO8", 0, 16), col(22), A.is_equal)
+        ts(B("SELU", 0, 16), B("SELT", 0, 16), 16.0, A.mult)
+        for h in range(2):
+            o = P4("PN", 0, 112, 16 * h, 16 * h + 16)
+            mm(o, B("THB", 112 * h, 112 * h + 112, 1, 8), B("SELU", 0, 16, 1, 8), True, False)
+            mm(o, B("THB", M + 112 * h, M + 112 * h + 112, 1, 8), B("SELT", 0, 16, 1, 8), False, True)
+        cp(B("LP", 0, 16), B("LPI", 0, 16))
+        ts(DN("hg"), aD, 1.0 / 28, A.mult, 0.5 / 28 - 0.5, A.add)
+        ts(DN("h3"), DN("hg"), 3, A.arith_shift_right)
+        ts(DF("h8"), DN("h3"), 8.0, A.mult)
+        tt(DF("h8"), DF("h8"), DN("hg"), A.add)
+        cp(B("LC", 0, 28), DF("h8"))
+
+    def thresholds2(): ts(B("TH0", 0, 32, 1, 112), P4("PN", 0, 112, 0, 32), 4096.0, A.mult, 4095.0, A.add)
+
+    def join_mats():
+        fill(B("W32", 0, 32), 1.0)
+        fill(B("B32", 0, 32), 1.0)
+        for h in (0, 16):
+            fill(B("W32", h, h + 8), 16.0)
+            fill(B("B32", h, h + 8), 0.0)
+        ts(col(24), col(22), 15.5, A.is_gt)
+        ts(col(25), col(22), 15.5, A.is_lt)
+        ts(B("EJ", 0, 128, 1, 32), B("IOM", 0, 128, 1, 32), col(23, 32), A.is_equal, col(25, 32), A.mult)
+        ts(B("EE0", 0, 128, 1, 32), B("IOM", 0, 128, 1, 32), col(23, 32), A.is_equal, col(24, 32), A.mult)
+        for a in range(8): cp(B("EE", 16 * a, 16 * a + 129 * 15 + 1, 129, 32), B("EE0", 16 * a, 16 * a + 16, 1, 32))
+
+    slots1(0, 0)
+    slots1(0, 1)
+    base1("LWE0")
+    fill(B("GF", 0, 1), -5.0)
+    fill(B("GF", V + 1, 464), -5.0)
+    ts(B("GF", 1, V + 1), B("GI", 0, V), 1.0, A.add)
+    ts(B("IOQ", 6, 7), B("IOQ", 0, 1), 1, A.add)
+    ts(B("IOQ", 7, 8), B("IOQ", 6, 7), 15, A.bitwise_and)
+    cp(col(26), B("IOQ", 7, 8))
+    ts(B("ID", 0, 912), B("SF", 0, 912), col(26), A.is_equal)
+    fill(B("DT", 56, 64), 0.0)
+    ts(B("NBT", 0, V), B("NBI", 0, V), 4, A.arith_shift_right)
+    ts(B("NBT", V, 2 * V), B("NBI", 0, V), 15, A.bitwise_and)
+    base2("0")
+    act(B("LWO", 0, 2048), B("LW", 0, 2048), scale=col(9))
+    dist(B("PD", 0, 28), "LWD", "TN", 1, 16, 28)
+    cp(B("NBD", 0, V), B("NBT", 0, V))
+    cp(B("NBD", V, 2 * V), B("NBT", V, 2 * V))
+    dma("y", (T["NW"][0:113:16, 0:7168], [("NW", 0, 7168)]), B("NBD", 0, V))
+    dma("y", (T["NW"][1:114:16, 0:7168], [("NW", 0, 7168)]), B("NBD", V, 2 * V))
+    for t in range(3):
+        fill(out32("mv%d" % t), 0.0)
+        fill(out32("cn%d" % t), 0.0)
+    base3("0", DF("e0"))
+    E1(0)
+    cp(B("DT", 0, 28), B("PD", 0, 28))
+    cp(DN("d0"), B("PD", 0, 28))
+    cp(DB("mv0"), B("PD", 0, 28))
+    iota(B("CK", 0, 512), [[0, 32], [-256, 16]], 3840, 0)
+    send_moved(0)
+    iota(B("PATP", 0, 256), [[0, 16], [1, 16]], 0, 0)
+    iota(B("PATC", 0, V), [[0, 16], [1, 28]], 28, 0)
+    iota(B("LPI", 0, 16), [[16, 2], [1, 8]], 8, 0)
+    asel(B("UPR", 0, 112), B("ONE", 0, 112), [[1, 112]], A.is_gt, 0, -1)
+    E2(0)
+    ze(0)
+    D1(0)
+    E3(0)
+    act(B("LW4", 0, 2048), B("LW", 0, 2048), scale=4.0)
+    fill(B("REC", W, W + 16), 0.0)
+    for j in range(3): fill(B("J84", 28 * j, 28 * j + 28), float(j))
+    act(B("TE", 0, 912), B("WD0", 0, 912))
+    ts(B("LOA", 0, 128), B("BD", 0, 128), col(9), A.mult)
+    ts(B("IP", 0, 128), B("IDN", 0, 128), col(17), A.mult)
+    F1(0)
+    D2(0)
+    R1(0, 0)
+    E4(0)
+    R1(0, 1)
+    E5a(0)
+    R1(0, 2)
+    R1x(0)
+    F1b(0)
+    E5b(0)
+    cp(B("DT", 28, 56), B("LG0", 0, 28))
+    D3(0)
+    sp0(0)
+    F1k(0)
+    F1c(0)
+    base1("LWE1")
+    spS(0)
+    spV(0)
+    slots2(0)
+    act(B("DA2", 0, 2048), B("WD0", 0, 2048))
+    act(B("EE", 0, 2048, 1, 32), B("WD0", 0, 2048, 1, 32))
+    asel(B("DA2", 2, 2035, 16), B("ONE", 0, 128), [[-1, 16], [-16, 8]], A.is_equal, 0, 1)
+    iota(B("IO8", 0, 16), [[0, 2], [1, 8]], 0, 0)
+    act(B("IT", 0, 448), B("WD0", 0, 448))
+    fill(B("II", 0, 128), 0.0)
+    act(B("RM", 0, CH), B("RA", 0, CH), relu=True)
+    base2("1")
+    D4(0)
+    slots3(0, 56)
+    slots3(56, 112)
+    R2(0)
+    thresholds1()
+    F2(0)
+    R3(0)
+    slots3(112, 168)
+    slots3(168, 224)
+    F3(0)
+    thresholds2()
+    ts(B("SELD", 0, 8), B("BD", 0, 113, 16), 4096.0, A.mult)
+    ts(B("SELD", 8, 16), B("BD", 0, 113, 16), 4096.0, A.mult)
+    ts(col(18), col(4), col(6), A.add)
+    ts(col(19), col(5), col(6), A.add)
+    ts(B("SELP", 0, 8), B("BD", 0, 113, 16), col(18), A.mult)
+    ts(B("SELP", 8, 16), B("BD", 0, 113, 16), col(19), A.mult)
+    open_keys()
+    keys("WD0", "SELD", False)
+    keys("WP", "SELP", True)
+    join_mats()
+    base3("1", DF("eb1"))
+    for t in range(3):
+        if t == 0: L1(0)
+        injuries(t)
+        if t == 1: base3("2", DF("eb2"))
+        if t > 0: L1(t)
+        if t == 2: break
+        n = t + 1
+        h = n & 1
+        next_e(t)
+        E1(n)
+        if n == 1:
+            lists(0)
+            table(False)
+            sp0(1)
+            sgather(0, 56)
+            sgather(56, 112)
+        F1(n)
+        if n == 1: spS(1)
+        count1(t)
+        L2(t, 0)
+        L2(t, 1)
+        own(t)
+        D1(n)
+        table(True, n == 2)
+        ghosts(t)
+        E2(n)
+        D2(n)
+        ze(n)
+        E3(n)
+        if n == 2:
+            lists(1)
+            spS(2)
+        spV(n)
+        sgather(224 * h, 224 * h + 56)
+        R1(n, 0)
+        E5a(n)
+        R1(n, 1)
+        R1(n, 2)
+        R1x(n)
+        E4(n)
+        F1b(n)
+        sgather(224 * h + 56, 224 * h + 112)
+        sgather(224 * h + 112, 224 * h + 168)
+        E5b(n)
+        D3(n)
+        F1c(n)
+        if n == 2: F2(2)
+        slots1(n, 0)
+        D4(n)
+        R2(n)
+        sgather(224 * h + 168, 224 * h + 224)
+        open_keys()
+        if n == 2:
+            F3(2)
+            keys("WP", "SELP", False)
+        slots1(n, 1)
+        R3(n)
+        if n == 1:
+            keys("WD1", "SELD", False)
+            scans(CELLS, 2 * CELLS)
+            F1k(1)
+        else: keys("WD2", "SELD", True)
+        slots2(n)
+        count2(t)
+        if n == 2: sp0(2)
+        if n == 1:
+            vgather(168, 224)
+            sgather(112, 168)
+        else: ts(B("WR", 16 * 168, CELLS), ind(B("REC", 0, W + 16), B("ISL", 168, 224)), 0.5, A.mult)
+        slots3(0, 56)
+        if n == 1: F2(1)
+        slots3(56, 112)
+        if n == 1: scans(0, CELLS)
+        slots3(112, 168)
+        if n == 1:
+            slots3(168, 224)
+            F3(1)
+            base1("LWE0")
+            keys("WP", "SELP", True)
+            base2("2")
+    L2(2, 0)
+    L2(2, 1)
+    own(2)
+    spread(B("DT", 0, 28), True)
+    lists(2)
+    ts(B("YL", 0, V), B("GF", 1, V + 1), -1.0, A.add)
+    dma("y", (T.yl[:, :], []), B("YL", 0, V))
+    act(B("YD", 0, V), B("PA", 0, V))
+    dma("y", (T.yd[:, :], []), (T["SF"][2:115:16, 0:V], [("SF", 0, V)]))
+    dma("y", (T.yz[:, :], []), B("LZ2", 0, M))
+    finish()

@@ -2,56 +2,95 @@ from concourse.mybir import AluOpType, AxisListType, ActivationFunctionType
 
 V, M, W, RO, CAP = 448, 224, 4096, 3, 44
 CELLS = 16 * M
-WIN = CELLS + V
-CH = 1792
+H = CELLS // 2
+CYCLE, GATHER, WAKE = 1.04, 1.56, 110
+BIAS = 700
+HUGE = float(2 ** 30)
+ROUND = float(3 * 2 ** 22)
 
 
-def bf(n): return ("sbuf", [128, n], "bfloat16")
-def f4(n): return ("sbuf", [128, n], "float32")
-def i4(n): return ("sbuf", [128, n], "int32")
+def bf(n, p=128): return ("sbuf", [p, n], "bfloat16")
+def f4(n, p=128): return ("sbuf", [p, n], "float32")
+def i4(n, p=128): return ("sbuf", [p, n], "int32")
 def u2(n): return ("sbuf", [128, n], "uint16")
 
 
+SHIFTED = ["L64", "LK", "LE", "LO", "L1", "L2", "DP", "DM", "EE0", "EE1"]
+SQUARE = ["IDN", "BIG", "P18", "HLF", "N1K", "BD", "B32", "R2B", "I567", "I012", "SLE", "SLV", "EJ", "EB", "UPM", "C64"]
 SCRATCH = {
-    "GI": i4(V), "NBI": i4(V), "VI": ("sbuf", [8, V], "int32"), "THI": ("sbuf", [8, M], "int32"), "Z0": bf(M),
-    "REC": bf(W + 16), "NW": bf(2 * CELLS), "KW": bf(2 * CELLS), "KC": bf(464), "KT": bf(2 * CH), "WR": bf(WIN), "WP": bf(WIN),
-    "GF": f4(464), "GU": u2(V), "G0": bf(V), "NBD": bf(2 * V), "NBT": i4(2 * V),
-    "VB": ("sbuf", [8, V], "bfloat16"), "THT": ("sbuf", [8, 2 * M], "int32"), "THB": ("sbuf", [8, 2 * M], "bfloat16"),
-    "TN": bf(464), "X34": bf(1024), "TE": bf(912), "ID": bf(912),
-    "IOQ": i4(8), "COL": f4(32), "IOM": f4(128), "IOX": f4(464), "IOC": f4(28), "S1": f4(4 * M), "IO8": f4(16),
-    "RA": bf(CH), "RM": bf(CH), "CK": bf(512), "J84": bf(84), "PATP": f4(256), "PATC": f4(V), "LPI": i4(16),
-    "LPC": u2(44), "SELS": bf(64), "ONE": bf(128), "UPR": bf(128), "IDN": bf(128), "E8": ("sbuf", [8, 128], "bfloat16"),
-    "EJ": ("sbuf", [32, 128], "bfloat16"), "EE0": ("sbuf", [32, 128], "bfloat16"), "EE": ("sbuf", [32, 2048], "bfloat16"),
-    "BD": bf(128), "MM": bf(1024),
-    "LW": bf(2048), "LW4": bf(2048), "LWE0": bf(2048), "LWE1": bf(2048), "LWD": bf(2048), "LWN": bf(2048),
-    "LWK": bf(2048), "LWO": bf(2048), "DA2": bf(2048), "W32": f4(32), "B32": f4(32), "TH0": f4(32), "THC": f4(32),
-    "MAT": bf(V), "NG": bf(V), "INL": bf(V), "MSK": bf(2 * V), "OG": bf(V), "OA": f4(V), "NVO": bf(2 * V), "KV": bf(V),
-    "PAY": bf(V), "GD": bf(2 * V), "ZE": bf(V), "MT": bf(3 * V), "RP": bf(V), "MN": bf(V), "MO": bf(V), "NMO": bf(V),
-    "SI": i4(M), "SF": f4(6 * M), "ISL": u2(M), "OHN": f4(M), "UPD": f4(M), "ZH": f4(M), "ZI": i4(M),
-    "SC": f4(512), "IT": f4(14 * 32), "II": i4(4 * 32), "IBC": bf(64), "XX": bf(64), "XT": ("sbuf", [32, M], "bfloat16"),
-    "OHP": bf(256), "OHC": bf(V), "DT": bf(64), "CF": f4(4), "CI": i4(4),
-    "DF": f4(28 * 104), "DN": i4(28 * 72), "DU": u2(28 * 64), "DB": bf(32 * 12),
-    "PA": ("psum", [128, 512], "float32"), "PB": ("psum", [128, 512], "float32"), "PC": ("psum", [128, 512], "float32"),
-    "PD": ("psum", [128, 512], "float32"), "PK": ("psum", [128, 512], "float32"), "PN": ("psum", [128, 512], "float32"),
-    "PS": ("psum", [128, 512], "float32"), "PJ": ("psum", [128, 512], "float32"),
+    "GI": i4(V), "NBI": i4(V), "VI": i4(28), "THI": i4(M, 8), "Z0": bf(M), "REC": bf(W + 16), "NW": bf(2 * CELLS), "KW": bf(2 * CELLS),
+    "WR": bf(CELLS), "KT": bf(CELLS), "GF": f4(464), "GU": u2(V), "GM": u2(3 * M), "G0": bf(V), "NBD": bf(2 * V), "THB": bf(2 * M, 8),
+    "TN": bf(464), "PB": bf(464), "T1": bf(V), "VT": bf(2 * V), "CR": bf(V), "ID": bf(M), "IDS": f4(M),
+    "ONE": bf(V), "LW": bf(144 * len(SHIFTED)), "SQ": bf(128 * len(SQUARE)), "DA": bf(2064), "DG": bf(8 * 112), "KS": bf(384, 1),
+    "SEL": bf(96), "THS": bf(24, 8), "G8": bf(16), "OH": f4(16), "IO": f4(16), "IOQ": i4(8), "COL": f4(40), "CB": bf(4), "IOM": f4(128),
+    "IOX": f4(V), "S17": f4(V), "RAP": bf(V), "RAM": bf(V), "RAK": bf(384), "RM": bf(H), "J16": bf(84), "PP": i4(384), "PC": bf(V),
+    "LPI": i4(24), "LPC": u2(52), "SE": f4(2 * V), "SC": f4(768),
+    "MSK": bf(V), "ZE": bf(V), "MAT": bf(V), "GD": bf(V), "OG": bf(V), "VO": bf(V), "MT": bf(3 * V), "MO": bf(V), "MN": bf(V),
+    "AB": bf(256), "PA": bf(512), "TI": i4(96), "THC": f4(48), "X": bf(64), "INJ": bf(64), "IB": bf(64), "TM": bf(64),
+    "OHP": bf(384), "OHC": bf(V), "XT": bf(M), "EQ": bf(M), "A2": bf(M), "S2": f4(M), "EM": bf(M), "X1": f4(M), "CC": f4(M),
+    "XI": i4(M), "ISL": u2(M), "CF": f4(16), "CI": i4(4), "SB": bf(32 * 6), "GN2": f4(28), "LD2": f4(28), "LG": bf(32),
+    "DF": f4(28 * 32), "DN": i4(28 * 24), "DU": u2(28 * 16), "DB": bf(28 * 8),
 }
-for _t in range(3):
-    SCRATCH["WD%d" % _t] = bf(WIN)
-    SCRATCH["LG%d" % _t] = bf(32)
-    SCRATCH["LN%d" % _t] = bf(32)
+PSUM = ["PT", "K0", "K1", "Q", "PS", "PD", "PM", "PN"]
+for _n in PSUM: SCRATCH[_n] = ("psum", [128, 512], "float32")
+for _t in range(RO):
+    SCRATCH["LM%d" % _t] = bf(32)
     SCRATCH["LZ%d" % _t] = bf(M)
     SCRATCH["ZB%d" % _t] = bf(M)
-SEMAPHORES = ["cv", "cs", "ct", "cg"] + ["dma%d" % k for k in range(40)] + ["rg%d" % k for k in range(3)] + \
-    ["rn%d" % k for k in range(3)] + ["rz%d" % k for k in range(3)] + ["ls%d" % k for k in range(9)]
-ALIAS = {"SELD": ("SELS", 0), "SELP": ("SELS", 16), "SELT": ("SELS", 32), "SELU": ("SELS", 48), "IB": ("IBC", 0), "CB": ("IBC", 32),
-         "LP": ("LPC", 0), "LC": ("LPC", 16), "R2B": ("MM", 0), "LOA": ("MM", 128), "IP": ("MM", 256), "N0W": ("MM", 384),
-         "N1W": ("MM", 512), "I3": ("MM", 640), "I4": ("MM", 768), "YD": ("SF", 0), "YL": ("SF", 448)}
-PSUM = {"PA", "PB", "PC", "PD", "PK", "PN", "PS", "PJ"}
+    if _t < 2: SCRATCH["LD%d" % _t] = bf(32)
+SEMAPHORES = ["cv", "cs", "ct", "cg", "rg"] + ["dma%d" % k for k in range(20)] + ["ls%d" % k for k in range(10)] + \
+    [a + str(k) for a in ("rm", "rd", "rz") for k in range(RO)]
+ALIAS = {n: ("SQ", 128 * k) for k, n in enumerate(SQUARE)}
+ALIAS.update({"V0": ("SB", 0), "MV0": ("SB", 32), "MV1": ("SB", 64), "MV2": ("SB", 96), "GN0": ("SB", 128), "GN1": ("SB", 160),
+              "LP": ("LPC", 0), "LC": ("LPC", 24), "SL1": ("SEL", 0), "SL2": ("SEL", 32), "S15": ("SEL", 48)})
+
+
+def meet(r, s): return r[1] < s[2] and s[1] < r[2] and r[3] < s[4] and s[3] < r[4]
+def covers(r, s): return r[1] <= s[1] and s[2] <= r[2] and r[3] <= s[3] and s[4] <= r[4]
+
+
+def order(calls):
+    log, pre = {}, []
+    for n, c in enumerate(calls):
+        d = dict(c[4])
+        for regs, w in ((c[2], False), (c[1], True)):
+            for r in regs:
+                for s, sw, m in log.get(r[0], []):
+                    if r[0] in PSUM or ((w or sw) and meet(r, s)):
+                        same = c[0] == calls[m][0] and len(c[0]) == 1 and c[0] in "vstg"
+                        d[m] = max(d.get(m, 0), 0 if same and (c[0] == "t" or not sw) else WAKE)
+        for regs, w in ((c[2], False), (c[1], True)):
+            for r in regs:
+                L = log.setdefault(r[0], [])
+                if r[0] in PSUM: L[:] = []
+                elif w: L[:] = [x for x in L if not covers(r, x[0])]
+                L.append((r, w, n))
+        d.pop(n, None)
+        pre.append(d)
+    tail = [min(x[1] for x in c[3].values()) for c in calls]
+    for n in range(len(calls) - 1, -1, -1):
+        for m, lag in pre[n].items(): tail[m] = max(tail[m], min(x[1] for x in calls[m][3].values()) + lag + tail[n])
+    taken, done, plan = {}, {}, []
+    for n in sorted(range(len(calls)), key=lambda n: (-tail[n], n)):
+        ready = max([done[m] + lag for m, lag in pre[n].items()], default=0.0)
+        best = None
+        for q, (busy, until) in calls[n][3].items():
+            t = ready
+            for a, b in taken.get(q, []):
+                if t + busy <= a: break
+                t = max(t, b)
+            if best is None or t + until - BIAS < best[0]: best = (t + until, t, q, busy)
+        done[n] = best[0]
+        L = taken.setdefault(best[2], [])
+        L.append((best[1], best[1] + best[3]))
+        L.sort()
+        plan.append((best[1], n, best[2]))
+    return sorted(plan)
 
 
 def builder(g, T):
     eng = {"v": g.vector, "s": g.scalar, "t": g.tensor, "g": g, "y": g.sync}
-    cnt = {"v": 0, "s": 0, "t": 0, "g": 0, "dma": 0, "ls": 0}
+    cnt = {"v": 0, "s": 0, "t": 0, "g": 0, "dma": 0, "ls": 0, "alone": False}
     known = {q: {} for q in eng}
     log = {}
     total = {}
@@ -71,26 +110,29 @@ def builder(g, T):
     def deps(q, outs, ins, comp):
         evs = []
         for regs, w in ((ins, False), (outs, True)):
-            for b, lo, hi in regs:
-                for r in log.get(b, []):
-                    same = comp and r[3] == q
-                    if b in PSUM:
-                        if not same or (q != "t" and (w or r[2])): evs.append(r[4])
-                    elif r[0] < hi and lo < r[1] and (w or r[2]):
-                        if same and (q == "t" or not r[2]): continue
-                        evs.append(r[4])
+            for r in regs:
+                for s, sw, sq, ev in log.get(r[0], []):
+                    same = comp and sq == q
+                    if r[0] in PSUM:
+                        if not same or (q != "t" and (w or sw)): evs.append(ev)
+                    elif (w or sw) and meet(r, s):
+                        if same and (q == "t" or not sw): continue
+                        evs.append(ev)
         return evs
 
     def note(q, outs, ins, ev):
         for regs, w in ((ins, False), (outs, True)):
-            for b, lo, hi in regs:
-                L = log.setdefault(b, [])
-                if b in PSUM: L[:] = [r for r in L if r[3] != q or r[2] != w]
-                else: L[:] = [r for r in L if not (lo <= r[0] and r[1] <= hi and (w or (not r[2] and r[3] == q and q in "vstg")))]
-                L.append((lo, hi, w, q, ev))
+            for r in regs:
+                L = log.setdefault(r[0], [])
+                if r[0] in PSUM: L[:] = [x for x in L if x[2] != q or x[1] != w]
+                else: L[:] = [x for x in L if not (covers(r, x[0]) and (w or (not x[1] and x[2] == q and q in "vstg")))]
+                L.append((r, w, q, ev))
 
-    def emit(q, outs, ins, call):
+    def emit(q, outs, ins, call, alone=False):
         wait(q, deps(q, outs, ins, True))
+        if q == "g":
+            if (alone or cnt["alone"]) and cnt[q]: wait(q, [("cg", cnt[q], {})])
+            cnt["alone"] = alone
         cnt[q] += 1
         s = "c" + q
         call().then_inc(T.sem[s], 1)
@@ -115,7 +157,7 @@ def builder(g, T):
 
     def arrive(view, sem, n):
         total[sem] = n
-        for b, lo, hi in view[1]: log.setdefault(b, []).append((lo, hi, True, "x" + sem, (sem, n, {})))
+        for r in view[1]: log.setdefault(r[0], []).append((r, True, "x" + sem, (sem, n, {})))
 
     def finish():
         wait("y", [(s, n, {}) for s, n in sorted(total.items())])
@@ -128,749 +170,546 @@ def rank_program(g, core, T, topo):
     if rank is None: return
     N = len(T.cores)
     A, F = AluOpType, ActivationFunctionType
-    emit, dma, send, arrive, finish = builder(g, T)
+    emit, dma_now, send_now, arrive, finish = builder(g, T)
+    calls = []
 
-    def B(n, lo, hi, st=1, p=128):
-        if n in ALIAS: n, lo, hi = ALIAS[n][0], lo + ALIAS[n][1], hi + ALIAS[n][1]
-        ap = T[n][0:p, lo:hi] if st == 1 else T[n][0:p, lo:hi:st]
-        return (ap, [(n, lo, hi)])
+    def B(n, lo, cnt, st=1, p=128, p0=0):
+        if n in ALIAS: n, lo = ALIAS[n][0], lo + ALIAS[n][1]
+        hi = lo + (cnt - 1) * st + 1
+        return (T[n][p0:p, lo:hi] if st == 1 else T[n][p0:p, lo:hi:st], [(n, lo, hi, p0, p)], cnt, n)
 
-    def P4(n, p0, p1, lo, hi): return (T[n][p0:p1, lo:hi], [(n, lo, hi)])
-    def ind(win, off): return (win[0].indirect(off[0]), win[1] + off[1])
+    def ind(win, off): return (win[0].indirect(off[0]), win[1] + off[1], 16 * off[2], None)
     def num(s): return (s, []) if s is None or isinstance(s, (int, float)) else s
-    def tt(o, a, b, op): emit("v", o[1], a[1] + b[1], lambda: g.vector.tensor_tensor(o[0], a[0], b[0], op))
-    def cp(o, a): emit("v", o[1], a[1], lambda: g.vector.tensor_copy(o[0], a[0]))
+    def short(*x): return 0.5 if all(SCRATCH[a[3]][2] in ("bfloat16", "uint16") for a in x) else 1.0
+
+    def call(q, outs, ins, ns, f, alone=False):
+        calls.append([q, outs, ins, {q: (ns, ns)}, {}, lambda _: emit(q, outs, ins, f, alone)])
+
+    def vec(o, a, ins, k, f): call("v", o[1], ins, 50 + GATHER * o[2] if a[3] is None else CYCLE * max(64, k * o[2]), f)
+    def tt(o, a, b, op): vec(o, a, a[1] + b[1], 1 if a[3] in PSUM or b[3] in PSUM else 2, lambda: g.vector.tensor_tensor(o[0], a[0], b[0], op))
+    def cp(o, a): vec(o, a, a[1], short(o, a), lambda: g.vector.tensor_copy(o[0], a[0]))
 
     def ts(o, a, s1, op0, s2=None, op1=None):
         x, y = num(s1), num(s2)
-        if op1 is None: emit("v", o[1], a[1] + x[1], lambda: g.vector.tensor_scalar(o[0], a[0], x[0], None, op0))
-        else: emit("v", o[1], a[1] + x[1] + y[1], lambda: g.vector.tensor_scalar(o[0], a[0], x[0], y[0], op0, op1))
+        if op1 is None: vec(o, a, a[1] + x[1], short(o, a), lambda: g.vector.tensor_scalar(o[0], a[0], x[0], None, op0))
+        else: vec(o, a, a[1] + x[1] + y[1], short(o, a), lambda: g.vector.tensor_scalar(o[0], a[0], x[0], y[0], op0, op1))
 
-    def scan(o, a, b, op0, op1): emit("v", o[1], a[1] + b[1], lambda: g.vector.tensor_tensor_scan(o[0], a[0], b[0], 0.0, op0, op1))
-    def fill(o, c): emit("v", o[1], [], lambda: g.vector.memset(o[0], c))
+    def scan(o, a, b, op0, op1): vec(o, a, a[1] + b[1], short(o, a, b), lambda: g.vector.tensor_tensor_scan(o[0], a[0], b[0], 0.0, op0, op1))
+    def fill(o, c): vec(o, o, [], short(o), lambda: g.vector.memset(o[0], c))
+    def total(o, a): vec(o, a, a[1], 1, lambda: g.vector.tensor_reduce(o[0], a[0], AxisListType.X, A.add))
 
-    def act(o, a, scale=1.0, bias=0.0, relu=False):
+    def act(o, a, scale=1.0, bias=0.0, fn=None, acc=None):
         x, y = num(scale), num(bias)
-        fn = F.Relu if relu else F.Copy if y[0] == 0.0 and not y[1] else F.Identity
-        emit("s", o[1], a[1] + x[1] + y[1], lambda: g.scalar.activation(o[0], a[0], fn, bias=y[0], scale=x[0]))
+        ns = 65 + GATHER * o[2] if a[3] is None else 60 + CYCLE * max(64, o[2])
+        if fn is None: fn = F.Copy if not y[1] and y[0] == 0.0 else F.Identity
+        if acc is None: call("s", o[1], a[1] + x[1] + y[1], ns, lambda: g.scalar.activation(o[0], a[0], fn, bias=y[0], scale=x[0]))
+        else: call("s", o[1] + acc[1], a[1], ns, lambda: g.scalar.activation(o[0], a[0], fn, accum_out=acc[0]))
 
-    def mm(o, l, r, start, stop): emit("t", o[1], l[1] + r[1], lambda: g.tensor.matmul(o[0], l[0], r[0], start, stop))
-    def iota(o, pat, base, cm): emit("g", o[1], [], lambda: g.iota(o[0], pat, base, cm, allow_small_or_imprecise_dtypes=True))
-    def asel(o, a, pat, op, base, cm): emit("g", o[1], a[1], lambda: g.affine_select(o[0], a[0], pat, op, 0.0, base, cm))
-    def mat(n, p, k=128): return (T[n][0:k, p * 128:p * 128 + 128], [(n, p * 128, p * 128 + 128)])
+    def move(o, a, qs="vs"):
+        f = {"v": lambda: g.vector.tensor_copy(o[0], a[0]), "s": lambda: g.scalar.activation(o[0], a[0], F.Copy)}
+        ns = {"v": 50 + GATHER * o[2], "s": 65 + GATHER * o[2]}
+        calls.append([qs, o[1], a[1], {q: (ns[q], ns[q]) for q in qs}, {}, lambda q: emit(q, o[1], a[1], f[q])])
 
-    def dist(o, n, src, base, st, cols, first=True):
-        for p in range(16):
-            lo = base + p
-            mm(o, mat(n, p), B(src, lo, lo + (cols - 1) * st + 1, st), first and p == 0, p == 15)
+    def mm(o, l, r, start, stop): call("t", o[1], l[1] + r[1], CYCLE / 2 * max(min(64, l[2]), r[2]), lambda: g.tensor.matmul(o[0], l[0], r[0], start, stop))
 
-    def spread(src, first):
-        for p in range(16): mm(B("PA", p, p + 433, 16), mat("DA2", p), src, first, first or p == 15)
+    def one(k):
+        L = calls[-k:]
+        ns = sum(c[3]["t"][0] for c in L)
+        calls[-k:] = [["t", sum((c[1] for c in L), []), sum((c[2] for c in L), []), {"t": (ns, ns)}, {}, lambda q: [c[5](q) for c in L]]]
+
+    def iota(o, pat, base, cm, alone=False):
+        call("g", o[1], [], 130 + 2 * CYCLE * o[2], lambda: g.iota(o[0], pat, base, cm, allow_small_or_imprecise_dtypes=True), alone)
+
+    def asel(o, a, pat, op, base, cm, c=0.0): call("g", o[1], a[1], 170 + 2 * CYCLE * o[2], lambda: g.affine_select(o[0], a[0], pat, op, c, base, cm))
+    def dma(q, o, a, ns=2000): calls.append([q + "d", o[1], a[1], {q: (60, ns)}, {}, lambda _: dma_now(q, o, a)])
+
+    def send(land, a, sem, step):
+        dst, src = T.cores[(rank + step) % N], T.cores[(rank - step) % N]
+        rid, pid = topo.addr(dst, core)
+        lanes = topo.engines(core, dst)[:8]
+        calls.append(["gd", [], a[1], {"g": (600, 1800)}, {}, lambda _: send_now(land, a, sem, (rid, pid, sum(1 << e for e in lanes), len(lanes)))])
+        calls.append(["x", land[1], [], {"x": (0, 1)}, {len(calls) - 1: 0}, lambda _: arrive(land, sem, len(topo.engines(src, core)[:8]))])
+
+    def sq(n, k=128, m=128): return B(n, 0, m, 1, k)
+    def lw(n, p): return B("LW", 144 * SHIFTED.index(n) + 15 - p, 128)
+    def lwc(n, d=0): return B("LW", 144 * SHIFTED.index(n) + 15 + d, 8, 16)
+
+    def dist(o, n, src, base, cols, first=True, last=True):
+        for p in range(16): mm(o, lw(n, p), B(src, base + p, cols, 16), first and p == 0, last and p == 15)
+        one(16)
+
+    def spread(bank, row, src, last=False):
+        for p in range(16): mm(B(bank, 28 * p, 28), B("DA", 128 * p + 15 - row, 128), src, False, last and p == 15)
+        one(16)
+
+    def unmix(l, src, last=False):
+        for p in range(16): mm(B("PT", 28 * p, 28), l, B(src, p, 28, 16), False, last and p == 15)
+        one(16)
 
     slots = {}
 
-    def slot(buf, width):
-        def f(name):
-            k = (buf, name[:-1] + "0" if name[-1] == "2" and buf != "DB" else name)
-            if k not in slots: slots[k] = sum(1 for x in slots if x[0] == buf)
-            return B(buf, slots[k] * width, slots[k] * width + 28)
+    def slot(buf):
+        def f(name, n=1):
+            if (buf, name) not in slots:
+                slots[(buf, name)] = sum(x[1] for k, x in slots.items() if k[0] == buf), n
+            return B(buf, slots[(buf, name)][0] * 28, 28 * n)
         return f
 
-    DF, DN, DU, DB = slot("DF", 28), slot("DN", 28), slot("DU", 28), slot("DB", 32)
+    DF, DN, DU, DB = slot("DF"), slot("DN"), slot("DU"), slot("DB")
+    def part(v, j, n=1): return B(v[3], v[1][0][1] + 28 * j, 28 * n)
+    def half(v, par): return B(v[3], v[1][0][1] + par, 14, 2)
+    cols = {}
+    def col(n, p=128, k=1): return B("COL", cols.setdefault(n, (sum(x[1] for x in cols.values()), k))[0], 1, 1, p)
+    def colj(n, j, p=128, k=1): return B("COL", cols[n][0] + j, k, 1, p)
+    def row(r, k=1): return B("OH", r, k)
+    def own(t, n=28): return B("V0" if t == 0 else "LD%d" % (t - 1), 0, n)
+    def ghost(t): return B("LG" if t == 0 else "GN%d" % (t - 1), 0, 28)
+    def dint(t): return B("VI", 0, 28) if t == 0 else DN("d")
+    def zin(t): return B("Z0" if t == 0 else "LZ%d" % (t - 1), 0, M)
+    def gf(t): return B("GF", 1 + (t & 1), M, 2)
+    REC = B("REC", 0, W + 16)
+    G8 = B("G8", 0, 8)
+    aD = DF("a")
 
-    def wide(f, n, s):
-        vs = [f("%s%d%s" % (n, j, s)) for j in range(3)]
-        return B(vs[0][1][0][0], vs[0][1][0][1], vs[2][1][0][2])
+    def loads():
+        dma("y", B("GI", 0, V), (T.gl[:, :], []))
+        dma("s", B("VI", 0, 28), (T.val[:, :], []))
+        dma("y", B("NBI", 0, V), (T.nb[:, :], []))
+        dma("y", B("REC", 0, W), (T.rec[:, :], []), 5000)
+        dma("y", B("Z0", 0, M), (T.zl[:, :], []))
+        dma("y", B("THI", 0, M, 1, 8), (T.th[:, :], []))
 
-    def out32(name):
-        b, lo, hi = DB(name)[1][0]
-        return B(b, lo, lo + 32)
+    def neighbours():
+        dma("y", B("NW", 0, W), B("REC", 0, W), 4000)
+        dma("y", B("NW", W, 2 * CELLS - W), B("REC", 0, 2 * CELLS - W), 4000)
+        cp(B("NBD", 0, V), B("NBI", 0, V))
+        tt(B("NBD", V, V), B("NBI", 0, V), B("NBD", 0, V), A.subtract)
+        for r in range(2):
+            dma("y", (T["NW"][r:r + 113:16, 0:2 * CELLS], [("NW", 0, 2 * CELLS, r, r + 113)]), B("NBD", r * V, V), 3000)
 
-    def lanes(src, dst): return topo.engines(src, dst)[:8]
+    def consts():
+        fill(B("ONE", 0, V), 1.0)
+        iota(B("IOQ", 0, 1), [[0, 1]], 0, 1)
+        iota(B("IO", 0, 16), [[1, 16]], 0, 0)
+        iota(B("CR", 0, V, 1, 32), [[0, 16], [1, 28]], 0, 0)
+        iota(B("CR", 0, V, 1, 64, 32), [[1, M], [0, 2]], 1, 0, True)
+        iota(B("CR", 0, V, 1, 96, 64), [[1, 16], [0, 28]], 0, 0, True)
+        asel(G8, B("ONE", 0, 8), [[-16, 8]], A.is_ge, 0, 1)
+        asel(G8, G8, [[16, 8]], A.is_ge, 15, -1)
+        for k in range(0, len(SHIFTED), 2): fill(B("LW", 144 * k, 288), 0.0)
+        fill(B("SLE", 0, 256), 0.0)
+        fill(B("SLE", 1, 8, 16, 1), 1.0)
+        fill(B("SLE", 2, 8, 16, 33, 32), 1.0)
+        fill(B("SLV", 6, 8, 16, 1), 1.0)
+        fill(B("SLV", 5, 8, 16, 65, 64), 1.0)
+        fill(B("TN", 0, 464), 0.0)
+        ts(B("IOQ", 1, 1), B("IOQ", 0, 1), 15, A.bitwise_and)
+        cp(col("p"), B("IOQ", 1, 1))
+        ts(B("OH", 0, 16), B("IO", 0, 16), col("p"), A.is_equal)
+        ts(col("-r0"), row(0), -1.0, A.mult)
+        cp(lwc("L1"), G8)
+        for k in range(4): fill(B("DA", 516 * k, 516), 0.0)
+        asel(sq("IDN"), B("ONE", 0, 128), [[1, 128]], A.is_equal, 0, -1)
+        asel(B("DA", 15, 128, 16), B("ONE", 0, 128), [[-1, 16], [-16, 8]], A.is_equal, 0, 1)
+        iota(B("IDS", 0, M), [[1, 16], [0, 14]], 0, 0)
+        iota(DF("c"), [[1, 28]], 0, 0)
+        iota(DF("ch"), [[2, 14], [0, 2]], -V, 0)
+        iota(DB("cl"), [[0, 14], [1, 2]], 0, 0)
+        iota(B("J16", 0, 84), [[16, 3], [0, 28]], 0, 0)
+        iota(B("IOX", 0, V), [[1, 28], [28, 16]], 0, 0)
+        ts(col("we0"), row(0), float(2 ** 17), A.mult, row(2), A.add)
+        ts(col("we"), row(1), 256.0, A.mult, col("we0"), A.add)
+        act(lwc("LE"), G8, scale=col("we"))
+        act(B("RAP", 0, V), B("ONE", 0, V), scale=8192.0)
+        act(B("RAP", 0, 28, 16), B("ONE", 0, 28), scale=-HUGE)
+        ts(col("28p"), col("p"), 28.0, A.mult)
+        ts(col("wk"), col("p"), 448.0, A.mult, 448.0, A.add)
+        ts(col("wo"), row(0), row(1), A.add)
+        ts(col("28r6"), row(6), 28.0, A.mult)
+        fill(B("KS", 0, 128, 1, 1), 0.0)
+        fill(B("KS", 7, 8, 16, 1), 2.0)
+        fill(B("KS", 128, 128, 1, 1), -1.0)
+        fill(B("KS", 256, 128, 1, 1), -0.25)
+        fill(B("SB", 0, 192), 0.0)
+        fill(B("GF", 0, 1), -5.0)
+        fill(B("GF", V + 1, 15), -5.0)
+        fill(B("REC", W, 16), 0.0)
+        fill(B("PB", 0, 1), 0.0)
+        fill(B("PB", V + 1, 15), 0.0)
+        act(lwc("L64"), G8, scale=64.0)
+        act(lwc("LK"), G8, scale=col("wk"))
+        act(lwc("LO"), G8, scale=col("wo"))
+        act(aD, DF("c"), bias=col("28p"))
+        act(DB("ch"), DF("ch"), bias=col("28p"))
+        act(sq("P18"), sq("IDN"), scale=float(2 ** 18))
+        act(B("RAM", 0, V), B("RAP", 0, V), scale=-1.0)
+        ts(B("ID", 0, M), B("IDS", 0, M), col("p"), A.is_equal)
+        ts(DF("a37"), aD, 0.5, A.mult, 9.25, A.add)
+        ts(DF("a17"), aD, 2.0, A.mult, 17.0, A.add)
+        ts(DF("a613"), aD, 32.0, A.mult, 16.0 * 613, A.add)
+        iota(B("S17", 0, V), [[2, V]], 17, 0)
+        asel(sq("BD"), B("ONE", 0, 128), [[-16, 8], [0, 16]], A.is_ge, 0, 1)
+        asel(sq("BD"), sq("BD"), [[16, 8], [0, 16]], A.is_ge, 15, -1)
+        for n, k in (("i", 2), ("s1", 4), ("ws", 3), ("hi", 4), ("lo", 4), ("w", 4)): col(n, 128, k)
+        iota(colj("i", 0, 128, 2), [[-H, 2]], -16, -16)
+        iota(colj("s1", 0, 128, 4), [[2, 2], [V, 2]], 613, 4)
+        asel(B("IB", 0, 64), B("ONE", 0, 64), [[0, 64]], A.is_equal, -112, 1)
+        iota(B("LPI", 0, 24), [[48, 2], [4, 4], [1, 3]], 0, 0)
+        iota(B("PP", 0, 384), [[0, 8], [1, 48]], 0, 0)
+        iota(B("PC", 0, V), [[1, 28], [0, 16]], 28, 0)
+        iota(B("IOM", 0, 128), [[1, 8], [0, 16]], 0, 0)
+        act(lwc("L2"), G8, scale=row(2))
+        for d in range(2):
+            act(lwc("DP", d), G8)
+            act(lwc("DM", d), G8, scale=-1.0)
+        total(col("567"), row(5, 3))
+        total(col("012"), row(0, 3))
+        ts(col("w34"), row(3), row(4), A.add, 4096.0, A.mult)
+        ts(colj("ws", 0, 128, 3), row(5, 3), col("w34"), A.add)
+        ts(col("w15"), row(15), float(2 ** 25), A.mult)
+        fill(B("S15", 0, 16), 0.0)
+        act(sq("I567"), sq("IDN"), scale=col("567"))
+        act(sq("R2B"), sq("BD"), scale=row(2))
+        for j in range(3): act(B("SL1", 8 * j, 8), G8, scale=colj("ws", j))
+        act(B("SL1", 24, 8), G8, scale=row(10))
+        for j in range(2): act(B("SL2", 8 * j, 8), G8, scale=row(8 + j))
+        act(B("S15", 16, 8), G8, scale=col("w15"))
+        act(B("THS", 0, 24, 1, 8), B("ONE", 0, 24, 1, 8), scale=4096.0)
+        asel(B("THS", 0, 24, 1, 8), B("THS", 0, 24, 1, 8), [[0, 3], [1, 8]], A.is_equal, 0, -1)
+        act(sq("C64"), B("ONE", 0, 128), scale=-64.0)
+        asel(sq("UPM", 128, 112), sq("C64", 128, 112), [[1, 112]], A.is_gt, 0, -1)
+        asel(sq("UPM", 128, 112), sq("UPM", 128, 112), [[0, 112]], A.not_equal, -112, 1, 64.0 * CAP)
+        act(sq("BIG"), sq("IDN"), scale=-float(2 ** 20))
+        act(B("RAK", 0, 384), B("ONE", 0, 384), scale=256.0)
+        act(B("RAK", 0, 24, 16), B("ONE", 0, 24), scale=-HUGE)
+        cp(B("THB", 0, M, 1, 8), B("THI", 0, M, 1, 8))
+        tt(B("THB", M, M, 1, 8), B("THI", 0, M, 1, 8), B("THB", 0, M, 1, 8), A.subtract)
+        fill(col("c"), 4095.0)
+        for n in ("X", "INJ", "TM"): fill(B(n, 0, 64), 0.0)
+        cp(B("CB", 0, 4), colj("s1", 0, 128, 4))
+        ts(colj("hi", 0, 128, 4), B("CB", 0, 4), 16.0, A.mult)
+        tt(colj("lo", 0, 128, 4), colj("s1", 0, 128, 4), B("CB", 0, 4), A.subtract)
+        ts(colj("lo", 0, 128, 4), colj("lo", 0, 128, 4), 16.0, A.mult)
+        for m in range(8):
+            act(B("DG", 112 * m, 112, 1, 112), sq("IDN", 112, 112), scale=colj(("hi", "lo")[m & 1], m >> 1, 112))
+        ts(B("LPI", 0, 24), B("LPI", 0, 24), 1, A.arith_shift_right)
+        cp(B("LP", 0, 24), B("LPI", 0, 24))
+        ts(col("la"), col("p"), 8.0, A.is_ge, 16.0, A.mult)
+        ts(col("lb"), col("p"), 8.0, A.add)
+        ts(B("LC", 0, 28), B("ONE", 0, 28), col("la"), A.mult, col("lb"), A.add)
+        ts(B("PP", 0, 384), B("PP", 0, 384), 31, A.bitwise_and)
+        ts(B("IOQ", 2, 1), B("IOQ", 0, 1), 7, A.bitwise_and)
+        cp(col("r7"), B("IOQ", 2, 1))
+        ts(B("G8", 8, 8), B("IO", 0, 8), col("r7"), A.is_equal)
+        ts(col("-p"), col("p"), -1.0, A.mult)
+        ts(col("-64r0"), row(0), -64.0, A.mult)
+        fill(colj("w", 0, 128, 4), 0.0)
 
-    def route(dst):
-        c = T.cores[dst % N]
-        rid, pid = topo.addr(c, core)
-        return (rid, pid, sum(1 << e for e in lanes(core, c)), len(lanes(core, c)))
+        def steps(j, k, L):
+            for hi, w in L: asel(colj("w", j, 128, k), colj("w", j, 128, k), [[0, k]], A.is_ge, -hi, 1, w)
+        steps(0, 2, [(104, 0.5), (96, 0.0)])
+        steps(0, 1, [(48, 0.5)])
+        steps(1, 1, [(48, 1.0)])
+        steps(0, 2, [(40, -float(2 ** 17)), (32, 0.0), (24, float(2 ** 17)), (16, 256.0), (8, 14.0)])
+        steps(2, 1, [(40, 1.0), (32, 0.0), (16, 1.0), (8, 28.0)])
+        steps(3, 1, [(80, 32.0), (72, 0.0)])
+        iota(B("RM", 0, H // 2), [[0, 56], [255, 16]], 0, 0)
+        for j in range(2): act(lwc("EE%d" % j), B("G8", 8, 8), scale=colj("w", j))
+        ts(sq("EJ"), B("IOM", 0, 128), col("r7"), A.is_equal, colj("w", 2), A.mult)
+        ts(sq("EB"), B("IOM", 0, 128), col("r7"), A.is_equal, colj("w", 3), A.mult)
+        act(sq("B32"), sq("BD"), scale=32.0)
+        act(sq("N1K"), sq("IDN"), scale=-1024.0)
+        act(sq("HLF"), sq("IDN"), scale=0.5)
+        act(sq("I012"), sq("IDN"), scale=col("012"))
 
-    def came(src, view, sem): arrive(view, sem, len(lanes(T.cores[src % N], core)))
+    def sizes(par, bank):
+        mm(B(bank, 0, M), sq("SLE", 64), B("CR", par, M, 2, 64), True, False)
+        mm(B(bank, 0, M), lw("L1", 0), B("G0", par, M, 2), False, True)
 
-    col = lambda j, p=128: B("COL", j, j + 1, 1, p)
-    dma("y", B("GI", 0, V), (T.gl[:, :], []))
-    dma("y", B("VI", 0, V, 1, 8), (T.val[:, :], []))
-    dma("y", B("NBI", 0, V), (T.nb[:, :], []))
-    dma("y", B("Z0", 0, M), (T.zl[:, :], []))
-    dma("y", B("REC", 0, W), (T.rec[:, :], []))
-    dma("y", B("THI", 0, M, 1, 8), (T.th[:, :], []))
-    for t in range(3):
-        came(rank + 1, B("LG%d" % t, 0, 32), "rg%d" % t)
-        came(rank - 1, B("LN%d" % t, 0, 32), "rn%d" % t)
-        came(rank - 1 - t, B("LZ%d" % t, 0, M), "rz%d" % t)
-    iota(B("IOQ", 0, 1), [[0, 1]], 0, 1)
-    iota(B("IOM", 0, 128), [[1, 8], [0, 16]], 0, 0)
-    fill(B("ONE", 0, 128), 1.0)
-    fill(B("WD0", 0, CH), 0.0)
-    asel(B("IDN", 0, 128), B("ONE", 0, 128), [[1, 128]], A.is_equal, 0, -1)
-    iota(B("X34", 0, 512), [[256, 2], [0, 256]], 0, 0)
-    iota(B("X34", 512, 1024), [[0, 2], [1, 256]], 0, 0)
-    iota(B("IOX", 0, 464), [[1, 464]], 0, 0)
-    asel(B("E8", 0, 128, 1, 8), B("ONE", 0, 128, 1, 8), [[1, 128]], A.is_equal, -2, -16)
-    iota(B("IOC", 0, 28), [[16, 28]], 0, 0)
-    ts(B("IOQ", 1, 2), B("IOQ", 0, 1), 15, A.bitwise_and)
-    ts(B("IOQ", 2, 3), B("IOQ", 0, 1), 4, A.arith_shift_right)
-    cp(col(0), B("IOQ", 1, 2))
-    cp(col(1), B("IOQ", 2, 3))
-    ts(B("BD", 0, 128), B("IOM", 0, 128), col(1), A.is_equal)
-    for j in range(5): ts(col(4 + j), col(0), float(j), A.is_equal)
-    ts(col(9), col(4), -128.0, A.mult)
-    ts(col(11), col(5), -256.0, A.mult, col(9), A.add)
-    ts(col(10), col(4), -256.0, A.mult)
-    ts(col(14), col(5), -128.0, A.mult, col(10), A.add)
-    ts(col(17), col(4), col(5), A.add)
-    ts(B("TN", 0, 1), col(17), -256.0, A.mult)
-    fill(B("TN", V + 1, 464), 0.0)
-    fill(B("N0W", 0, 256), 0.0)
-    ts(B("N0W", 0, 113, 16), B("BD", 0, 113, 16), 16.0, A.mult)
-    ts(B("N1W", 1, 114, 16), B("BD", 0, 113, 16), 16.0, A.mult)
-    ts(B("R2B", 0, 128), B("BD", 0, 128), col(6), A.mult)
-    ts(B("I3", 0, 128), B("IDN", 0, 128), col(7), A.mult)
-    ts(B("I4", 0, 128), B("IDN", 0, 128), col(8), A.mult)
-    ts(B("G0", 0, V), B("GI", 0, V), 0.0, A.is_ge)
-    ts(B("GU", 0, M), B("GI", 0, V - 1, 2), 1.0, A.add)
-    ts(B("GU", M, V), B("GI", 1, V, 2), 1.0, A.add)
-    cp(B("VB", 0, V, 1, 8), B("VI", 0, V, 1, 8))
+    def gather(out, tab, off, n, step, qs="vs"):
+        for c in range(0, n, step): move(B("KW", out + 16 * c, 16 * step), ind(B(tab, 0, 464), B(off[0], off[1] + c, step)), qs)
 
-    def sizes(last):
-        mm(B("PA", 0, V), B("I3", 0, 128), B("X34", 1, V + 1), True, False)
-        mm(B("PA", 0, V), B("I4", 0, 128), B("X34", 513, 513 + V), False, False)
-        mm(B("PA", 0, V - 1, 2), B("N0W", 0, 128), B("G0", 0, V - 1, 2), False, False)
-        mm(B("PA", 1, V, 2), B("N1W", 0, 128), B("G0", 1, V, 2), False, last)
+    def keys_e(bank, base, n):
+        for p in range(16): mm(B(bank, 0, n), lw("LE", p), B("KW", base + n * p, n), p == 0, p == 15)
 
-    sizes(False)
-    mm(B("PA", 0, V), B("E8", 0, 128, 1, 8), B("VB", 0, V, 1, 8), False, True)
-    ts(B("TN", 1, V, 2), B("PA", 0, V - 1, 2), col(11), A.add)
-    ts(B("TN", 2, V + 1, 2), B("PA", 1, V, 2), col(14), A.add)
-    TNW = B("TN", 0, 464)
+    def winners(par, bank):
+        scan(B("SE", 0, M), B("RAP", 0, M), B(bank, 0, M), A.add, A.max)
+        ts(half(DF("key2"), par), B("SE", 15, 14, 16), 0.0, A.max)
 
-    def table(values, alone=False):
-        if alone:
-            spread(B("DT", 0, 28), True)
-            act(B("TN", 1, V + 1), B("PA", 0, V))
-            return
-        sizes(not values)
-        if values: spread(B("DT", 0, 28), False)
-        act(B("TN", 1, V, 2), B("PA", 0, V - 1, 2), bias=col(11))
-        act(B("TN", 2, V + 1, 2), B("PA", 1, V, 2), bias=col(14))
+    def table2():
+        mm(B("Q", 0, V), sq("SLE", 64), B("CR", 0, V, 1, 64), True, False)
+        mm(B("Q", 0, V), lw("L1", 0), B("G0", 0, V), False, True)
+        act(B("TN", 1, M, 2), B("Q", 0, M, 2), bias=row(0))
+        act(B("TN", 2, M, 2), B("Q", 1, M, 2), bias=col("-64r0"))
 
-    def sgather(c0, c1): act(B("KW", 16 * c0, 16 * c1), ind(TNW, B("GU", c0, c1)))
-    def vgather(c0, c1): cp(B("KW", 16 * c0, 16 * c1), ind(TNW, B("GU", c0, c1)))
-    turn = [0]
+    def elected(t):
+        par, e = t & 1, DN("e")
+        if t: cp(DN("key"), DF("key%d" % t))
+        ts(e, DN("key"), 255, A.bitwise_and)
+        ts(DN("vc"), DN("key"), 8, A.arith_shift_right, 31, A.bitwise_and)
+        ts(DU("z"), e, -1.0, A.add)
+        ts(DU("g"), e, 2.0, A.mult, par - 1.0, A.add)
+        cp(DU("vc"), DN("vc"))
+        act(B("MSK", 0, V), ind(B("ID", 0, M), DU("z")))
+        tt(B("MAT", 0, V), ind(B("GF", 0, 464), DU("g")), B("IOX", 0, V), A.is_equal)
+        mm(B("PM", 0, 28), sq("IDN"), DB("ch"), True, False)
+        mm(B("PM", 0, 28), sq("IDN"), DB("cl"), False, False)
+        dist(B("PM", 0, 28), "LK", "MAT", 0, 28, first=False)
+        ts(DF("u"), e, 4.0, A.mult, 13.0 + 2 * par, A.add)
+        ts(DF("s"), e, 64.0, A.mult, 16.0 * (609 + 2 * par), A.add)
+        cp(DB("e"), e)
+        tt(DF("m"), DF("u"), aD, A.mult)
+        cp(DU("nk"), B("PM", 0, 28))
+        ts(DB("no"), B("PM", 0, 28), 0.0, A.is_lt)
+        act(B("OG", 0, V), ind(B("NW", 0, 2 * CELLS), DU("nk")))
+        dist(B("PM", 32, 28), "LO", "OG", 0, 28)
+        cp(DU("o"), B("PM", 32, 28))
+        ts(DF("s37"), B("PM", 32, 28), 32.0, A.mult, 16.0 * 37, A.add)
+        tt(DF("ob"), B("PM", 32, 28), DF("a17"), A.mult)
 
-    def half():
-        turn[0] ^= 1
-        return turn[0] * CH
+    def values(t, who):
+        nxt = (t + 1) & 1
+        mm(B("Q", 0, V), sq("SLV", 96), B("CR", 0, V, 1, 96), True, False)
+        if who == 0 and t < 2:
+            mm(B("Q", nxt, M, 2), lw("L1", 7), B("G0", nxt, M, 2), False, False)
+            mm(B("Q", nxt, M, 2), B("KS", 0, 128, 1, 1), B("ONE", 0, M, 1, 1), False, False)
+        spread("Q", 2, ghost(t) if who else own(t), True)
+        if who: act(B("VT", V, V), B("Q", 0, V), bias=col("28r6"))
+        else: act(B("VT", 0, V), B("Q", 0, V))
 
-    def scans(lo, hi):
-        while lo < hi:
-            n, b = min(CH, hi - lo), half()
-            scan(B("KT", b, b + n), B("RA", 0, n), B("KW", lo, lo + n), A.add, A.max)
-            cp(B("KC", lo // 16, (lo + n) // 16), B("KT", b + 15, b + n, 16))
-            lo += n
+    def place(u, x):
+        ts(x, x, 4, A.arith_shift_right, W - 1, A.bitwise_and)
+        cp(u, x)
 
-    CUT = 320
-    for c in range(0, CUT, 80): sgather(c, c + 80)
-    fill(B("LW", 0, 2048), 0.0)
-    for a in range(8): cp(B("LW", 16 * a, 16 * a + 129 * 15 + 1, 129), B("BD", 16 * a, 16 * a + 16))
-    for n, op, b in (("LWD", A.is_equal, -2), ("LWN", A.is_ge, -3)):
-        asel(B(n, 0, 2048), B("LW", 0, 2048), [[0, 16], [-16, 8], [0, 16]], op, b, 1)
-    iota(B("SF", 0, 912), [[0, 57], [1, 16]], 0, 0)
-    asel(B("LWE1", 0, 2048), B("LW", 0, 2048), [[0, 16], [-16, 8], [0, 16]], A.is_equal, -1, 1)
-    for j, b in enumerate((1, 3, 613, 615)): iota(B("S1", j * M, j * M + M), [[4, M]], b, 0)
-    fill(B("RA", 0, CH), 1.0)
-    fill(B("RA", 0, CH - 15, 16), -512.0)
-    fill(B("KC", V, 464), 0.0)
-    vgather(CUT, 448)
-    for n, m in (("NW", 4), ("WP", 2), ("WD1", 2), ("WD2", 2)):
-        for j in range(m): dma("y", B(n, j * CH, j * CH + CH), B("WD0", 0, CH))
-    dma("y", B("WD0", CH, 2 * CH), B("WP", CH, 2 * CH))
-    scans(16 * CUT, 7168)
-    aD = DF("aD")
-    ts(aD, B("IOC", 0, 28), col(0), A.add)
-    ts(DF("A37"), aD, 2.0, A.mult, 37.0, A.add)
-    ts(DF("A1"), aD, 2.0, A.mult, 1.0, A.add)
-    ts(DF("A613"), aD, 2.0, A.mult, 613.0, A.add)
-    ts(DF("CNB"), aD, -448.0, A.add)
-    ts(DF("CPOS"), aD, float(CELLS), A.add)
-    ts(B("IOQ", 5, 6), B("IOQ", 0, 1), 1, A.bitwise_and)
-    ts(col(3), B("IOQ", 5, 6), 3576.0, A.mult, 15.0, A.add)
-    ts(DF("CM"), aD, 8.0, A.mult, col(3), A.add)
-    ts(col(2), col(0), 1.0, A.add)
-    for j, x in ((28, -1.0), (29, 35.0), (30, 8192.0)): fill(col(j), x)
-    ts(col(9), col(4), 16.0, A.mult, col(5), A.add)
-    act(B("LWE0", 0, 2048), B("LW", 0, 2048), scale=col(4))
-    act(B("LWK", 0, 2048), B("LW", 0, 2048), scale=col(2))
-    scans(0, 16 * CUT)
-
-    def base1(rows):
-        for p in range(16):
-            lo = (p & 1) * M + (p >> 1)
-            mm(B("PB", 0, 28), mat(rows, p), B("KC", lo, lo + 27 * 8 + 1, 8), p == 0, p == 15)
-
-    def base2(nm):
-        ts(DN("kI" + nm), B("PB", 0, 28), 128.0, A.add)
-        ts(DF("val" + nm), B("PB", 0, 28), -200.0, A.is_gt)
-        ts(DN("r" + nm), DN("kI" + nm), 15, A.bitwise_and)
-        tt(DN("ce" + nm), DF("CM"), DN("r" + nm), A.subtract)
-        cp(DU("ce" + nm), DN("ce" + nm))
-        act(B("NG", 0, V), ind(B("KW", 0, 7168), DU("ce" + nm)))
-        dist(B("PB", 32, 60), "LWN", "NG", 0, 16, 28)
-
-    def base3(nm, e): tt(e, B("PB", 32, 60), DF("val" + nm), A.mult)
-
-    def send_moved(t): send(B("LG%d" % t, 0, 32), out32("mv%d" % t), "rg%d" % t, route(rank + N - 1))
-    def zin(t): return B("Z0", 0, M) if t == 0 else B("LZ%d" % (t - 1), 0, M)
-    def rec(u): return ind(B("REC", 0, W + 16), DU(u))
-
-    def E1(t):
-        s = str(t)
-        e1, em, ei = DF("e" + s), DN("em" + s), DN("ei" + s)
-        cp(DU("e" + s), e1)
-        act(B("MSK", 0, V), ind(B("ID", 0, 912), DU("e" + s)))
-        ts(em, e1, -1.0, A.add)
-        ts(DN("ec" + s), em, 4, A.arith_shift_right)
-        cp(DU("ec" + s), DN("ec" + s))
-        ts(ei, em, 1, A.arith_shift_right)
-        cp(DU("ei" + s), ei)
-
-    def E2(t):
-        s = str(t)
-        tt(B("MAT", 0, V), ind(B("GF", 0, 464), DU("e" + s)), B("IOX", 1, V + 1), A.is_equal)
-        dist(B("PB", 64, 92), "LWK", "MAT", 0, 16, 28)
-        ts(DF("s1" + s), DF("e" + s), 2.0, A.mult, -1.0, A.add)
-        tt(DN("m1" + s), DF("s1" + s), aD, A.mult)
-        ts(DN("m2" + s), DN("m1" + s), 4, A.arith_shift_right)
-        tt(DF("c1" + s), DN("m2" + s), aD, A.add)
-        ts(DF("sl0" + s), DF("s1" + s), 612.0, A.add)
-
-    def E3(t):
-        s = str(t)
-        ts(DF("nk" + s), B("PB", 64, 92), 448.0, A.mult)
-        cp(DF("kk" + s), B("PB", 64, 92))
-        tt(DF("nk" + s), DF("nk" + s), DF("CNB"), A.add)
-        cp(DU("nk" + s), DF("nk" + s))
-        act(B("OG", 0, V), ind(B("NW", 0, 7168), DU("nk" + s)))
-        dist(B("PB", 96, 124), "LWO", "OG", 0, 16, 28)
-
-    def E4(t):
-        s = str(t)
-        ts(DF("mi" + s), DF("kk" + s), 0.5, A.is_gt)
-        t1 = DF("ps" + s)
-        ts(t1, DN("ei" + s), 16.0, A.mult, -1.0 - CELLS, A.add)
-        tt(t1, t1, DF("kk" + s), A.add)
-        tt(t1, t1, aD, A.subtract)
-        tt(t1, t1, DF("mi" + s), A.mult)
-        tt(t1, t1, DF("CPOS"), A.add)
-        cp(DU("ps" + s), t1)
-
-    def E5a(t):
-        s = str(t)
-        ts(DU("o" + s), B("PB", 96, 124), 1.0, A.add)
-        act(B("MSK", V, 2 * V), ind(B("ID", 0, 912), DU("o" + s)))
-
-    def E5b(t):
-        s = str(t)
-        cp(DN("o" + s), B("PB", 96, 124))
-        ts(DN("oc" + s), DN("o" + s), 4, A.arith_shift_right)
-        cp(DU("oc" + s), DN("oc" + s))
-        tt(DN("om" + s), DN("o" + s), DF("A1"), A.mult)
-        ts(DN("om" + s), DN("om" + s), 4, A.arith_shift_right)
-        tt(DF("ob" + s), DN("om" + s), DN("o" + s), A.add)
-        ts(DF("s37" + s), DN("o" + s), 2.0, A.mult, 37.0, A.add)
-
-    def D1(t):
-        s = str(t)
-        tt(B("GD", 0, V), ind(B("DT", 0, 64), DU("ec" + s)), B("MSK", 0, V), A.mult)
-        dist(B("PD", 0, 28), "LW", "GD", 0, 16, 28)
-        for j in range(3): ts(DN("pj%d%s" % (j, s)), DN("d" + s), float(j), A.add)
-        pj = wide(DN, "pj", s)
+    def trials(t):
+        d, pj, b = dint(t), DN("p", 2), DF("b", 3)
+        tt(B("GD", 0, V), ind(own(t, 32), DU("vc")), B("MSK", 0, V), A.mult)
+        dist(B("PD", 0, 28), "L64", "GD", 0, 28)
+        act(B("ZE", 0, V), ind(zin(t), DU("z")))
+        if t: cp(d, own(t))
+        for j in range(2): ts(part(pj, j), d, j + 1.0, A.add)
+        tt(part(b, 0), d, DF("s"), A.mult)
         ts(pj, pj, 15, A.bitwise_and)
+        for j in range(2): tt(part(b, j + 1), part(pj, j), DF("s"), A.mult)
+        cp(DB("p", 2), pj)
+        tt(DF("q"), B("PD", 0, 28), DF("a37"), A.mult)
+        tt(DF("q"), DF("q"), DF("m"), A.add)
+        for j in range(3): tt(part(DN("ix", 3), j), part(DF("b", 3), j), DF("q"), A.add)
+        place(DU("ix", 3), DN("ix", 3))
+        mm(B("PD", 64, 84), sq("IDN"), B("J16", 0, 84), True, False)
+        mm(B("PD", 64, 28), sq("IDN"), own(t), False, False)
+        mm(B("PD", 92, 56), sq("IDN"), DB("p", 2), False, False)
+        for j in (1, 2): mm(B("PD", 64 + 28 * j, 28), sq("P18"), DB("no"), False, False)
+        one(5)
+        for j in range(3):
+            tt(B("MT", j * V, V), ind(REC, part(DU("ix", 3), j)), B("ZE", 0, V), A.max)
+            if j == 1: dist(B("PD", 64, 56), "L64", "MT", 0, 56, first=False, last=False)
+            if j == 2: dist(B("PD", 120, 28), "L64", "MT", 2 * V, 28, first=False)
 
-    def D2(t):
+    def old_damage(t):
+        act(B("VO", 0, V), ind(B("VT", 0, 2 * V), DU("o")))
+        dist(B("PM", 64, 28), "LE", "VO", 0, 28)
+        mm(B("PT", 0, V), lw("L2", 9), B("VT", 0, V), True, False)
+        if t == 1: mm(B("PT", 0, V), sq("I012"), B("TN", 1, V), False, False)
+        spread("PT", 8, DB("e"))
+        unmix(sq("I567"), "VO")
+        tt(DF("ot"), dint(t), DF("s37"), A.mult)
+        tt(DF("od"), B("PM", 64, 28), DF("a613"), A.mult)
+        tt(DF("co"), DF("ob"), DF("od"), A.add)
+        tt(DN("io"), DF("ot"), DF("co"), A.add)
+        place(DU("io"), DN("io"))
+        tt(B("MO", 0, V), ind(REC, DU("io")), B("ZE", 0, V), A.max)
+
+    def choose(t):
         s = str(t)
-        for j in range(3): tt(DF("bs%d%s" % (j, s)), DN("pj%d%s" % (j, s)), DF("sl0" + s), A.mult)
-        tt(DF("qt" + s), B("PD", 0, 28), DF("A37"), A.mult)
-        tt(DF("c0" + s), DF("c1" + s), DF("qt" + s), A.add)
-        for j in range(3): tt(DN("ix%d%s" % (j, s)), DF("bs%d%s" % (j, s)), DF("c0" + s), A.add)
-        ix = wide(DN, "ix", s)
-        ts(ix, ix, 4095, A.bitwise_and)
-        cp(wide(DU, "ix", s), ix)
+        cp(DF("x"), B("PD", 64, 28))
+        tt(DF("x"), B("PD", 92, 28), DF("x"), A.min)
+        tt(DN("x"), B("PD", 120, 28), DF("x"), A.min)
+        ts(DN("nd"), DN("x"), 15, A.bitwise_and)
+        tt(DF("nt"), DN("nd"), DF("s37"), A.mult)
+        cp(B("MV" + s, 0, 28), DN("nd"))
+        tt(DN("in"), DF("nt"), DF("co"), A.add)
+        place(DU("in"), DN("in"))
+        tt(B("MN", 0, V), ind(REC, DU("in")), B("ZE", 0, V), A.max)
+        send(B("LM" + s, 0, 32), B("MV" + s, 0, 32), "rm" + s, -1)
+        spread("PT", 10, B("MV" + s, 0, 28))
+        unmix(lw("DM", 3), "MO")
+        unmix(lw("DP", 3), "MN", True)
+        act(B("T1", 0, V), B("PT", 0, V), scale=row(4))
+        tt(B("PB", 1, V), B("PT", 0, V), B("T1", 0, V), A.subtract)
 
-    def D3(t):
-        tt(B("GD", V, 2 * V), ind(B("DT", 0, 64), DU("oc%d" % t)), B("MSK", V, 2 * V), A.mult)
-        dist(B("PC", 128, 156), "LW", "GD", V, 16, 28)
+    GM = [("GM", 0), ("GM", M), ("GM", 2 * M)]
+    def members(t): ts(B("GM", t * M, M), gf(t), 1.0, A.add)
 
-    def ze(t): act(B("ZE", 0, V), ind(zin(t), DU("ei" + str(t))))
-    def R1(t, j): tt(B("MT", j * V, j * V + V), rec("ix%d%d" % (j, t)), B("ZE", 0, V), A.max)
-
-    def R1x(t):
-        mm(B("PC", 0, 84), B("IDN", 0, 128), B("J84", 0, 84), True, False)
-        dist(B("PC", 0, 84), "LW4", "MT", 0, 16, 84, first=False)
-
-    def D4(t):
-        s = str(t)
-        tt(DF("od" + s), B("PC", 128, 156), DF("A613"), A.mult)
-        tt(DF("co" + s), DF("ob" + s), DF("od" + s), A.add)
-        tt(DF("ot" + s), DN("d" + s), DF("s37" + s), A.mult)
-        tt(DN("io" + s), DF("ot" + s), DF("co" + s), A.add)
-        ts(DN("io" + s), DN("io" + s), 4095, A.bitwise_and)
-        cp(DU("io" + s), DN("io" + s))
-
-    def R2(t):
-        tt(B("MO", 0, V), rec("io%d" % t), B("ZE", 0, V), A.max)
-        act(B("NMO", 0, V), B("MO", 0, V), scale=-1.0)
-
-    def R3(t):
-        s = str(t)
-        cp(DF("x" + s), B("PC", 0, 28))
-        tt(DF("x" + s), B("PC", 28, 56), DF("x" + s), A.min)
-        tt(DN("x" + s), B("PC", 56, 84), DF("x" + s), A.min)
-        ts(DN("x" + s), DN("x" + s), 3, A.bitwise_and)
-        tt(DF("jm" + s), DN("x" + s), DF("mi" + s), A.mult)
-        tt(DN("np" + s), DF("jm" + s), DN("d" + s), A.add)
-        nd = DN("nd" + s)
-        ts(nd, DN("np" + s), 15, A.bitwise_and)
-        for a, b, c, d in (("nt", "s37", "co", "in"), ("pt", "sl0", "c0", "ip")):
-            tt(DF(a + s), nd, DF(b + s), A.mult)
-            tt(DN(d + s), DF(a + s), DF(c + s), A.add)
-            ts(DN(d + s), DN(d + s), 4095, A.bitwise_and)
-            cp(DU(d + s), DN(d + s))
-            if d == "in": tt(B("MN", 0, V), rec("in" + s), B("ZE", 0, V), A.max)
-        act(B("RP", 0, V), rec("ip" + s), scale=0.5)
-        wd = "WD" + s
-        emit("v", [(wd, 0, WIN)], [("MN", 0, V), ("NMO", 0, V)] + DU("ps" + s)[1],
-             lambda: g.vector.tensor_tensor(T[wd][:, 0:WIN].indirect(DU("ps" + s)[0]), T["MN"][:, 0:V], T["NMO"][:, 0:V], A.add))
-        if t < 2:
-            cp(DB("mv%d" % (t + 1)), nd)
-            send_moved(t + 1)
-
-    def open_keys(): mm(B("PK", 0, 512), B("IDN", 0, 128), B("CK", 0, 512), True, False)
-
-    def keys(w, sel, stop):
+    def thresholds(t):
         for h in range(2):
-            for k in range(16):
-                lo = h * 112 * 16 + k
-                o = (T["PK"][0:112, h * 256 + k:h * 256 + 241 + k:16], [("PK", 0, 512)])
-                mm(o, B(w, lo, lo + 111 * 16 + 1, 16), B(sel, 0, 16), False, stop and h == 1 and k == 15)
+            o = B("PN", 24 * h, 24, 1, 112)
+            mm(o, B("THB", 112 * h, 112, 1, 8), B("THS", 0, 24, 1, 8), h == 0, False)
+            mm(o, B("THB", M + 112 * h, 112, 1, 8), B("THS", 0, 24, 1, 8), False, False)
+            mm(o, B("G0", (t & 1) + M * h, 112, 2), B("S15", 0, 24), False, h == 1)
+        one(6)
+        act(B("THC", 0, 48, 1, 112), B("PN", 0, 48, 1, 112), bias=col("c", 112))
 
-    def F1(t):
-        s, par = str(t), t & 1
-        if t == 2: return
-        mm(B("PA", 0, V), B("N0W", 0, 128), B("G0", 0, V), True, True)
-        act(B("TE", 1, V + 1), B("PA", 0, V))
-        act(B("NVO", 0, V), ind(B("TE", 0, 912), DU("e" + s)))
-        ts(DU("kc" + s), DN("ei" + s), float(par * M), A.add)
+    def count():
+        for h in range(2): mm(B("PN", 160, 8), B("ONE", 0, 128, 1, 112), B("INJ", 24 * h, 8, 1, 112), h == 0, h == 1)
+        act(B("CF", 8, 8), B("PN", 160, 8), acc=B("CF", 0, 1))
+        cp(B("CI", 0, 1), B("CF", 0, 1))
+        ts(B("CI", 1, 1), B("CI", 0, 1), 31, A.bitwise_and)
+        ts(col("c"), B("CI", 1, 1), 4096.0, A.mult, 4095.0, A.add)
 
-    def F1b(t):
-        if t < 2: act(B("NVO", V, 2 * V), ind(B("TE", 0, 912), DU("o%d" % t)))
-        mm(B("PA", 0, V), B("LOA", 0, 128), B("OG", 0, V), True, True)
-        act(B("OA", 0, V), B("PA", 0, V), bias=1.0)
+    def slot_bases(t):
+        act(B("S2", 0, M), gf(t), scale=32.0, bias=16.0 * 37)
+        act(B("EM", 0, M), gf(t), scale=-129.0 * 2 ** 15, fn=F.Relu)
+        mm(B("PS", 256, M), sq("R2B"), B("VT", t & 1, M, 2), True, True)
+        tt(B("X1", 0, M), gf(t), B("S17", t & 1, M, 2), A.mult)
+        tt(B("PS", 256, M), B("PS", 256, M), B("S2", 0, M), A.mult)
+        tt(B("CC", 0, M), B("PS", 256, M), B("X1", 0, M), A.add)
 
-    def F1c(t):
+    def keys(t, h):
+        K, E, AB = "K%d" % h, ("Q", "PT")[h], B("AB", 128 * h, 128, 1, 112)
+        for k in range(16): mm(B(E, k, 16, 16, 112), B("KW", H * h + k, 112, 16), B("SL2", 0, 16), k == 0, k == 15)
+        one(16)
+        for k in range(16): mm(B(K, k, 32, 16, 112), B("KW", H * h + k, 112, 16), B("SL1", 0, 32), k == 0, False)
+        one(16)
+        act(AB, B(E, 0, 128, 1, 112), scale=16.0, bias=colj("i", h, 112), fn=F.Abs)
+        for j in (0, 1, 2, 3) if t < 2 else (0, 1, 3): mm(B(K, 128 * j, 128, 1, 112), sq("BIG", 112, 112), AB, False, j == 3)
+        one(4 if t < 2 else 3)
+        n = 384 if t < 2 else 256
+        scan(B("SC", 384 * h, n, 1, 112), B("RAK", 0, n, 1, 112), B(K, 0, n, 1, 112), A.add, A.max)
+        act(B("PA", 256 + 128 * h, 128, 1, 112), B(K, 384, 128, 1, 112), fn=F.Relu)
+        tt(B("PA", 128 * h, 128, 1, 112), B(E, 128, 128, 1, 112), AB, A.min)
+
+    def injured(t):
+        top = B("SC", 15, 48, 16, 112)
+        ts(B("TI", 0, 48, 1, 112), top, 0.0, A.max)
+        tt(B("INJ", 0, 48, 1, 112), top, B("THC", 0, 48, 1, 112), A.is_gt)
+        ts(B("TI", 48, 48, 1, 112), B("TI", 0, 48, 1, 112), 255, A.bitwise_and)
+        tt(B("X", 0, 48, 1, 112), B("TI", 48, 48, 1, 112), B("INJ", 0, 48, 1, 112), A.mult)
+        ts(B("IB", 0, 48, 1, 112), B("X", 0, 48, 1, 112), 28.0, A.is_ge)
+        mm(B("PN", 64, 48, 1, 112), sq("UPM", 113, 112), B("IB", 0, 48, 1, 113), True, False)
+        mm(B("PN", 88, 24, 1, 112), sq("C64", 112, 112), B("IB", 0, 24, 1, 112), False, True)
+        one(2)
+        tt(B("OHP", 0, 384), ind(B("X", 0, 64), B("LP", 0, 24)), B("PP", 0, 384), A.is_equal)
+        tt(B("TM", 0, 48, 1, 112), B("PN", 64, 48, 1, 112), B("X", 0, 48, 1, 112), A.min)
+        tt(B("OHC", 0, V), ind(B("TM", 0, 64), B("LC", 0, 28)), B("PC", 0, V), A.is_equal)
+
+    def notices(t):
         s = str(t)
-        if t < 2: dist(B("PJ", 0, 56), "LWE0", "NVO", 0, 16, 56)
-        tt(B("INL", 0, V), ind(B("GF", 0, 464), DU("e" + s)), B("OA", 0, V), A.is_equal)
-        dist(B("PJ", 64, 92), "LW", "INL", 0, 16, 28)
-
-    def F1k(t):
-        act(B("KV", 0, V), ind(B("KC", 0, 464), DU("kc%d" % t)))
-        dist(B("PJ", 128, 156), "LWE1" if t == 0 else "LWE0", "KV", 0, 16, 28)
-
-    def F2(t):
-        s, par = str(t), t & 1
-        jo, pa, kv = DF("jo" + s), DF("pa" + s), DF("kv" + s)
-        ts(DF("ow" + s), DN("o" + s), 448.0, A.is_lt)
-        ts(jo, B("PJ", 64, 92), 0.5, A.is_lt)
-        tt(jo, jo, DF("ow" + s), A.mult)
-        if t < 2:
-            ts(DN("pa" + s), DN("o" + s), 1, A.bitwise_and)
-            ts(pa, DN("pa" + s), float(1 - par), A.is_equal)
-            tt(pa, pa, jo, A.mult)
-            ts(DF("nf" + s), B("PJ", 0, 28), 255.0, A.is_lt)
-            tt(pa, pa, DF("nf" + s), A.mult)
-            ts(kv, B("PJ", 128, 156), 128.0, A.add)
-            tt(kv, B("PJ", 28, 56), kv, A.is_gt)
-            tt(pa, pa, kv, A.mult)
-            ts(pa, pa, 128.0, A.mult)
-            ts(jo, jo, 64.0, A.mult)
-            tt(DB("fl"), jo, pa, A.add)
-        else: ts(DB("fl"), jo, 64.0, A.mult)
-        mm(B("PA", 0, V), B("IP", 0, 128), B("OG", 0, V), True, False)
-        spread(DB("fl"), False)
-        act(B("PAY", 0, V), B("PA", 0, V))
-
-    def F3(t):
-        u = DU("ps%d" % t)
-        emit("v", [("WP", 0, WIN)], [("PAY", 0, V)] + u[1], lambda: g.vector.tensor_copy(T["WP"][:, 0:WIN].indirect(u[0]), T["PAY"][:, 0:V]))
-
-    it = lambda k, n=32: B("IT", 32 * k, 32 * k + n, 1, 112)
-    ii = lambda k: B("II", 32 * k, 32 * k + 32, 1, 112)
-
-    def injuries(t):
-        s = str(t)
-        scan(B("SC", 0, 512, 1, 112), B("RM", 0, 512, 1, 112), B("PK", 0, 512, 1, 112), A.mult, A.max)
-        top = B("SC", 15, 512, 16, 112)
-        cp(ii(0), top)
-        tt(it(0), top, B("TH0" if t == 0 else "THC", 0, 32, 1, 112), A.is_gt)
-        ts(ii(1), ii(0), 63, A.bitwise_and)
-        ts(it(2), ii(1), 28.0, A.is_ge)
-        ib, ib0, ib1 = B("IB", 0, 32, 1, 112), B("IB", 0, 16, 1, 112), B("IB", 16, 32, 1, 112)
-        tt(ib, it(2), it(0), A.mult)
-        up, on = B("UPR", 0, 112, 1, 112), B("ONE", 0, 112, 1, 112)
-        mm(P4("PN", 0, 112, 0, 16), up, ib0, True, True)
-        mm(P4("PN", 0, 112, 16, 32), up, ib1, True, False)
-        mm(P4("PN", 0, 112, 16, 32), on, ib0, False, True)
-        tt(B("OHP", 0, 256), ind(B("II", 32, 64), B("LP", 0, 16)), B("PATP", 0, 256), A.is_equal)
-        tt(it(3), ib, ii(1), A.mult)
-        ts(it(4), P4("PN", 0, 112, 0, 32), float(CAP), A.is_lt)
-        tt(it(5), it(4), it(3), A.mult)
-        tt(B("OHC", 0, V), ind(B("IT", 160, 192), B("LC", 0, 28)), B("PATC", 0, V), A.is_equal)
         for q in range(4):
-            for h in range(2):
-                b = h * 8 + 2 * q
-                mm(P4("PN", 32 * q, 32 * q + 32, 64, 120), B("OHP", b * 16, b * 16 + 32), B("OHC", b * 28, b * 28 + 56), h == 0, h == 1)
-        joins(t)
-        ts(DF("n0" + s), B("PN", 64, 92), col(20), A.mult)
-        ts(DF("n1" + s), B("PN", 92, 120), col(21), A.mult)
-        tt(DB("cn" + s), DF("n0" + s), DF("n1" + s), A.add)
-        send(B("LN" + s, 0, 32), out32("cn" + s), "rn" + s, route(rank + 1))
+            for j in range(4):
+                gg, h = j >> 1, j & 1
+                mm(B("PN", 128, 28, 1, 32 * q + 32, 32 * q), B("OHP", 48 * (4 * h + q) + 16 * gg, 32, 1, 112),
+                   B("OHC", 8 * h + 2 * q + gg, 28, 16, 112), j == 0, j == 3)
+        one(16)
+        tt(DN("gn"), B("PN", 128, 28), B("LM" + s, 0, 28), A.add)
+        ts(DN("gn"), DN("gn"), 15, A.bitwise_and)
+        cp(B("GN" + s, 0, 28), DN("gn"))
+        n = 32 if t < 2 else 28
+        send(B("LD" + s, 0, n), B("GN" + s, 0, n), "rd" + s, 1)
+
+    def turn(t):
+        for h in range(2):
+            for b, (n, lo) in enumerate((("X", 0), ("INJ", 0), ("IB", 0), ("X", 8))):
+                mm(B("K0", 112 * h, 112, 1, 32 * b + 32, 32 * b), B(n, 24 * h + lo, 32, 1, 112), sq("IDN", 112, 112), True, True)
+        one(8)
+        act(B("XT", 0, M), B("K0", 0, M))
+
+    def patch(t):
+        par = t & 1
+        for p in range(16): mm(B("PD", 192 + par, 14, 2), lw("EE%d" % t, p), B("XT", 14 * p, 14), p == 0, p == 15)
+        one(16)
+        k = half(DF("key%d" % (t + 1)), par)
+        tt(k, B("PD", 192 + par, 14, 2), k, A.max)
 
     def joins(t):
-        par = t & 1
-        tt(it(8), ii(1), B("W32", 0, 32, 1, 112), A.mult)
-        tt(it(8), it(8), B("B32", 0, 32, 1, 112), A.add)
-        for j in range(2 if t < 2 else 1):
-            ts(ii(2 + j), ii(0), 64 << j, A.bitwise_and)
-            ts(it(6 + j), ii(2 + j), 1.0, A.is_ge)
-            tt(it(6 + j), it(6 + j), it(0), A.mult)
+        def name(lo, last):
+            mm(B("K1", lo, M), sq("EJ"), B("XT", 0, M), True, False)
+            mm(B("K1", lo, M), B("KS", 128, 128, 1, 1), B("ONE", 0, M, 1, 1), False, last)
+        name(0, True)
+        mm(B("K0", 256, M), sq("BD"), B("G0", t & 1, M, 2), True, False)
+        mm(B("K0", 256, M), sq("EB"), B("XT", 0, M), False, False)
+        tt(B("EQ", 0, M), B("K1", 0, M), gf(t), A.is_equal)
+        mm(B("K0", 256, M), sq("B32"), B("EQ", 0, M), False, True)
+        name(256, False)
+        act(B("A2", 0, M), B("K0", 256, M), bias=col("-p"), fn=F.Abs)
+        mm(B("K1", 256, M), sq("N1K"), B("A2", 0, M), False, True)
+        tt(gf(t), B("K1", 256, M), gf(t), A.max)
+        if t < 2: act(B("G0", t & 1, M, 2), gf(t), bias=1.0, fn=F.Sign)
+
+    def levels(t):
+        s = str(t)
+        mm(B("PS", 0, M), sq("IDN"), B("EM", 0, M), True, False)
+        for b in (1, 0):
             for h in range(2):
-                tt(B("XX", 32 * h + 16 * j, 32 * h + 16 * j + 16, 1, 112), B("IT", 192 + 32 * j + 16 * h, 208 + 32 * j + 16 * h, 1, 112),
-                   B("IT", 256 + 16 * h, 272 + 16 * h, 1, 112), A.mult)
-        for h in range(2):
-            mm(P4("PJ", 0, 32, 112 * h, 112 * h + 112), B("XX", 32 * h, 32 * h + 32, 1, 112), B("IDN", 0, 112, 1, 112), True, True)
-        act(P4("XT", 0, 32, 0, M), P4("PJ", 0, 32, 0, M))
+                for j in range(2):
+                    mm(B("PS", 112 * h, 112), B("PA", 256 * b + 128 * h, 128, 1, 112), B("DG", 112 * (4 * (t & 1) + 2 * h + j), 112, 1, 112),
+                       False, b == 0 and h + j == 2)
+        tt(B("XI", 0, M), B("PS", 0, M), B("CC", 0, M), A.add)
+        ts(B("XI", 0, M), B("XI", 0, M), 4, A.arith_shift_right, W - 1 + 2 ** 18, A.bitwise_and)
+        ts(B("ISL", 0, M), B("XI", 0, M), float(W), A.min)
+        for c in range(0, M, 56):
+            move(B("WR", 16 * c, 896), ind(REC, B("ISL", c, 56)))
+            scan(B("KT", 16 * c, 896), B("RM", 0, 896), B("WR", 16 * c, 896), A.min, A.max)
+        mm(B("PS", 0, M), sq("HLF"), zin(t), True, False)
+        mm(B("PS", 0, M), B("KS", 256, 128, 1, 1), B("ONE", 0, M, 1, 1), False, False)
+        mm(B("PS", 0, M), sq("HLF"), B("KT", 15, M, 16), False, True)
+        ts(B("ZB" + s, 0, M), B("PS", 0, M), ROUND, A.add, -ROUND, A.add)
+        send(B("LZ" + s, 0, M), B("ZB" + s, 0, M), "rz" + s, 1 + t)
+
+    loads()
+    consts()
+    neighbours()
+    ts(B("G0", 0, V), B("GI", 0, V), 0.0, A.is_ge)
+    ts(B("GU", 0, V), B("GI", 0, V), 1.0, A.add)
+    cp(B("GF", 1, V), B("GI", 0, V))
+    cp(B("V0", 0, 28), B("VI", 0, 28))
+    send(B("LG", 0, 32), B("V0", 0, 32), "rg", -1)
+    sizes(0, "Q")
+    sizes(1, "PT")
+    ts(B("TN", 1, M, 2), B("Q", 0, M), row(0), A.add)
+    act(B("TN", 2, M, 2), B("PT", 0, M), scale=-1.0, bias=col("-r0"))
+    gather(0, "TN", ("GU", 0), V, 28)
+    keys_e("K0", 0, V)
+    scan(B("SE", 0, V), B("RAP", 0, V), B("K0", 0, V), A.add, A.max)
+    ts(DN("key"), B("SE", 15, 28, 16), 0.0, A.max)
+    scan(B("SE", V, V), B("RAM", 0, V), B("K0", 0, V), A.add, A.min)
+    ts(DF("key1"), B("SE", V + 15, 28, 16), -1.0, A.mult, 0.0, A.max)
+    members(0)
+    members(1)
+    values(0, 1)
+    elected(0)
+    for t in range(RO):
+        values(t, 0)
+        trials(t)
+        old_damage(t)
+        slot_bases(t)
+        if t == 1:
+            gather(CELLS, "TN", GM[2], M, 28)
+            keys_e("K0", CELLS, M)
+            winners(0, "K0")
+        thresholds(t)
+        choose(t)
+        gather(0, "PB", GM[t], M, 56)
+        keys(t, 0)
+        keys(t, 1)
+        injured(t)
+        notices(t)
+        turn(t)
+        if t == 1:
+            keys_e("PT", 0, M)
+            winners(1, "PT")
+        if t < 2: patch(t)
+        joins(t)
         if t < 2:
-            for a in range(8):
-                mm(B("PJ", 480, 508), mat("EE", 2 * a + par, 32), B("XT", a, a + 217, 8, 32), a == 0, a == 7)
-        mm(B("PJ", 224, 448), B("EJ", 0, 128, 1, 32), B("XT", 0, M, 1, 32), True, True)
-
-    def next_e(t):
-        s, n = str(t), str(t + 1)
-        ts(DF("cq" + s), B("PJ", 480, 508), 0.0, A.is_equal)
-        tt(DF("cq" + s), DF("cq" + s), DF("eb" + n), A.mult)
-        tt(DF("e" + n), B("PJ", 480, 508), DF("cq" + s), A.add)
-
-    def ghosts(t):
-        s = str(t)
-        tt(DN("gd" + s), B("LG%d" % (t + 1), 0, 28), DB("cn" + s), A.add)
-        ts(DN("gd" + s), DN("gd" + s), 15, A.bitwise_and)
-        cp(B("DT", 28, 56), DN("gd" + s))
-
-    def own(t):
-        s, n = str(t), str(t + 1)
-        tt(DN("dd" + s), DN("nd" + s), B("LN" + s, 0, 28), A.add)
-        ts(DN("d" + n), DN("dd" + s), 15, A.bitwise_and)
-        cp(B("DT", 0, 28), DN("d" + n))
-
-    def lists(t):
-        par = t & 1
-        gf = B("GF", 1 + par, 448 + par, 2)
-        tt(B("UPD", 0, M), B("PJ", 224, 448), B("OHN", 0, M), A.mult)
-        tt(gf, gf, B("UPD", 0, M), A.add)
-        if t < 2: ts(B("G0", par, V - 1 + par, 2), gf, 0.5, A.is_gt)
-        if t == 0: cp(B("GU", 0, M), gf)
-
-    def count1(t):
-        cp(B("CB", 0, 32, 1, 112), it(0))
-        mm(B("PN", 128, 160), B("ONE", 0, 128, 1, 112), B("CB", 0, 32, 1, 112), True, True)
-
-    def count2(t):
-        for j in range(2):
-            lo = 128 + 16 * j
-            emit("v", [("CF", 0, 2)], [("PN", 0, 512)], lambda: g.vector.tensor_reduce(T["CF"][:, j:j + 1], T["PN"][:, lo:lo + 8], AxisListType.X, A.add))
-        tt(B("CI", 0, 1), B("CF", 0, 1), B("CF", 1, 2), A.add)
-        ts(B("CI", 1, 2), B("CI", 0, 1), 31, A.bitwise_and)
-        ts(B("CF", 2, 3), B("CI", 1, 2), 4096.0, A.mult)
-        ts(B("THC", 0, 32, 1, 112), B("TH0", 0, 32, 1, 112), B("CF", 2, 3, 1, 112), A.add)
-
-    SF = lambda k: B("SF", k * M, k * M + M)
-    SI = B("SI", 0, M)
-
-    def sp0(t):
-        mm(B("PN", 256, 480), B("BD", 0, 128), B("G0", t & 1, V - 1 + (t & 1), 2), True, True)
-        ts(B("OHN", 0, M), B("PN", 256, 480), col(0), A.is_equal)
-
-    def spS(t):
-        gf = B("GF", 1 + (t & 1), 448 + (t & 1), 2)
-        act(SF(0), gf, bias=col(28))
-        act(SF(3), gf, scale=2.0, bias=col(29))
-        act(SF(4), gf, scale=-8192.0, bias=col(30), relu=True)
-
-    def spV(t):
-        par = t & 1
-        tt(SI, SF(0), B("S1", par * M, par * M + M), A.mult)
-        ts(SI, SI, 4, A.arith_shift_right)
-        tt(SF(1), SI, SF(0), A.add)
-
-    def slots1(t, j):
-        par = t & 1
-        dist(B("PS", 112 * j, 112 * j + 112), "LWD", "KW", par * CELLS + j * CH, 16, 112)
-        if j: mm(B("PS", 256, 480), B("R2B", 0, 128), B("TN", 1 + par, 448 + par, 2), True, True)
-
-    def slots2(t):
-        par = t & 1
-        tt(SF(2), B("PS", 0, M), B("S1", (2 + par) * M, (3 + par) * M), A.mult)
-        tt(SF(3), B("PS", 256, 480), SF(3), A.mult)
-        tt(SF(1), SF(1), SF(2), A.add)
-        tt(SI, SF(1), SF(3), A.add)
-        ts(SI, SI, 4095, A.bitwise_and)
-        tt(SF(1), SI, SF(4), A.add)
-        ts(B("ISL", 0, M), SF(1), float(W), A.min)
-
-    def slots3(a, b):
-        act(B("WR", 16 * a, 16 * b), ind(B("REC", 0, W + 16), B("ISL", a, b)), scale=0.5)
-
-    def L1(t):
-        u = DU("ps%d" % t)
-        ts(B("ZH", 0, M), zin(t), 0.5, A.mult, -0.25, A.add)
-        emit("v", [("WR", 0, WIN)], [("RP", 0, V)] + u[1], lambda: g.vector.tensor_copy(T["WR"][:, 0:WIN].indirect(u[0]), T["RP"][:, 0:V]))
-
-    def L2(t, j):
-        s = str(t)
-        b, z = half(), j * CH // 16
-        scan(B("KT", b, b + CH), B("RM", 0, CH), B("WR", j * CH, j * CH + CH), A.mult, A.max)
-        tt(B("ZI", z, z + 112), B("KT", b + 15, b + CH, 16), B("ZH", z, z + 112), A.add)
-        if j == 0: return
-        cp(B("ZB" + s, 0, M), B("ZI", 0, M))
-        send(B("LZ" + s, 0, M), B("ZB" + s, 0, M), "rz" + s, route(rank + 1 + t))
-
-    def thresholds1():
-        ts(B("IOQ", 3, 4), B("IOQ", 0, 1), 7, A.bitwise_and)
-        ts(B("IOQ", 4, 5), B("IOQ", 2, 3), 1, A.bitwise_and)
-        cp(col(21), B("IOQ", 4, 5))
-        ts(col(20), col(21), -1.0, A.mult, 1.0, A.add)
-        cp(col(22), B("IOQ", 0, 1))
-        cp(col(23), B("IOQ", 3, 4))
-        ts(B("THT", 0, M, 1, 8), B("THI", 0, M, 1, 8), 4, A.arith_shift_right)
-        ts(B("THT", M, 2 * M, 1, 8), B("THI", 0, M, 1, 8), 15, A.bitwise_and)
-        cp(B("THB", 0, 2 * M, 1, 8), B("THT", 0, 2 * M, 1, 8))
-        ts(B("SELT", 0, 16), B("IO8", 0, 16), col(22), A.is_equal)
-        ts(B("SELU", 0, 16), B("SELT", 0, 16), 16.0, A.mult)
-        for h in range(2):
-            o = P4("PN", 0, 112, 16 * h, 16 * h + 16)
-            mm(o, B("THB", 112 * h, 112 * h + 112, 1, 8), B("SELU", 0, 16, 1, 8), True, False)
-            mm(o, B("THB", M + 112 * h, M + 112 * h + 112, 1, 8), B("SELT", 0, 16, 1, 8), False, True)
-        cp(B("LP", 0, 16), B("LPI", 0, 16))
-        ts(DN("hg"), aD, 1.0 / 28, A.mult, 0.5 / 28 - 0.5, A.add)
-        ts(DN("h3"), DN("hg"), 3, A.arith_shift_right)
-        ts(DF("h8"), DN("h3"), 8.0, A.mult)
-        tt(DF("h8"), DF("h8"), DN("hg"), A.add)
-        cp(B("LC", 0, 28), DF("h8"))
-
-    def thresholds2(): ts(B("TH0", 0, 32, 1, 112), P4("PN", 0, 112, 0, 32), 4096.0, A.mult, 4095.0, A.add)
-
-    def join_mats():
-        fill(B("W32", 0, 32), 1.0)
-        fill(B("B32", 0, 32), 1.0)
-        for h in (0, 16):
-            fill(B("W32", h, h + 8), 16.0)
-            fill(B("B32", h, h + 8), 0.0)
-        ts(col(24), col(22), 15.5, A.is_gt)
-        ts(col(25), col(22), 15.5, A.is_lt)
-        ts(B("EJ", 0, 128, 1, 32), B("IOM", 0, 128, 1, 32), col(23, 32), A.is_equal, col(25, 32), A.mult)
-        ts(B("EE0", 0, 128, 1, 32), B("IOM", 0, 128, 1, 32), col(23, 32), A.is_equal, col(24, 32), A.mult)
-        for a in range(8): cp(B("EE", 16 * a, 16 * a + 129 * 15 + 1, 129, 32), B("EE0", 16 * a, 16 * a + 16, 1, 32))
-
-    slots1(0, 0)
-    slots1(0, 1)
-    base1("LWE0")
-    fill(B("GF", 0, 1), -5.0)
-    fill(B("GF", V + 1, 464), -5.0)
-    ts(B("GF", 1, V + 1), B("GI", 0, V), 1.0, A.add)
-    ts(B("IOQ", 6, 7), B("IOQ", 0, 1), 1, A.add)
-    ts(B("IOQ", 7, 8), B("IOQ", 6, 7), 15, A.bitwise_and)
-    cp(col(26), B("IOQ", 7, 8))
-    ts(B("ID", 0, 912), B("SF", 0, 912), col(26), A.is_equal)
-    fill(B("DT", 56, 64), 0.0)
-    ts(B("NBT", 0, V), B("NBI", 0, V), 4, A.arith_shift_right)
-    ts(B("NBT", V, 2 * V), B("NBI", 0, V), 15, A.bitwise_and)
-    base2("0")
-    act(B("LWO", 0, 2048), B("LW", 0, 2048), scale=col(9))
-    dist(B("PD", 0, 28), "LWD", "TN", 1, 16, 28)
-    cp(B("NBD", 0, V), B("NBT", 0, V))
-    cp(B("NBD", V, 2 * V), B("NBT", V, 2 * V))
-    dma("y", (T["NW"][0:113:16, 0:7168], [("NW", 0, 7168)]), B("NBD", 0, V))
-    dma("y", (T["NW"][1:114:16, 0:7168], [("NW", 0, 7168)]), B("NBD", V, 2 * V))
-    for t in range(3):
-        fill(out32("mv%d" % t), 0.0)
-        fill(out32("cn%d" % t), 0.0)
-    base3("0", DF("e0"))
-    E1(0)
-    cp(B("DT", 0, 28), B("PD", 0, 28))
-    cp(DN("d0"), B("PD", 0, 28))
-    cp(DB("mv0"), B("PD", 0, 28))
-    iota(B("CK", 0, 512), [[0, 32], [-256, 16]], 3840, 0)
-    send_moved(0)
-    iota(B("PATP", 0, 256), [[0, 16], [1, 16]], 0, 0)
-    iota(B("PATC", 0, V), [[0, 16], [1, 28]], 28, 0)
-    iota(B("LPI", 0, 16), [[16, 2], [1, 8]], 8, 0)
-    asel(B("UPR", 0, 112), B("ONE", 0, 112), [[1, 112]], A.is_gt, 0, -1)
-    E2(0)
-    ze(0)
-    D1(0)
-    E3(0)
-    act(B("LW4", 0, 2048), B("LW", 0, 2048), scale=4.0)
-    fill(B("REC", W, W + 16), 0.0)
-    for j in range(3): fill(B("J84", 28 * j, 28 * j + 28), float(j))
-    act(B("TE", 0, 912), B("WD0", 0, 912))
-    ts(B("LOA", 0, 128), B("BD", 0, 128), col(9), A.mult)
-    ts(B("IP", 0, 128), B("IDN", 0, 128), col(17), A.mult)
-    F1(0)
-    D2(0)
-    R1(0, 0)
-    E4(0)
-    R1(0, 1)
-    E5a(0)
-    R1(0, 2)
-    R1x(0)
-    F1b(0)
-    E5b(0)
-    cp(B("DT", 28, 56), B("LG0", 0, 28))
-    D3(0)
-    sp0(0)
-    F1k(0)
-    F1c(0)
-    base1("LWE1")
-    spS(0)
-    spV(0)
-    slots2(0)
-    act(B("DA2", 0, 2048), B("WD0", 0, 2048))
-    act(B("EE", 0, 2048, 1, 32), B("WD0", 0, 2048, 1, 32))
-    asel(B("DA2", 2, 2035, 16), B("ONE", 0, 128), [[-1, 16], [-16, 8]], A.is_equal, 0, 1)
-    iota(B("IO8", 0, 16), [[0, 2], [1, 8]], 0, 0)
-    act(B("IT", 0, 448), B("WD0", 0, 448))
-    fill(B("II", 0, 128), 0.0)
-    act(B("RM", 0, CH), B("RA", 0, CH), relu=True)
-    base2("1")
-    D4(0)
-    slots3(0, 56)
-    slots3(56, 112)
-    R2(0)
-    thresholds1()
-    F2(0)
-    R3(0)
-    slots3(112, 168)
-    slots3(168, 224)
-    F3(0)
-    thresholds2()
-    ts(B("SELD", 0, 8), B("BD", 0, 113, 16), 4096.0, A.mult)
-    ts(B("SELD", 8, 16), B("BD", 0, 113, 16), 4096.0, A.mult)
-    ts(col(18), col(4), col(6), A.add)
-    ts(col(19), col(5), col(6), A.add)
-    ts(B("SELP", 0, 8), B("BD", 0, 113, 16), col(18), A.mult)
-    ts(B("SELP", 8, 16), B("BD", 0, 113, 16), col(19), A.mult)
-    open_keys()
-    keys("WD0", "SELD", False)
-    keys("WP", "SELP", True)
-    join_mats()
-    base3("1", DF("eb1"))
-    for t in range(3):
-        if t == 0: L1(0)
-        injuries(t)
-        if t == 1: base3("2", DF("eb2"))
-        if t > 0: L1(t)
-        if t == 2: break
-        n = t + 1
-        h = n & 1
-        next_e(t)
-        E1(n)
-        if n == 1:
-            lists(0)
-            table(False)
-            sp0(1)
-            sgather(0, 56)
-            sgather(56, 112)
-        F1(n)
-        if n == 1: spS(1)
-        count1(t)
-        L2(t, 0)
-        L2(t, 1)
-        own(t)
-        D1(n)
-        table(True, n == 2)
-        ghosts(t)
-        E2(n)
-        D2(n)
-        ze(n)
-        E3(n)
-        if n == 2:
-            lists(1)
-            spS(2)
-        spV(n)
-        sgather(224 * h, 224 * h + 56)
-        R1(n, 0)
-        E5a(n)
-        R1(n, 1)
-        R1(n, 2)
-        R1x(n)
-        E4(n)
-        F1b(n)
-        sgather(224 * h + 56, 224 * h + 112)
-        sgather(224 * h + 112, 224 * h + 168)
-        E5b(n)
-        D3(n)
-        F1c(n)
-        if n == 2: F2(2)
-        slots1(n, 0)
-        D4(n)
-        R2(n)
-        sgather(224 * h + 168, 224 * h + 224)
-        open_keys()
-        if n == 2:
-            F3(2)
-            keys("WP", "SELP", False)
-        slots1(n, 1)
-        R3(n)
-        if n == 1:
-            keys("WD1", "SELD", False)
-            scans(CELLS, 2 * CELLS)
-            F1k(1)
-        else: keys("WD2", "SELD", True)
-        slots2(n)
-        count2(t)
-        if n == 2: sp0(2)
-        if n == 1:
-            vgather(168, 224)
-            sgather(112, 168)
-        else: ts(B("WR", 16 * 168, CELLS), ind(B("REC", 0, W + 16), B("ISL", 168, 224)), 0.5, A.mult)
-        slots3(0, 56)
-        if n == 1: F2(1)
-        slots3(56, 112)
-        if n == 1: scans(0, CELLS)
-        slots3(112, 168)
-        if n == 1:
-            slots3(168, 224)
-            F3(1)
-            base1("LWE0")
-            keys("WP", "SELP", True)
-            base2("2")
-    L2(2, 0)
-    L2(2, 1)
-    own(2)
-    spread(B("DT", 0, 28), True)
-    lists(2)
-    ts(B("YL", 0, V), B("GF", 1, V + 1), -1.0, A.add)
-    dma("y", (T.yl[:, :], []), B("YL", 0, V))
-    act(B("YD", 0, V), B("PA", 0, V))
-    dma("y", (T.yd[:, :], []), (T["SF"][2:115:16, 0:V], [("SF", 0, V)]))
+            elected(t + 1)
+            count()
+            values(t + 1, 1)
+        levels(t)
+        if t == 0:
+            members(2)
+            table2()
+    dma("y", (T.yl[:, :], []), B("GF", 1, V))
+    dma("y", (T.yd[:, :], []), B("LD2", 0, 28))
     dma("y", (T.yz[:, :], []), B("LZ2", 0, M))
+    for _, n, q in order(calls): calls[n][5](q)
     finish()

@@ -3,9 +3,7 @@ from concourse.mybir import AluOpType, AxisListType, ActivationFunctionType
 V, M, W, RO, CAP = 448, 224, 4096, 3, 44
 CELLS = 16 * M
 H = CELLS // 2
-CYCLE, GATHER, WAKE = 1.04, 1.56, 110
-BIAS = 700
-HUGE = float(2 ** 30)
+CYCLE, GATHER, SCATTER, WAKE = 1.04, 1.56, 3.64, 110
 ROUND = float(3 * 2 ** 22)
 
 
@@ -15,34 +13,36 @@ def i4(n, p=128): return ("sbuf", [p, n], "int32")
 def u2(n): return ("sbuf", [128, n], "uint16")
 
 
-SHIFTED = ["L64", "LK", "LE", "LO", "L1", "L2", "DP", "DM", "EE0", "EE1"]
-SQUARE = ["IDN", "BIG", "P18", "HLF", "N1K", "BD", "B32", "R2B", "I567", "I012", "SLE", "SLV", "EJ", "EB", "UPM", "C64"]
+SHIFTED = ["L07", "LE", "L64", "LK", "LK1", "LO", "L3", "DP", "DM", "EE0", "EE1"]
+SQUARE = ["SLX", "I567", "IDN", "P18", "P13", "P14", "I16", "HLF", "N1K", "BD", "B32", "R2B", "R5B", "EJ", "EB", "UPM", "C64",
+          "D64", "D00", "D01", "D10", "D11", "K4"]
 SCRATCH = {
-    "GI": i4(V), "NBI": i4(V), "VI": i4(28), "THI": i4(M, 8), "Z0": bf(M), "REC": bf(W + 16), "NW": bf(2 * CELLS), "KW": bf(2 * CELLS),
-    "WR": bf(CELLS), "KT": bf(CELLS), "GF": f4(464), "GU": u2(V), "GM": u2(3 * M), "G0": bf(V), "NBD": bf(2 * V), "THB": bf(2 * M, 8),
-    "TN": bf(464), "PB": bf(464), "T1": bf(V), "VT": bf(2 * V), "CR": bf(V), "ID": bf(M), "IDS": f4(M),
-    "ONE": bf(V), "LW": bf(144 * len(SHIFTED)), "SQ": bf(128 * len(SQUARE)), "DA": bf(2064), "DG": bf(8 * 112), "KS": bf(384, 1),
-    "SEL": bf(96), "THS": bf(24, 8), "G8": bf(16), "OH": f4(16), "IO": f4(16), "IOQ": i4(8), "COL": f4(40), "CB": bf(4), "IOM": f4(128),
-    "IOX": f4(V), "S17": f4(V), "RAP": bf(V), "RAM": bf(V), "RAK": bf(384), "RM": bf(H), "J16": bf(84), "PP": i4(384), "PC": bf(V),
+    "GI": i4(V), "NBI": i4(V), "VI": i4(28), "THI": i4(M, 8), "Z0": bf(M + 16), "REC": bf(W + 16), "NW": bf(2 * CELLS), "KW": bf(2 * CELLS),
+    "WR": bf(CELLS), "KT": bf(CELLS), "WD": bf(4096), "ZR": bf(904), "GF": f4(480), "YL": f4(V), "GU": u2(V), "GM": u2(2 * M), "G0": bf(V),
+    "NBD": bf(2 * V), "THB": bf(2 * M, 8), "TN": bf(V + 16), "PB": bf(V), "T1": bf(V), "VT": bf(2 * V + 16), "CR": bf(V),
+    "ONE": bf(V), "LW": bf(144 * len(SHIFTED)), "SQ": bf(128 * len(SQUARE)), "DA": bf(2064), "KS": bf(512, 1),
+    "SEL": bf(64), "THS": bf(24, 8), "G8": bf(8), "OH": f4(16), "IO": f4(16), "IOQ": i4(2), "COL": f4(24),
+    "IOX": f4(V), "RAP": bf(V), "RAM": bf(V), "RAK": bf(384), "RM": bf(H // 2), "J16": bf(84), "PP": i4(384), "PC": bf(V),
     "LPI": i4(24), "LPC": u2(52), "SE": f4(2 * V), "SC": f4(768),
-    "MSK": bf(V), "ZE": bf(V), "MAT": bf(V), "GD": bf(V), "OG": bf(V), "VO": bf(V), "MT": bf(3 * V), "MO": bf(V), "MN": bf(V),
-    "AB": bf(256), "PA": bf(512), "TI": i4(96), "THC": f4(48), "X": bf(64), "INJ": bf(64), "IB": bf(64), "TM": bf(64),
-    "OHP": bf(384), "OHC": bf(V), "XT": bf(M), "EQ": bf(M), "A2": bf(M), "S2": f4(M), "EM": bf(M), "X1": f4(M), "CC": f4(M),
+    "ZE": bf(V), "MAT": bf(V), "GD": bf(V), "OG": bf(V), "VO": bf(V), "MT": bf(3 * V), "MO": bf(V), "MN": bf(V),
+    "PA": bf(512), "TI": i4(96), "THC": f4(48), "X": bf(64), "INJ": bf(64), "IB": bf(64), "TM": bf(64),
+    "OHP": bf(384), "OHC": bf(V), "XT": bf(M), "EQ": bf(M), "A2": bf(M), "EM": bf(M), "CC": f4(M),
     "XI": i4(M), "ISL": u2(M), "CF": f4(16), "CI": i4(4), "SB": bf(32 * 6), "GN2": f4(28), "LD2": f4(28), "LG": bf(32),
-    "DF": f4(28 * 32), "DN": i4(28 * 24), "DU": u2(28 * 16), "DB": bf(28 * 8),
+    "DF": f4(28 * 24), "DN": i4(28 * 20), "DU": u2(28 * 14), "DB": bf(28 * 8),
 }
 PSUM = ["PT", "K0", "K1", "Q", "PS", "PD", "PM", "PN"]
 for _n in PSUM: SCRATCH[_n] = ("psum", [128, 512], "float32")
 for _t in range(RO):
     SCRATCH["LM%d" % _t] = bf(32)
-    SCRATCH["LZ%d" % _t] = bf(M)
+    SCRATCH["LZ%d" % _t] = bf(M + 16)
     SCRATCH["ZB%d" % _t] = bf(M)
     if _t < 2: SCRATCH["LD%d" % _t] = bf(32)
-SEMAPHORES = ["cv", "cs", "ct", "cg", "rg"] + ["dma%d" % k for k in range(20)] + ["ls%d" % k for k in range(10)] + \
+SEMAPHORES = ["cv", "cs", "ct", "cg", "rg"] + ["dma%d" % k for k in range(32)] + ["ls%d" % k for k in range(10)] + \
     [a + str(k) for a in ("rm", "rd", "rz") for k in range(RO)]
 ALIAS = {n: ("SQ", 128 * k) for k, n in enumerate(SQUARE)}
 ALIAS.update({"V0": ("SB", 0), "MV0": ("SB", 32), "MV1": ("SB", 64), "MV2": ("SB", 96), "GN0": ("SB", 128), "GN1": ("SB", 160),
-              "LP": ("LPC", 0), "LC": ("LPC", 24), "SL1": ("SEL", 0), "SL2": ("SEL", 32), "S15": ("SEL", 48)})
+              "LP": ("LPC", 0), "LC": ("LPC", 24), "SL1": ("SEL", 0), "SL2": ("SEL", 32), "S15": ("SEL", 40)})
+PLAN = []
 
 
 def meet(r, s): return r[1] < s[2] and s[1] < r[2] and r[3] < s[4] and s[3] < r[4]
@@ -57,7 +57,7 @@ def order(calls):
             for r in regs:
                 for s, sw, m in log.get(r[0], []):
                     if r[0] in PSUM or ((w or sw) and meet(r, s)):
-                        same = c[0] == calls[m][0] and len(c[0]) == 1 and c[0] in "vstg"
+                        same = c[0] == calls[m][0] and c[0] in ("v", "s", "t", "g")
                         d[m] = max(d.get(m, 0), 0 if same and (c[0] == "t" or not sw) else WAKE)
         for regs, w in ((c[2], False), (c[1], True)):
             for r in regs:
@@ -67,25 +67,51 @@ def order(calls):
                 L.append((r, w, n))
         d.pop(n, None)
         pre.append(d)
-    tail = [min(x[1] for x in c[3].values()) for c in calls]
-    for n in range(len(calls) - 1, -1, -1):
-        for m, lag in pre[n].items(): tail[m] = max(tail[m], min(x[1] for x in calls[m][3].values()) + lag + tail[n])
-    taken, done, plan = {}, {}, []
-    for n in sorted(range(len(calls)), key=lambda n: (-tail[n], n)):
-        ready = max([done[m] + lag for m, lag in pre[n].items()], default=0.0)
+    N = len(calls)
+    post = [{} for c in calls]
+    for n, d in enumerate(pre):
+        for m, lag in d.items(): post[m][n] = lag
+    cost = [min(x[1] for x in c[3].values()) for c in calls]
+    tail = list(cost)
+    for n in range(N - 1, -1, -1):
+        for m, lag in pre[n].items(): tail[m] = max(tail[m], cost[m] + lag + tail[n])
+
+    def place(rank, queue, back):
+        taken, done, plan = {}, [0.0] * N, []
+        for n in sorted(range(N), key=lambda n: (-rank[n], -n if back else n)):
+            busy, until = calls[n][3][queue[n]]
+            t = max([done[m] + lag for m, lag in (post if back else pre)[n].items()], default=0.0) + (until - busy if back else 0)
+            L = taken.setdefault(queue[n], [])
+            lo, hi = 0, len(L)
+            while lo < hi:
+                if L[(lo + hi) // 2][1] <= t: lo = (lo + hi) // 2 + 1
+                else: hi = (lo + hi) // 2
+            while lo < len(L) and t + busy > L[lo][0]:
+                t = max(t, L[lo][1])
+                lo += 1
+            L.insert(lo, (t, t + busy))
+            done[n] = t + (busy if back else until)
+            plan.append((t, n, queue[n]))
+        return done, plan
+
+    def both_ways(rank, queue, passes):
         best = None
-        for q, (busy, until) in calls[n][3].items():
-            t = ready
-            for a, b in taken.get(q, []):
-                if t + busy <= a: break
-                t = max(t, b)
-            if best is None or t + until - BIAS < best[0]: best = (t + until, t, q, busy)
-        done[n] = best[0]
-        L = taken.setdefault(best[2], [])
-        L.append((best[1], best[1] + best[3]))
-        L.sort()
-        plan.append((best[1], n, best[2]))
-    return sorted(plan)
+        for k in range(passes):
+            done, plan = place(rank, queue, False)
+            if best is None or max(done) < best[0]: best = (max(done), plan, rank)
+            if k < passes - 1: rank = place(done, queue, True)[0]
+        return best
+
+    queue = [list(c[3])[-1] for c in calls]
+    best = both_ways(tail, queue, 4)
+    for least in (200, 200, 0, 200):
+        for n in sorted(range(N), key=lambda n: -tail[n]):
+            for q in calls[n][3]:
+                if q == queue[n] or cost[n] < least: continue
+                other = queue[:n] + [q] + queue[n + 1:]
+                b = both_ways(best[2], other, 2)
+                if b[0] < best[0] - 1: best, queue = b, other
+    return sorted(best[1])
 
 
 def builder(g, T):
@@ -178,6 +204,7 @@ def rank_program(g, core, T, topo):
         hi = lo + (cnt - 1) * st + 1
         return (T[n][p0:p, lo:hi] if st == 1 else T[n][p0:p, lo:hi:st], [(n, lo, hi, p0, p)], cnt, n)
 
+    def like(n, o): return B(n, 0, o[2], 1, o[1][0][4], o[1][0][3])
     def ind(win, off): return (win[0].indirect(off[0]), win[1] + off[1], 16 * off[2], None)
     def num(s): return (s, []) if s is None or isinstance(s, (int, float)) else s
     def short(*x): return 0.5 if all(SCRATCH[a[3]][2] in ("bfloat16", "uint16") for a in x) else 1.0
@@ -187,7 +214,7 @@ def rank_program(g, core, T, topo):
 
     def vec(o, a, ins, k, f): call("v", o[1], ins, 50 + GATHER * o[2] if a[3] is None else CYCLE * max(64, k * o[2]), f)
     def tt(o, a, b, op): vec(o, a, a[1] + b[1], 1 if a[3] in PSUM or b[3] in PSUM else 2, lambda: g.vector.tensor_tensor(o[0], a[0], b[0], op))
-    def cp(o, a): vec(o, a, a[1], short(o, a), lambda: g.vector.tensor_copy(o[0], a[0]))
+    def cp(o, a): vec(o, a, a[1], a[3] and short(o, a), lambda: g.vector.tensor_copy(o[0], a[0]))
 
     def ts(o, a, s1, op0, s2=None, op1=None):
         x, y = num(s1), num(s2)
@@ -196,7 +223,6 @@ def rank_program(g, core, T, topo):
 
     def scan(o, a, b, op0, op1): vec(o, a, a[1] + b[1], short(o, a, b), lambda: g.vector.tensor_tensor_scan(o[0], a[0], b[0], 0.0, op0, op1))
     def fill(o, c): vec(o, o, [], short(o), lambda: g.vector.memset(o[0], c))
-    def total(o, a): vec(o, a, a[1], 1, lambda: g.vector.tensor_reduce(o[0], a[0], AxisListType.X, A.add))
 
     def act(o, a, scale=1.0, bias=0.0, fn=None, acc=None):
         x, y = num(scale), num(bias)
@@ -205,10 +231,24 @@ def rank_program(g, core, T, topo):
         if acc is None: call("s", o[1], a[1] + x[1] + y[1], ns, lambda: g.scalar.activation(o[0], a[0], fn, bias=y[0], scale=x[0]))
         else: call("s", o[1] + acc[1], a[1], ns, lambda: g.scalar.activation(o[0], a[0], fn, accum_out=acc[0]))
 
-    def move(o, a, qs="vs"):
-        f = {"v": lambda: g.vector.tensor_copy(o[0], a[0]), "s": lambda: g.scalar.activation(o[0], a[0], F.Copy)}
-        ns = {"v": 50 + GATHER * o[2], "s": 65 + GATHER * o[2]}
-        calls.append([qs, o[1], a[1], {q: (ns[q], ns[q]) for q in qs}, {}, lambda q: emit(q, o[1], a[1], f[q])])
+    def iota(o, pat, base, cm):
+        call("g", o[1], [], 130 + 2 * CYCLE * o[2], lambda: g.iota(o[0], pat, base, cm, allow_small_or_imprecise_dtypes=True), o[1][0][3] > 0)
+
+    def asel(o, a, pat, op, base, cm, c=0.0): call("g", o[1], a[1], 170 + 2 * CYCLE * o[2], lambda: g.affine_select(o[0], a[0], pat, op, c, base, cm))
+    def mark(o, a, pat, base, c): asel(o, a, pat, A.not_equal, base, 1, c)
+
+    def either(*ways):
+        for f in ways: f()
+        L = calls[-len(ways):]
+        calls[-len(ways):] = [["any", L[0][1], sum((c[2] for c in L), []), {c[0]: c[3][c[0]] for c in L}, {},
+                               lambda q: [c[5](q) for c in L if c[0] == q]]]
+
+    def move(o, a): either(lambda: cp(o, a), lambda: act(o, a))
+    def lin(o, a, scale=1.0, bias=0.0): either(lambda: ts(o, a, scale, A.mult, bias, A.add), lambda: act(o, a, scale, bias))
+
+    def const(o, c):
+        ways = [lambda: fill(o, c), lambda: act(o, like("ONE", o), c)]
+        either(*(ways + [lambda: iota(o, [[0, o[2]]], int(c), 0)] * (c == int(c))))
 
     def mm(o, l, r, start, stop): call("t", o[1], l[1] + r[1], CYCLE / 2 * max(min(64, l[2]), r[2]), lambda: g.tensor.matmul(o[0], l[0], r[0], start, stop))
 
@@ -217,11 +257,8 @@ def rank_program(g, core, T, topo):
         ns = sum(c[3]["t"][0] for c in L)
         calls[-k:] = [["t", sum((c[1] for c in L), []), sum((c[2] for c in L), []), {"t": (ns, ns)}, {}, lambda q: [c[5](q) for c in L]]]
 
-    def iota(o, pat, base, cm, alone=False):
-        call("g", o[1], [], 130 + 2 * CYCLE * o[2], lambda: g.iota(o[0], pat, base, cm, allow_small_or_imprecise_dtypes=True), alone)
-
-    def asel(o, a, pat, op, base, cm, c=0.0): call("g", o[1], a[1], 170 + 2 * CYCLE * o[2], lambda: g.affine_select(o[0], a[0], pat, op, c, base, cm))
-    def dma(q, o, a, ns=2000): calls.append([q + "d", o[1], a[1], {q: (60, ns)}, {}, lambda _: dma_now(q, o, a)])
+    def dma(q, o, a, ns=2000, behind=False):
+        calls.append([q + "d", o[1], a[1], {q: (60, ns)}, {len(calls) - 1: 60 - calls[-1][3][q][1]} if behind else {}, lambda _: dma_now(q, o, a)])
 
     def send(land, a, sem, step):
         dst, src = T.cores[(rank + step) % N], T.cores[(rank - step) % N]
@@ -233,17 +270,14 @@ def rank_program(g, core, T, topo):
     def sq(n, k=128, m=128): return B(n, 0, m, 1, k)
     def lw(n, p): return B("LW", 144 * SHIFTED.index(n) + 15 - p, 128)
     def lwc(n, d=0): return B("LW", 144 * SHIFTED.index(n) + 15 + d, 8, 16)
+    def ks(j): return B("KS", 128 * j, 128, 1, 1)
 
     def dist(o, n, src, base, cols, first=True, last=True):
         for p in range(16): mm(o, lw(n, p), B(src, base + p, cols, 16), first and p == 0, last and p == 15)
         one(16)
 
-    def spread(bank, row, src, last=False):
-        for p in range(16): mm(B(bank, 28 * p, 28), B("DA", 128 * p + 15 - row, 128), src, False, last and p == 15)
-        one(16)
-
-    def unmix(l, src, last=False):
-        for p in range(16): mm(B("PT", 28 * p, 28), l, B(src, p, 28, 16), False, last and p == 15)
+    def spread(src, last=False):
+        for p in range(16): mm(B("Q", 28 * p, 28), B("DA", 128 * p + 12, 128), src, False, last and p == 15)
         one(16)
 
     slots = {}
@@ -256,32 +290,30 @@ def rank_program(g, core, T, topo):
         return f
 
     DF, DN, DU, DB = slot("DF"), slot("DN"), slot("DU"), slot("DB")
-    def part(v, j, n=1): return B(v[3], v[1][0][1] + 28 * j, 28 * n)
+    def part(v, j, n=28): return B(v[3], v[1][0][1] + n * j, n)
     def half(v, par): return B(v[3], v[1][0][1] + par, 14, 2)
     cols = {}
-    def col(n, p=128, k=1): return B("COL", cols.setdefault(n, (sum(x[1] for x in cols.values()), k))[0], 1, 1, p)
-    def colj(n, j, p=128, k=1): return B("COL", cols[n][0] + j, k, 1, p)
-    def row(r, k=1): return B("OH", r, k)
+    def col(n, p=128): return B("COL", cols.setdefault(n, len(cols)), 1, 1, p)
+    def row(r): return B("OH", r, 1)
     def own(t, n=28): return B("V0" if t == 0 else "LD%d" % (t - 1), 0, n)
-    def ghost(t): return B("LG" if t == 0 else "GN%d" % (t - 1), 0, 28)
-    def dint(t): return B("VI", 0, 28) if t == 0 else DN("d")
-    def zin(t): return B("Z0" if t == 0 else "LZ%d" % (t - 1), 0, M)
-    def gf(t): return B("GF", 1 + (t & 1), M, 2)
+    def zin(t, lo=16): return B("Z0" if t == 0 else "LZ%d" % (t - 1), lo, M + 16 - lo)
+    def gf(t): return B("GF", 240 * (t & 1) + 16, M)
     REC = B("REC", 0, W + 16)
     G8 = B("G8", 0, 8)
     aD = DF("a")
+    GROUP = [[-16, 8]]
 
     def loads():
-        dma("y", B("GI", 0, V), (T.gl[:, :], []))
         dma("s", B("VI", 0, 28), (T.val[:, :], []))
-        dma("y", B("NBI", 0, V), (T.nb[:, :], []))
-        dma("y", B("REC", 0, W), (T.rec[:, :], []), 5000)
-        dma("y", B("Z0", 0, M), (T.zl[:, :], []))
-        dma("y", B("THI", 0, M, 1, 8), (T.th[:, :], []))
+        dma("y", B("GI", 0, V), (T.gl[:, :], []))
+        dma("y", B("NBI", 0, V), (T.nb[:, :], []), 2200, True)
+        dma("y", B("Z0", 16, M), (T.zl[:, :], []), 2400, True)
+        dma("y", B("THI", 0, M, 1, 8), (T.th[:, :], []), 2400, True)
+        dma("y", B("REC", 0, W), (T.rec[:, :], []), 5000, True)
+        dma("y", B("NW", 0, W), (T.rec[:, :], []), 7000, True)
+        dma("y", B("NW", W, 2 * CELLS - W), (T.rec[:, 0:2 * CELLS - W], []), 9000, True)
 
     def neighbours():
-        dma("y", B("NW", 0, W), B("REC", 0, W), 4000)
-        dma("y", B("NW", W, 2 * CELLS - W), B("REC", 0, 2 * CELLS - W), 4000)
         cp(B("NBD", 0, V), B("NBI", 0, V))
         tt(B("NBD", V, V), B("NBI", 0, V), B("NBD", 0, V), A.subtract)
         for r in range(2):
@@ -289,204 +321,152 @@ def rank_program(g, core, T, topo):
 
     def consts():
         fill(B("ONE", 0, V), 1.0)
+        fill(B("ZR", 0, 904), 0.0)
         iota(B("IOQ", 0, 1), [[0, 1]], 0, 1)
         iota(B("IO", 0, 16), [[1, 16]], 0, 0)
         iota(B("CR", 0, V, 1, 32), [[0, 16], [1, 28]], 0, 0)
-        iota(B("CR", 0, V, 1, 64, 32), [[1, M], [0, 2]], 1, 0, True)
-        iota(B("CR", 0, V, 1, 96, 64), [[1, 16], [0, 28]], 0, 0, True)
-        asel(G8, B("ONE", 0, 8), [[-16, 8]], A.is_ge, 0, 1)
+        iota(B("CR", 0, V, 1, 64, 32), [[1, M], [0, 2]], 1, 0)
+        iota(B("CR", 0, V, 1, 96, 64), [[1, 16], [0, 28]], 0, 0)
+        asel(G8, B("ONE", 0, 8), GROUP, A.is_ge, 0, 1)
         asel(G8, G8, [[16, 8]], A.is_ge, 15, -1)
-        for k in range(0, len(SHIFTED), 2): fill(B("LW", 144 * k, 288), 0.0)
-        fill(B("SLE", 0, 256), 0.0)
-        fill(B("SLE", 1, 8, 16, 1), 1.0)
-        fill(B("SLE", 2, 8, 16, 33, 32), 1.0)
-        fill(B("SLV", 6, 8, 16, 1), 1.0)
-        fill(B("SLV", 5, 8, 16, 65, 64), 1.0)
-        fill(B("TN", 0, 464), 0.0)
+        for k in range(0, len(SHIFTED), 3): const(B("LW", 144 * k, 144 * min(3, len(SHIFTED) - k)), 0.0)
+        for k in range(4): fill(B("DA", 516 * k, 516), 0.0)
+        asel(B("DA", 15, 128, 16), B("ONE", 0, 128), [[-1, 16], [-16, 8]], A.is_equal, 0, 1)
+        const(B("SLX", 0, 256), 0.0)
+        for r, p in ((1, 0), (6, 0), (2, 32), (5, 64)): const(B("SLX", r, 8, 16, p + 1, p), 1.0)
+        for n in ("TN", "VT", "Z0", "LZ0", "LZ1"): const(B(n, 0, 16), 0.0)
+        const(B("REC", W, 16), 0.0)
+        const(B("SB", 0, 192), 0.0)
+        const(B("GF", 15, 2, 240), -5.0)
+        const(B("SEL", 0, 64), 0.0)
+        for n in ("X", "INJ", "TM"): const(B(n, 0, 64), 0.0)
+        for j, c in enumerate((-1.0, -0.25, 13.0, 15.0)): const(ks(j), c)
+        const(col("c"), 4095.0)
         ts(B("IOQ", 1, 1), B("IOQ", 0, 1), 15, A.bitwise_and)
         cp(col("p"), B("IOQ", 1, 1))
         ts(B("OH", 0, 16), B("IO", 0, 16), col("p"), A.is_equal)
-        ts(col("-r0"), row(0), -1.0, A.mult)
-        cp(lwc("L1"), G8)
-        for k in range(4): fill(B("DA", 516 * k, 516), 0.0)
-        asel(sq("IDN"), B("ONE", 0, 128), [[1, 128]], A.is_equal, 0, -1)
-        asel(B("DA", 15, 128, 16), B("ONE", 0, 128), [[-1, 16], [-16, 8]], A.is_equal, 0, 1)
-        iota(B("IDS", 0, M), [[1, 16], [0, 14]], 0, 0)
+        for n, r, a, b in (("-r0", 0, -1.0, 0.0), ("odd", 3, 2.0, -1.0), ("28r6", 6, 28.0, 0.0), ("no7", 7, -1.0, 1.0), ("2r7", 7, 2.0, 0.0),
+                           ("r07", 7, 2.0, row(0)), ("-64r0", 0, -64.0, 0.0)): lin(col(n), row(r), a, b)
+        for n, a, b in (("28p", 28.0, 0.0), ("wk", 448.0, 448.0), ("p1", 1.0, 1.0), ("-p", -1.0, 0.0), ("lb", 1.0, 8.0)): lin(col(n), col("p"), a, b)
+        for n, d, a in (("L07", 0, 1.0), ("L07", 7, 1.0), ("L64", 0, 64.0), ("LK", 0, col("wk")), ("LK1", 0, col("p1")), ("DP", 0, 1.0),
+                        ("DP", 1, 1.0), ("DM", 0, -1.0), ("DM", 1, -1.0)): lin(lwc(n, d), G8, a)
+        for n, r, c in (("LE", 0, 2.0 ** 17), ("LE", 1, 256.0), ("LE", 2, 1.0), ("LO", 0, 1.0), ("LO", 1, 1.0), ("L3", 3, 1.0)):
+            mark(lwc(n), lwc(n), GROUP, -r, c)
+        mark(sq("IDN"), B("ZR", 0, 128), [[-1, 128]], 0, 1.0)
+        for n, c in (("P18", 2.0 ** 18), ("P13", 8192.0), ("P14", 16384.0), ("I16", 16.0), ("HLF", 0.5), ("N1K", -1024.0),
+                     ("D00", 1616.0), ("D01", 592.0), ("D10", 1648.0), ("D11", 624.0)):
+            either(lambda: ts(sq(n), sq("IDN"), c, A.mult), lambda: act(sq(n), sq("IDN"), c), lambda: mark(sq(n), B("ZR", 0, 128), [[-1, 128]], 0, c))
+        mark(sq("K4", 64), B("ZR", 0, 128, 1, 64), [[0, 128]], -32, 4.0)
+        iota(sq("D64"), [[0, 128]], 0, 64)
+        asel(sq("D64"), sq("D64"), [[-1, 128]], A.is_equal, 0, 1)
+        for r in (5, 6, 7): mark(B("I567", r, 8, 16), B("I567", r, 8, 16), GROUP, -r, 1.0)
+        mark(sq("R2B"), B("ZR", 0, 128), GROUP + [[0, 16]], -3, 32.0)
+        lin(sq("R5B"), sq("R2B"), 18.5)
+        asel(sq("BD"), B("ONE", 0, 128), GROUP + [[0, 16]], A.is_ge, 0, 1)
+        asel(sq("BD"), sq("BD"), [[16, 8], [0, 16]], A.is_ge, 15, -1)
+        lin(sq("B32"), sq("BD"), 32.0)
+        for r in (8, 9): mark(B("SL1", 0, 24), B("SL1", 0, 24), [[0, 3]] + GROUP, -r, 4096.0)
+        mark(B("SL1", 0, 24), B("SL1", 0, 24), [[-1, 3]] + GROUP, -5, 1.0)
+        for n, lo, r, c in (("SL1", 24, 10, 1.0), ("SL2", 0, 3, 1.0), ("S15", 16, 15, 2.0 ** 25)): mark(B(n, lo, 8), B(n, lo, 8), GROUP, -r, c)
+        mark(B("THS", 0, 24, 1, 8), B("ZR", 0, 24, 1, 8), [[0, 3], [-1, 8]], 0, 4096.0)
+        const(sq("C64"), -64.0)
+        asel(sq("UPM", 128, 112), sq("C64", 128, 112), [[1, 112]], A.is_gt, 0, -1)
+        mark(sq("UPM", 128, 112), sq("UPM", 128, 112), [[0, 112]], -112, 64.0 * CAP)
+        mark(B("IB", 0, 64), B("ZR", 0, 64), [[0, 64]], -112, 1.0)
+        for j in range(2):
+            for b, c in ((0, 14.0), (1, 256.0), (2, 2.0 ** 17), (4, -2.0 ** 17), (5, 0.5 + 0.5 * j), (12, 0.5)):
+                mark(lwc("EE%d" % j), lwc("EE%d" % j), [[-1, 8]], -8 * b, c)
+        for n, first, b, c in (("EJ", "ZR", 0, 28.0), ("EJ", "EJ", 1, 1.0), ("EJ", "EJ", 4, 1.0), ("EB", "ZR", 9, 32.0)):
+            mark(sq(n), B(first, 0, 128), [[-1, 8], [0, 16]], -8 * b, c)
+        for n, w, a, b in (("RAP", V, 8192.0, -2.0 ** 23), ("RAM", V, -8192.0, 2.0 ** 23), ("RAK", 384, 256.0, 1.0 - 2 ** 24)):
+            const(B(n, 0, w), a)
+            const(B(n, 0, w // 16, 16), b)
+        iota(B("RM", 0, H // 2), [[0, 56], [255, 16]], 0, 0)
         iota(DF("c"), [[1, 28]], 0, 0)
         iota(DF("ch"), [[2, 14], [0, 2]], -V, 0)
         iota(DB("cl"), [[0, 14], [1, 2]], 0, 0)
         iota(B("J16", 0, 84), [[16, 3], [0, 28]], 0, 0)
         iota(B("IOX", 0, V), [[1, 28], [28, 16]], 0, 0)
-        ts(col("we0"), row(0), float(2 ** 17), A.mult, row(2), A.add)
-        ts(col("we"), row(1), 256.0, A.mult, col("we0"), A.add)
-        act(lwc("LE"), G8, scale=col("we"))
-        act(B("RAP", 0, V), B("ONE", 0, V), scale=8192.0)
-        act(B("RAP", 0, 28, 16), B("ONE", 0, 28), scale=-HUGE)
-        ts(col("28p"), col("p"), 28.0, A.mult)
-        ts(col("wk"), col("p"), 448.0, A.mult, 448.0, A.add)
-        ts(col("wo"), row(0), row(1), A.add)
-        ts(col("28r6"), row(6), 28.0, A.mult)
-        fill(B("KS", 0, 128, 1, 1), 0.0)
-        fill(B("KS", 7, 8, 16, 1), 2.0)
-        fill(B("KS", 128, 128, 1, 1), -1.0)
-        fill(B("KS", 256, 128, 1, 1), -0.25)
-        fill(B("SB", 0, 192), 0.0)
-        fill(B("GF", 0, 1), -5.0)
-        fill(B("GF", V + 1, 15), -5.0)
-        fill(B("REC", W, 16), 0.0)
-        fill(B("PB", 0, 1), 0.0)
-        fill(B("PB", V + 1, 15), 0.0)
-        act(lwc("L64"), G8, scale=64.0)
-        act(lwc("LK"), G8, scale=col("wk"))
-        act(lwc("LO"), G8, scale=col("wo"))
-        act(aD, DF("c"), bias=col("28p"))
-        act(DB("ch"), DF("ch"), bias=col("28p"))
-        act(sq("P18"), sq("IDN"), scale=float(2 ** 18))
-        act(B("RAM", 0, V), B("RAP", 0, V), scale=-1.0)
-        ts(B("ID", 0, M), B("IDS", 0, M), col("p"), A.is_equal)
-        ts(DF("a37"), aD, 0.5, A.mult, 9.25, A.add)
-        ts(DF("a17"), aD, 2.0, A.mult, 17.0, A.add)
-        ts(DF("a613"), aD, 32.0, A.mult, 16.0 * 613, A.add)
-        iota(B("S17", 0, V), [[2, V]], 17, 0)
-        asel(sq("BD"), B("ONE", 0, 128), [[-16, 8], [0, 16]], A.is_ge, 0, 1)
-        asel(sq("BD"), sq("BD"), [[16, 8], [0, 16]], A.is_ge, 15, -1)
-        for n, k in (("i", 2), ("s1", 4), ("ws", 3), ("hi", 4), ("lo", 4), ("w", 4)): col(n, 128, k)
-        iota(colj("i", 0, 128, 2), [[-H, 2]], -16, -16)
-        iota(colj("s1", 0, 128, 4), [[2, 2], [V, 2]], 613, 4)
-        asel(B("IB", 0, 64), B("ONE", 0, 64), [[0, 64]], A.is_equal, -112, 1)
         iota(B("LPI", 0, 24), [[48, 2], [4, 4], [1, 3]], 0, 0)
         iota(B("PP", 0, 384), [[0, 8], [1, 48]], 0, 0)
         iota(B("PC", 0, V), [[1, 28], [0, 16]], 28, 0)
-        iota(B("IOM", 0, 128), [[1, 8], [0, 16]], 0, 0)
-        act(lwc("L2"), G8, scale=row(2))
-        for d in range(2):
-            act(lwc("DP", d), G8)
-            act(lwc("DM", d), G8, scale=-1.0)
-        total(col("567"), row(5, 3))
-        total(col("012"), row(0, 3))
-        ts(col("w34"), row(3), row(4), A.add, 4096.0, A.mult)
-        ts(colj("ws", 0, 128, 3), row(5, 3), col("w34"), A.add)
-        ts(col("w15"), row(15), float(2 ** 25), A.mult)
-        fill(B("S15", 0, 16), 0.0)
-        act(sq("I567"), sq("IDN"), scale=col("567"))
-        act(sq("R2B"), sq("BD"), scale=row(2))
-        for j in range(3): act(B("SL1", 8 * j, 8), G8, scale=colj("ws", j))
-        act(B("SL1", 24, 8), G8, scale=row(10))
-        for j in range(2): act(B("SL2", 8 * j, 8), G8, scale=row(8 + j))
-        act(B("S15", 16, 8), G8, scale=col("w15"))
-        act(B("THS", 0, 24, 1, 8), B("ONE", 0, 24, 1, 8), scale=4096.0)
-        asel(B("THS", 0, 24, 1, 8), B("THS", 0, 24, 1, 8), [[0, 3], [1, 8]], A.is_equal, 0, -1)
-        act(sq("C64"), B("ONE", 0, 128), scale=-64.0)
-        asel(sq("UPM", 128, 112), sq("C64", 128, 112), [[1, 112]], A.is_gt, 0, -1)
-        asel(sq("UPM", 128, 112), sq("UPM", 128, 112), [[0, 112]], A.not_equal, -112, 1, 64.0 * CAP)
-        act(sq("BIG"), sq("IDN"), scale=-float(2 ** 20))
-        act(B("RAK", 0, 384), B("ONE", 0, 384), scale=256.0)
-        act(B("RAK", 0, 24, 16), B("ONE", 0, 24), scale=-HUGE)
+        lin(aD, DF("c"), bias=col("28p"))
+        lin(DB("ch"), DF("ch"), bias=col("28p"))
+        for n, a, b in (("a37", 32.0, 16.0 * 37), ("a17", 2.0, 17.0), ("a613", 32.0, 16.0 * 613), ("spare", 1.0, 3616.0)): lin(DF(n), aD, a, b)
         cp(B("THB", 0, M, 1, 8), B("THI", 0, M, 1, 8))
         tt(B("THB", M, M, 1, 8), B("THI", 0, M, 1, 8), B("THB", 0, M, 1, 8), A.subtract)
-        fill(col("c"), 4095.0)
-        for n in ("X", "INJ", "TM"): fill(B(n, 0, 64), 0.0)
-        cp(B("CB", 0, 4), colj("s1", 0, 128, 4))
-        ts(colj("hi", 0, 128, 4), B("CB", 0, 4), 16.0, A.mult)
-        tt(colj("lo", 0, 128, 4), colj("s1", 0, 128, 4), B("CB", 0, 4), A.subtract)
-        ts(colj("lo", 0, 128, 4), colj("lo", 0, 128, 4), 16.0, A.mult)
-        for m in range(8):
-            act(B("DG", 112 * m, 112, 1, 112), sq("IDN", 112, 112), scale=colj(("hi", "lo")[m & 1], m >> 1, 112))
         ts(B("LPI", 0, 24), B("LPI", 0, 24), 1, A.arith_shift_right)
         cp(B("LP", 0, 24), B("LPI", 0, 24))
         ts(col("la"), col("p"), 8.0, A.is_ge, 16.0, A.mult)
-        ts(col("lb"), col("p"), 8.0, A.add)
         ts(B("LC", 0, 28), B("ONE", 0, 28), col("la"), A.mult, col("lb"), A.add)
         ts(B("PP", 0, 384), B("PP", 0, 384), 31, A.bitwise_and)
-        ts(B("IOQ", 2, 1), B("IOQ", 0, 1), 7, A.bitwise_and)
-        cp(col("r7"), B("IOQ", 2, 1))
-        ts(B("G8", 8, 8), B("IO", 0, 8), col("r7"), A.is_equal)
-        ts(col("-p"), col("p"), -1.0, A.mult)
-        ts(col("-64r0"), row(0), -64.0, A.mult)
-        fill(colj("w", 0, 128, 4), 0.0)
 
-        def steps(j, k, L):
-            for hi, w in L: asel(colj("w", j, 128, k), colj("w", j, 128, k), [[0, k]], A.is_ge, -hi, 1, w)
-        steps(0, 2, [(104, 0.5), (96, 0.0)])
-        steps(0, 1, [(48, 0.5)])
-        steps(1, 1, [(48, 1.0)])
-        steps(0, 2, [(40, -float(2 ** 17)), (32, 0.0), (24, float(2 ** 17)), (16, 256.0), (8, 14.0)])
-        steps(2, 1, [(40, 1.0), (32, 0.0), (16, 1.0), (8, 28.0)])
-        steps(3, 1, [(80, 32.0), (72, 0.0)])
-        iota(B("RM", 0, H // 2), [[0, 56], [255, 16]], 0, 0)
-        for j in range(2): act(lwc("EE%d" % j), B("G8", 8, 8), scale=colj("w", j))
-        ts(sq("EJ"), B("IOM", 0, 128), col("r7"), A.is_equal, colj("w", 2), A.mult)
-        ts(sq("EB"), B("IOM", 0, 128), col("r7"), A.is_equal, colj("w", 3), A.mult)
-        act(sq("B32"), sq("BD"), scale=32.0)
-        act(sq("N1K"), sq("IDN"), scale=-1024.0)
-        act(sq("HLF"), sq("IDN"), scale=0.5)
-        act(sq("I012"), sq("IDN"), scale=col("012"))
+    def table0():
+        mm(B("Q", 0, V), sq("SLX", 64), B("CR", 0, V, 1, 64), True, False)
+        spread(own(0))
+        mm(B("Q", 0, V), lw("L07", 0), B("G0", 0, V), False, True)
+        lin(B("TN", 16, M, 2), B("Q", 0, M, 2), bias=row(0))
+        lin(B("TN", 17, M, 2), B("Q", 1, M, 2), col("odd"), col("-r0"))
 
-    def sizes(par, bank):
-        mm(B(bank, 0, M), sq("SLE", 64), B("CR", par, M, 2, 64), True, False)
-        mm(B(bank, 0, M), lw("L1", 0), B("G0", par, M, 2), False, True)
+    def values(t):
+        mm(B("Q", 0, V), sq("SLX", 96), B("CR", 0, V, 1, 96), True, False)
+        if t < 2: mm(B("Q", 0, V), lw("L07", 0), B("G0", 0, V), False, False)
+        spread(own(t), True)
+        if t == 2: move(B("VT", 16, V), B("Q", 0, V))
+        for par, a, b in (((0, col("no7"), 0.0), (1, 1.0, col("2r7"))), ((0, 1.0, col("r07")), (1, col("no7"), col("-64r0"))), ())[t]:
+            lin(B("VT", 16 + par, M, 2), B("Q", par, M, 2), a, b)
 
-    def gather(out, tab, off, n, step, qs="vs"):
-        for c in range(0, n, step): move(B("KW", out + 16 * c, 16 * step), ind(B(tab, 0, 464), B(off[0], off[1] + c, step)), qs)
+    def ghosts(t):
+        if t == 0:
+            mm(B("K1", 0, V), sq("SLX", 96), B("CR", 0, V, 1, 96), True, True)
+            lin(B("VT", V + 16, V), B("K1", 0, V), bias=col("28r6"))
+        dma("y", (T["VT"][3:116:16, V + 16:2 * V + 16], [("VT", V + 16, 2 * V + 16, 0, 128)]), B("LG" if t == 0 else "GN%d" % (t - 1), 0, 28))
+
+    def gather(out, tab, off, lo, n):
+        for c in range(0, n, 28): move(B("KW", out + 16 * c, V), ind(B(tab, 0, V + 16), B(off, lo + c, 28)))
 
     def keys_e(bank, base, n):
         for p in range(16): mm(B(bank, 0, n), lw("LE", p), B("KW", base + n * p, n), p == 0, p == 15)
 
     def winners(par, bank):
         scan(B("SE", 0, M), B("RAP", 0, M), B(bank, 0, M), A.add, A.max)
-        ts(half(DF("key2"), par), B("SE", 15, 14, 16), 0.0, A.max)
-
-    def table2():
-        mm(B("Q", 0, V), sq("SLE", 64), B("CR", 0, V, 1, 64), True, False)
-        mm(B("Q", 0, V), lw("L1", 0), B("G0", 0, V), False, True)
-        act(B("TN", 1, M, 2), B("Q", 0, M, 2), bias=row(0))
-        act(B("TN", 2, M, 2), B("Q", 1, M, 2), bias=col("-64r0"))
+        ts(half(DN("key2"), par), B("SE", 15, 14, 16), 0.0, A.max)
 
     def elected(t):
         par, e = t & 1, DN("e")
-        if t: cp(DN("key"), DF("key%d" % t))
-        ts(e, DN("key"), 255, A.bitwise_and)
-        ts(DN("vc"), DN("key"), 8, A.arith_shift_right, 31, A.bitwise_and)
-        ts(DU("z"), e, -1.0, A.add)
-        ts(DU("g"), e, 2.0, A.mult, par - 1.0, A.add)
-        cp(DU("vc"), DN("vc"))
-        act(B("MSK", 0, V), ind(B("ID", 0, M), DU("z")))
-        tt(B("MAT", 0, V), ind(B("GF", 0, 464), DU("g")), B("IOX", 0, V), A.is_equal)
+        ts(e, DN("key%d" % t), 255, A.bitwise_and)
+        ts(DU("z"), e, 15.0, A.add)
+        ts(DU("v"), e, 2.0, A.mult, par + 14.0, A.add)
+        tt(B("MAT", 0, V), ind(B("GF", 240 * par, 240), DU("z")), B("IOX", 0, V), A.is_equal)
         mm(B("PM", 0, 28), sq("IDN"), DB("ch"), True, False)
         mm(B("PM", 0, 28), sq("IDN"), DB("cl"), False, False)
         dist(B("PM", 0, 28), "LK", "MAT", 0, 28, first=False)
-        ts(DF("u"), e, 4.0, A.mult, 13.0 + 2 * par, A.add)
-        ts(DF("s"), e, 64.0, A.mult, 16.0 * (609 + 2 * par), A.add)
         cp(DB("e"), e)
+        lin(DF("u"), DB("e"), 4.0, 13.0 + 2 * par)
+        lin(DF("s"), DB("e"), 64.0, 16.0 * (609 + 2 * par))
         tt(DF("m"), DF("u"), aD, A.mult)
         cp(DU("nk"), B("PM", 0, 28))
         ts(DB("no"), B("PM", 0, 28), 0.0, A.is_lt)
-        act(B("OG", 0, V), ind(B("NW", 0, 2 * CELLS), DU("nk")))
+        move(B("OG", 0, V), ind(B("NW", 0, 2 * CELLS), DU("nk")))
         dist(B("PM", 32, 28), "LO", "OG", 0, 28)
-        cp(DU("o"), B("PM", 32, 28))
-        ts(DF("s37"), B("PM", 32, 28), 32.0, A.mult, 16.0 * 37, A.add)
+        ts(DU("o"), B("PM", 32, 28), 16.0, A.add)
+        lin(DF("s37"), B("PM", 32, 28), 32.0, 16.0 * 37)
         tt(DF("ob"), B("PM", 32, 28), DF("a17"), A.mult)
-
-    def values(t, who):
-        nxt = (t + 1) & 1
-        mm(B("Q", 0, V), sq("SLV", 96), B("CR", 0, V, 1, 96), True, False)
-        if who == 0 and t < 2:
-            mm(B("Q", nxt, M, 2), lw("L1", 7), B("G0", nxt, M, 2), False, False)
-            mm(B("Q", nxt, M, 2), B("KS", 0, 128, 1, 1), B("ONE", 0, M, 1, 1), False, False)
-        spread("Q", 2, ghost(t) if who else own(t), True)
-        if who: act(B("VT", V, V), B("Q", 0, V), bias=col("28r6"))
-        else: act(B("VT", 0, V), B("Q", 0, V))
+        dist(B("PM", 96, 28), "LK1", "MAT", 0, 28, last=False)
+        mm(B("PM", 96, 28), sq("I16"), DB("e"), False, False)
+        mm(B("PM", 96, 28), sq("P13"), DB("no"), False, True)
+        tt(DN("ps"), B("PM", 96, 28), DF("spare"), A.min)
+        cp(DU("ps"), DN("ps"))
 
     def place(u, x):
         ts(x, x, 4, A.arith_shift_right, W - 1, A.bitwise_and)
         cp(u, x)
 
     def trials(t):
-        d, pj, b = dint(t), DN("p", 2), DF("b", 3)
-        tt(B("GD", 0, V), ind(own(t, 32), DU("vc")), B("MSK", 0, V), A.mult)
-        dist(B("PD", 0, 28), "L64", "GD", 0, 28)
-        act(B("ZE", 0, V), ind(zin(t), DU("z")))
-        if t: cp(d, own(t))
+        d, pj, b = own(t), DN("p", 2), DF("b", 3)
+        move(B("GD", 0, V), ind(B("TN" if t == 0 else "VT", 0, V + 16), DU("v")))
+        dist(B("PD", 0, 28), "L3", "GD", 0, 28)
+        move(B("ZE", 0, V), ind(zin(t, 0), DU("z")))
         for j in range(2): ts(part(pj, j), d, j + 1.0, A.add)
         tt(part(b, 0), d, DF("s"), A.mult)
         ts(pj, pj, 15, A.bitwise_and)
@@ -494,26 +474,35 @@ def rank_program(g, core, T, topo):
         cp(DB("p", 2), pj)
         tt(DF("q"), B("PD", 0, 28), DF("a37"), A.mult)
         tt(DF("q"), DF("q"), DF("m"), A.add)
-        for j in range(3): tt(part(DN("ix", 3), j), part(DF("b", 3), j), DF("q"), A.add)
+        for j in range(3): tt(part(DN("ix", 3), j), part(b, j), DF("q"), A.add)
         place(DU("ix", 3), DN("ix", 3))
-        mm(B("PD", 64, 84), sq("IDN"), B("J16", 0, 84), True, False)
-        mm(B("PD", 64, 28), sq("IDN"), own(t), False, False)
-        mm(B("PD", 92, 56), sq("IDN"), DB("p", 2), False, False)
-        for j in (1, 2): mm(B("PD", 64 + 28 * j, 28), sq("P18"), DB("no"), False, False)
-        one(5)
-        for j in range(3):
-            tt(B("MT", j * V, V), ind(REC, part(DU("ix", 3), j)), B("ZE", 0, V), A.max)
-            if j == 1: dist(B("PD", 64, 56), "L64", "MT", 0, 56, first=False, last=False)
-            if j == 2: dist(B("PD", 120, 28), "L64", "MT", 2 * V, 28, first=False)
+        mm(B("PD", 64, 56), sq("IDN"), B("J16", 0, 56), True, False)
+        mm(B("PD", 64, 28), sq("IDN"), d, False, False)
+        mm(B("PD", 92, 28), sq("IDN"), part(DB("p", 2), 0), False, False)
+        mm(B("PD", 92, 28), sq("P18"), DB("no"), False, False)
+        one(4)
+        mm(B("PN", 464, 28), sq("IDN"), B("J16", 56, 28), True, False)
+        mm(B("PN", 464, 28), sq("IDN"), part(DB("p", 2), 1), False, False)
+        mm(B("PN", 464, 28), sq("P18"), DB("no"), False, False)
+        one(3)
+        for j in range(3): tt(B("MT", j * V, V), ind(REC, part(DU("ix", 3), j)), B("ZE", 0, V), A.max)
+        dist(B("PD", 64, 56), "L64", "MT", 0, 56, first=False)
+        dist(B("PN", 464, 28), "L64", "MT", 2 * V, 28, first=False)
+        cp(DF("x"), B("PD", 64, 28))
+        tt(DF("x"), B("PD", 92, 28), DF("x"), A.min)
+        tt(DN("x"), B("PN", 464, 28), DF("x"), A.min)
+
+    def old_values(t):
+        st = 32 if t == 0 else 16
+        for h in range(2):
+            for k in range(16): mm(B("PT", 128 * h + k, 8, 16, 112), B("KW", 112 * st * h + k, 112, st), B("SL2", 0, 8), h + k == 0, h + k == 16)
+            one(16)
+        move(B("PA", 0, 256, 1, 112), B("PT", 0, 256, 1, 112))
 
     def old_damage(t):
-        act(B("VO", 0, V), ind(B("VT", 0, 2 * V), DU("o")))
-        dist(B("PM", 64, 28), "LE", "VO", 0, 28)
-        mm(B("PT", 0, V), lw("L2", 9), B("VT", 0, V), True, False)
-        if t == 1: mm(B("PT", 0, V), sq("I012"), B("TN", 1, V), False, False)
-        spread("PT", 8, DB("e"))
-        unmix(sq("I567"), "VO")
-        tt(DF("ot"), dint(t), DF("s37"), A.mult)
+        move(B("VO", 0, V), ind(B("VT", 0, 2 * V + 16), DU("o")))
+        dist(B("PM", 64, 28), "L3", "VO", 0, 28)
+        tt(DF("ot"), own(t), DF("s37"), A.mult)
         tt(DF("od"), B("PM", 64, 28), DF("a613"), A.mult)
         tt(DF("co"), DF("ob"), DF("od"), A.add)
         tt(DN("io"), DF("ot"), DF("co"), A.add)
@@ -522,9 +511,6 @@ def rank_program(g, core, T, topo):
 
     def choose(t):
         s = str(t)
-        cp(DF("x"), B("PD", 64, 28))
-        tt(DF("x"), B("PD", 92, 28), DF("x"), A.min)
-        tt(DN("x"), B("PD", 120, 28), DF("x"), A.min)
         ts(DN("nd"), DN("x"), 15, A.bitwise_and)
         tt(DF("nt"), DN("nd"), DF("s37"), A.mult)
         cp(B("MV" + s, 0, 28), DN("nd"))
@@ -532,14 +518,23 @@ def rank_program(g, core, T, topo):
         place(DU("in"), DN("in"))
         tt(B("MN", 0, V), ind(REC, DU("in")), B("ZE", 0, V), A.max)
         send(B("LM" + s, 0, 32), B("MV" + s, 0, 32), "rm" + s, -1)
-        spread("PT", 10, B("MV" + s, 0, 28))
-        unmix(lw("DM", 3), "MO")
-        unmix(lw("DP", 3), "MN", True)
-        act(B("T1", 0, V), B("PT", 0, V), scale=row(4))
-        tt(B("PB", 1, V), B("PT", 0, V), B("T1", 0, V), A.subtract)
+        tt(DB("dl"), DN("nd"), own(t), A.subtract)
+        for h, bank in enumerate(("PT", "PS")):
+            mm(B(bank, 0, M), sq("I567"), B("VO", M * h, M), True, False)
+            mm(B(bank, 0, M), lw("DM", 8), B("MO", M * h, M), False, False)
+            for p in range(16): mm(B(bank, p, 14, 16), B("DA", 128 * p + 5, 128), part(DB("dl"), h, 14), False, False)
+            one(16)
+        for h, bank in enumerate(("PT", "PS")):
+            mm(B(bank, 0, M), lw("DP", 8), B("MN", M * h, M), False, True)
+            lin(B("T1", M * h, M), B(bank, 0, M), row(9))
+            tt(B("PB", M * h, M), B(bank, 0, M), B("T1", M * h, M), A.subtract)
+        o, a = ind(B("WD", 0, 4096), DU("ps")), B("PB", 0, V)
+        call("v", o[1][:1], o[1][1:] + a[1], 50 + SCATTER * V, lambda: g.vector.tensor_copy(o[0], a[0]))
 
-    GM = [("GM", 0), ("GM", M), ("GM", 2 * M)]
-    def members(t): ts(B("GM", t * M, M), gf(t), 1.0, A.add)
+    def clear():
+        for j in range(4): dma("y", B("WD", 904 * j, 904), B("ZR", 0, 904), 4000)
+
+    def members(t): ts(B("GM", (t & 1) * M, M), gf(t), 16.0, A.add)
 
     def thresholds(t):
         for h in range(2):
@@ -548,7 +543,7 @@ def rank_program(g, core, T, topo):
             mm(o, B("THB", M + 112 * h, 112, 1, 8), B("THS", 0, 24, 1, 8), False, False)
             mm(o, B("G0", (t & 1) + M * h, 112, 2), B("S15", 0, 24), False, h == 1)
         one(6)
-        act(B("THC", 0, 48, 1, 112), B("PN", 0, 48, 1, 112), bias=col("c", 112))
+        lin(B("THC", 0, 48, 1, 112), B("PN", 0, 48, 1, 112), bias=col("c", 112))
 
     def count():
         for h in range(2): mm(B("PN", 160, 8), B("ONE", 0, 128, 1, 112), B("INJ", 24 * h, 8, 1, 112), h == 0, h == 1)
@@ -558,26 +553,36 @@ def rank_program(g, core, T, topo):
         ts(col("c"), B("CI", 1, 1), 4096.0, A.mult, 4095.0, A.add)
 
     def slot_bases(t):
-        act(B("S2", 0, M), gf(t), scale=32.0, bias=16.0 * 37)
-        act(B("EM", 0, M), gf(t), scale=-129.0 * 2 ** 15, fn=F.Relu)
-        mm(B("PS", 256, M), sq("R2B"), B("VT", t & 1, M, 2), True, True)
-        tt(B("X1", 0, M), gf(t), B("S17", t & 1, M, 2), A.mult)
-        tt(B("PS", 256, M), B("PS", 256, M), B("S2", 0, M), A.mult)
-        tt(B("CC", 0, M), B("PS", 256, M), B("X1", 0, M), A.add)
+        par, o, big = t & 1, B("PS", 256, M), -129.0 * 2 ** 15
+        either(lambda: ts(B("EM", 0, M), gf(t), big, A.mult, 0.0, A.max), lambda: act(B("EM", 0, M), gf(t), big, fn=F.Relu))
+        mm(o, sq("K4", 64), B("CR", par, M, 2, 64), True, False)
+        mm(o, ks(2 + par), B("ONE", 0, M, 1, 1), False, False)
+        mm(o, sq("R2B"), B("VT", 16 + par, M, 2), False, True)
+        tt(B("CC", 0, M), o, gf(t), A.mult)
+
+    def times(o, b, t, h, last):
+        for j, n in enumerate(("D64", ("P13", "P14")[h], "D%d%d" % (t & 1, h))):
+            mm(o, B("PA", 256 * b + 128 * h, 128, 1, 112), sq(n, 112, 112), False, last and j == 2)
+        one(3)
+
+    def slot_open(t):
+        for h in range(2):
+            o = B(("PD", "PM")[h], 256, 112)
+            mm(o, sq("IDN"), B("EM", 112 * h, 112), True, False)
+            mm(o, sq("R5B"), B("VT", 16 + (t & 1) + M * h, 112, 2), False, False)
+            times(o, 0, t, h, False)
 
     def keys(t, h):
-        K, E, AB = "K%d" % h, ("Q", "PT")[h], B("AB", 128 * h, 128, 1, 112)
-        for k in range(16): mm(B(E, k, 16, 16, 112), B("KW", H * h + k, 112, 16), B("SL2", 0, 16), k == 0, k == 15)
+        K, o, x = "K%d" % h, B(("PD", "PM")[h], 256, 112), B("XI", 112 * h, 112)
+        for k in range(16): mm(B(K, k, 32, 16, 112), B("WD", H * h + k + 17, 112, 16), B("SL1", 0, 32), k == 0, k == 15)
         one(16)
-        for k in range(16): mm(B(K, k, 32, 16, 112), B("KW", H * h + k, 112, 16), B("SL1", 0, 32), k == 0, False)
-        one(16)
-        act(AB, B(E, 0, 128, 1, 112), scale=16.0, bias=colj("i", h, 112), fn=F.Abs)
-        for j in (0, 1, 2, 3) if t < 2 else (0, 1, 3): mm(B(K, 128 * j, 128, 1, 112), sq("BIG", 112, 112), AB, False, j == 3)
-        one(4 if t < 2 else 3)
+        move(B("PA", 256 + 128 * h, 128, 1, 112), B(K, 384, 128, 1, 112))
         n = 384 if t < 2 else 256
         scan(B("SC", 384 * h, n, 1, 112), B("RAK", 0, n, 1, 112), B(K, 0, n, 1, 112), A.add, A.max)
-        act(B("PA", 256 + 128 * h, 128, 1, 112), B(K, 384, 128, 1, 112), fn=F.Relu)
-        tt(B("PA", 128 * h, 128, 1, 112), B(E, 128, 128, 1, 112), AB, A.min)
+        times(o, 1, t, h, True)
+        tt(x, o, B("CC", 112 * h, 112), A.add)
+        ts(x, x, 4, A.arith_shift_right, W - 1 + 2 ** 18, A.bitwise_and)
+        ts(B("ISL", 112 * h, 112), x, float(W), A.min)
 
     def injured(t):
         top = B("SC", 15, 48, 16, 112)
@@ -612,104 +617,94 @@ def rank_program(g, core, T, topo):
             for b, (n, lo) in enumerate((("X", 0), ("INJ", 0), ("IB", 0), ("X", 8))):
                 mm(B("K0", 112 * h, 112, 1, 32 * b + 32, 32 * b), B(n, 24 * h + lo, 32, 1, 112), sq("IDN", 112, 112), True, True)
         one(8)
-        act(B("XT", 0, M), B("K0", 0, M))
+        move(B("XT", 0, M), B("K0", 0, M))
 
     def patch(t):
         par = t & 1
         for p in range(16): mm(B("PD", 192 + par, 14, 2), lw("EE%d" % t, p), B("XT", 14 * p, 14), p == 0, p == 15)
         one(16)
-        k = half(DF("key%d" % (t + 1)), par)
+        k = half(DN("key%d" % (t + 1)), par)
         tt(k, B("PD", 192 + par, 14, 2), k, A.max)
 
     def joins(t):
         def name(lo, last):
             mm(B("K1", lo, M), sq("EJ"), B("XT", 0, M), True, False)
-            mm(B("K1", lo, M), B("KS", 128, 128, 1, 1), B("ONE", 0, M, 1, 1), False, last)
+            mm(B("K1", lo, M), ks(0), B("ONE", 0, M, 1, 1), False, last)
         name(0, True)
         mm(B("K0", 256, M), sq("BD"), B("G0", t & 1, M, 2), True, False)
         mm(B("K0", 256, M), sq("EB"), B("XT", 0, M), False, False)
         tt(B("EQ", 0, M), B("K1", 0, M), gf(t), A.is_equal)
         mm(B("K0", 256, M), sq("B32"), B("EQ", 0, M), False, True)
         name(256, False)
-        act(B("A2", 0, M), B("K0", 256, M), bias=col("-p"), fn=F.Abs)
+        either(lambda: ts(B("A2", 0, M), B("K0", 256, M), col("p"), A.not_equal), lambda: act(B("A2", 0, M), B("K0", 256, M), bias=col("-p"), fn=F.Abs))
         mm(B("K1", 256, M), sq("N1K"), B("A2", 0, M), False, True)
         tt(gf(t), B("K1", 256, M), gf(t), A.max)
-        if t < 2: act(B("G0", t & 1, M, 2), gf(t), bias=1.0, fn=F.Sign)
+        if t < 2: either(lambda: ts(B("G0", t & 1, M, 2), gf(t), 0.0, A.is_ge), lambda: act(B("G0", t & 1, M, 2), gf(t), bias=1.0, fn=F.Sign))
 
     def levels(t):
         s = str(t)
-        mm(B("PS", 0, M), sq("IDN"), B("EM", 0, M), True, False)
-        for b in (1, 0):
-            for h in range(2):
-                for j in range(2):
-                    mm(B("PS", 112 * h, 112), B("PA", 256 * b + 128 * h, 128, 1, 112), B("DG", 112 * (4 * (t & 1) + 2 * h + j), 112, 1, 112),
-                       False, b == 0 and h + j == 2)
-        tt(B("XI", 0, M), B("PS", 0, M), B("CC", 0, M), A.add)
-        ts(B("XI", 0, M), B("XI", 0, M), 4, A.arith_shift_right, W - 1 + 2 ** 18, A.bitwise_and)
-        ts(B("ISL", 0, M), B("XI", 0, M), float(W), A.min)
-        for c in range(0, M, 56):
-            move(B("WR", 16 * c, 896), ind(REC, B("ISL", c, 56)))
-            scan(B("KT", 16 * c, 896), B("RM", 0, 896), B("WR", 16 * c, 896), A.min, A.max)
+        for c in range(0, M, 28): move(B("WR", 16 * c, V), ind(REC, B("ISL", c, 28)))
+        for c in range(0, M, 56): scan(B("KT", 16 * c, 896), B("RM", 0, 896), B("WR", 16 * c, 896), A.min, A.max)
         mm(B("PS", 0, M), sq("HLF"), zin(t), True, False)
-        mm(B("PS", 0, M), B("KS", 256, 128, 1, 1), B("ONE", 0, M, 1, 1), False, False)
+        mm(B("PS", 0, M), ks(1), B("ONE", 0, M, 1, 1), False, False)
         mm(B("PS", 0, M), sq("HLF"), B("KT", 15, M, 16), False, True)
         ts(B("ZB" + s, 0, M), B("PS", 0, M), ROUND, A.add, -ROUND, A.add)
-        send(B("LZ" + s, 0, M), B("ZB" + s, 0, M), "rz" + s, 1 + t)
+        send(B("LZ" + s, 16, M), B("ZB" + s, 0, M), "rz" + s, 1 + t)
 
     loads()
     consts()
     neighbours()
     ts(B("G0", 0, V), B("GI", 0, V), 0.0, A.is_ge)
-    ts(B("GU", 0, V), B("GI", 0, V), 1.0, A.add)
-    cp(B("GF", 1, V), B("GI", 0, V))
+    ts(B("GU", 0, V), B("GI", 0, V), 16.0, A.add)
+    for par in range(2): cp(gf(par), B("GI", par, M, 2))
     cp(B("V0", 0, 28), B("VI", 0, 28))
     send(B("LG", 0, 32), B("V0", 0, 32), "rg", -1)
-    sizes(0, "Q")
-    sizes(1, "PT")
-    ts(B("TN", 1, M, 2), B("Q", 0, M), row(0), A.add)
-    act(B("TN", 2, M, 2), B("PT", 0, M), scale=-1.0, bias=col("-r0"))
-    gather(0, "TN", ("GU", 0), V, 28)
+    table0()
+    clear()
+    ghosts(0)
+    gather(0, "TN", "GU", 0, V)
     keys_e("K0", 0, V)
     scan(B("SE", 0, V), B("RAP", 0, V), B("K0", 0, V), A.add, A.max)
-    ts(DN("key"), B("SE", 15, 28, 16), 0.0, A.max)
+    ts(DN("key0"), B("SE", 15, 28, 16), 0.0, A.max)
     scan(B("SE", V, V), B("RAM", 0, V), B("K0", 0, V), A.add, A.min)
-    ts(DF("key1"), B("SE", V + 15, 28, 16), -1.0, A.mult, 0.0, A.max)
-    members(0)
+    ts(DN("key1"), B("SE", V + 15, 28, 16), -1.0, A.mult, 0.0, A.max)
     members(1)
-    values(0, 1)
     elected(0)
     for t in range(RO):
-        values(t, 0)
-        trials(t)
-        old_damage(t)
-        slot_bases(t)
-        if t == 1:
-            gather(CELLS, "TN", GM[2], M, 28)
-            keys_e("K0", CELLS, M)
-            winners(0, "K0")
         thresholds(t)
+        values(t)
+        if t: gather(0, "VT", "GM", (t & 1) * M, M)
+        if t == 1: gather(CELLS, "VT", "GM", 0, M)
+        trials(t)
+        slot_bases(t)
+        old_values(t)
+        old_damage(t)
+        slot_open(t)
+        if t == 1:
+            keys_e("K0", 0, M)
+            winners(1, "K0")
+            keys_e("K1", CELLS, M)
+            winners(0, "K1")
         choose(t)
-        gather(0, "PB", GM[t], M, 56)
         keys(t, 0)
         keys(t, 1)
+        if t < 2: clear()
         injured(t)
         notices(t)
         turn(t)
-        if t == 1:
-            keys_e("PT", 0, M)
-            winners(1, "PT")
-        if t < 2: patch(t)
+        if t < 2:
+            ghosts(t + 1)
+            patch(t)
         joins(t)
         if t < 2:
             elected(t + 1)
             count()
-            values(t + 1, 1)
         levels(t)
-        if t == 0:
-            members(2)
-            table2()
-    dma("y", (T.yl[:, :], []), B("GF", 1, V))
+        if t == 0: members(2)
+        if t > 0: move(B("YL", t & 1, M, 2), gf(t))
+    dma("y", (T.yl[:, :], []), B("YL", 0, V))
     dma("y", (T.yd[:, :], []), B("LD2", 0, 28))
-    dma("y", (T.yz[:, :], []), B("LZ2", 0, M))
-    for _, n, q in order(calls): calls[n][5](q)
+    dma("y", (T.yz[:, :], []), B("LZ2", 16, M))
+    if not PLAN: PLAN.extend(order(calls))
+    for _, n, q in PLAN: calls[n][5](q)
     finish()

@@ -3,7 +3,7 @@ from concourse.mybir import AluOpType, AxisListType, ActivationFunctionType
 V, M, W, RO, CAP = 448, 224, 4096, 3, 44
 CELLS = 16 * M
 H = CELLS // 2
-CYCLE, GATHER, SCATTER, WAKE = 1.04, 1.56, 3.64, 110
+CYCLE, GATHER, SCATTER, WAKE = 0.9, 1.35, 3.2, 175
 ROUND = float(3 * 2 ** 22)
 
 
@@ -264,7 +264,7 @@ def rank_program(g, core, T, topo):
         dst, src = T.cores[(rank + step) % N], T.cores[(rank - step) % N]
         rid, pid = topo.addr(dst, core)
         lanes = topo.engines(core, dst)[:8]
-        calls.append(["gd", [], a[1], {"g": (600, 1800)}, {}, lambda _: send_now(land, a, sem, (rid, pid, sum(1 << e for e in lanes), len(lanes)))])
+        calls.append(["gd", [], a[1], {"g": (600, 2000) if sem != "rg" else (2000, 3500)}, {}, lambda _: send_now(land, a, sem, (rid, pid, sum(1 << e for e in lanes), len(lanes)))])
         calls.append(["x", land[1], [], {"x": (0, 1)}, {len(calls) - 1: 0}, lambda _: arrive(land, sem, len(topo.engines(src, core)[:8]))])
 
     def sq(n, k=128, m=128): return B(n, 0, m, 1, k)
@@ -310,14 +310,12 @@ def rank_program(g, core, T, topo):
         dma("y", B("Z0", 16, M), (T.zl[:, :], []), 2400, True)
         dma("y", B("THI", 0, M, 1, 8), (T.th[:, :], []), 2400, True)
         dma("y", B("REC", 0, W), (T.rec[:, :], []), 5000, True)
-        dma("y", B("NW", 0, W), (T.rec[:, :], []), 7000, True)
-        dma("y", B("NW", W, 2 * CELLS - W), (T.rec[:, 0:2 * CELLS - W], []), 9000, True)
 
     def neighbours():
         cp(B("NBD", 0, V), B("NBI", 0, V))
         tt(B("NBD", V, V), B("NBI", 0, V), B("NBD", 0, V), A.subtract)
         for r in range(2):
-            dma("y", (T["NW"][r:r + 113:16, 0:2 * CELLS], [("NW", 0, 2 * CELLS, r, r + 113)]), B("NBD", r * V, V), 3000)
+            dma("y", (T["NW"][r:r + 113:16, 0:2 * CELLS], [("NW", 0, 2 * CELLS, r, r + 1)]), B("NBD", r * V, V), 3000)
 
     def consts():
         fill(B("ONE", 0, V), 1.0)
@@ -422,11 +420,11 @@ def rank_program(g, core, T, topo):
             lin(B("VT", V + 16, V), B("K1", 0, V), bias=col("28r6"))
         dma("y", (T["VT"][3:116:16, V + 16:2 * V + 16], [("VT", V + 16, 2 * V + 16, 0, 128)]), B("LG" if t == 0 else "GN%d" % (t - 1), 0, 28))
 
-    def gather(out, tab, off, lo, n):
-        for c in range(0, n, 28): move(B("KW", out + 16 * c, V), ind(B(tab, 0, V + 16), B(off, lo + c, 28)))
+    def gather(out, tab, off, lo, n, buf="KW"):
+        for c in range(0, n, 28): move(B(buf, out + 16 * c, V), ind(B(tab, 0, V + 16), B(off, lo + c, 28)))
 
-    def keys_e(bank, base, n):
-        for p in range(16): mm(B(bank, 0, n), lw("LE", p), B("KW", base + n * p, n), p == 0, p == 15)
+    def keys_e(bank, base, n, buf="KW"):
+        for p in range(16): mm(B(bank, 0, n), lw("LE", p), B(buf, base + n * p, n), p == 0, p == 15)
 
     def winners(par, bank):
         scan(B("SE", 0, M), B("RAP", 0, M), B(bank, 0, M), A.add, A.max)
@@ -495,7 +493,7 @@ def rank_program(g, core, T, topo):
     def old_values(t):
         st = 32 if t == 0 else 16
         for h in range(2):
-            for k in range(16): mm(B("PT", 128 * h + k, 8, 16, 112), B("KW", 112 * st * h + k, 112, st), B("SL2", 0, 8), h + k == 0, h + k == 16)
+            for k in range(16): mm(B("PT", 128 * h + k, 8, 16, 112), B("KW" if t else "NW", 112 * st * h + k, 112, st), B("SL2", 0, 8), h + k == 0, h + k == 16)
             one(16)
         move(B("PA", 0, 256, 1, 112), B("PT", 0, 256, 1, 112))
 
@@ -653,7 +651,6 @@ def rank_program(g, core, T, topo):
 
     loads()
     consts()
-    neighbours()
     ts(B("G0", 0, V), B("GI", 0, V), 0.0, A.is_ge)
     ts(B("GU", 0, V), B("GI", 0, V), 16.0, A.add)
     for par in range(2): cp(gf(par), B("GI", par, M, 2))
@@ -662,8 +659,10 @@ def rank_program(g, core, T, topo):
     table0()
     clear()
     ghosts(0)
-    gather(0, "TN", "GU", 0, V)
-    keys_e("K0", 0, V)
+    gather(0, "TN", "GU", 0, V, "NW")
+    keys_e("K0", 0, V, "NW")
+    old_values(0)
+    neighbours()
     scan(B("SE", 0, V), B("RAP", 0, V), B("K0", 0, V), A.add, A.max)
     ts(DN("key0"), B("SE", 15, 28, 16), 0.0, A.max)
     scan(B("SE", V, V), B("RAM", 0, V), B("K0", 0, V), A.add, A.min)
@@ -677,7 +676,7 @@ def rank_program(g, core, T, topo):
         if t == 1: gather(CELLS, "VT", "GM", 0, M)
         trials(t)
         slot_bases(t)
-        old_values(t)
+        if t: old_values(t)
         old_damage(t)
         slot_open(t)
         if t == 1:

@@ -4,6 +4,7 @@ V, M, W, RO, CAP = 448, 224, 4096, 3, 44
 CELLS = 16 * M
 H = CELLS // 2
 CYCLE, GATHER, SCATTER, WAKE = 0.9, 1.35, 3.2, 175
+TRIES = 6000
 ROUND = float(3 * 2 ** 22)
 
 
@@ -19,9 +20,9 @@ SQUARE = ["SLX", "I567", "IDN", "P18", "P13", "P14", "I16", "HLF", "N1K", "BD", 
 SCRATCH = {
     "GI": i4(V), "NBI": i4(V), "VI": i4(28), "THI": i4(M, 8), "Z0": bf(M + 16), "REC": bf(W + 16), "NW": bf(2 * CELLS), "KW": bf(2 * CELLS),
     "WR": bf(CELLS), "KT": bf(CELLS), "WD": bf(4096), "ZR": bf(904), "GF": f4(480), "YL": f4(V), "GU": u2(V), "GM": u2(2 * M), "G0": bf(V),
-    "NBD": bf(2 * V), "THB": bf(2 * M, 8), "TN": bf(V + 16), "PB": bf(V), "T1": bf(V), "VT": bf(2 * V + 16), "CR": bf(V),
+    "NBD": bf(2 * V), "THB": f4(M, 8), "TN": bf(V + 16), "PB": bf(V), "T1": bf(V), "VT": bf(2 * V + 16), "CR": bf(V),
     "ONE": bf(V), "LW": bf(144 * len(SHIFTED)), "SQ": bf(128 * len(SQUARE)), "DA": bf(2064), "KS": bf(512, 1),
-    "SEL": bf(64), "THS": bf(24, 8), "G8": bf(8), "OH": f4(16), "IO": f4(16), "IOQ": i4(2), "COL": f4(24),
+    "SEL": bf(64), "THS": f4(24, 8), "G8": bf(8), "OH": f4(16), "IO": f4(16), "IOQ": i4(2), "COL": f4(24),
     "IOX": f4(V), "RAP": bf(V), "RAM": bf(V), "RAK": bf(384), "RM": bf(H // 2), "J16": bf(84), "PP": i4(384), "PC": bf(V),
     "LPI": i4(24), "LPC": u2(52), "SE": f4(2 * V), "SC": f4(768),
     "ZE": bf(V), "MAT": bf(V), "GD": bf(V), "OG": bf(V), "VO": bf(V), "MT": bf(3 * V), "MO": bf(V), "MN": bf(V),
@@ -45,8 +46,8 @@ ALIAS.update({"V0": ("SB", 0), "MV0": ("SB", 32), "MV1": ("SB", 64), "MV2": ("SB
 PLAN = []
 
 
-def meet(r, s): return r[1] < s[2] and s[1] < r[2] and r[3] < s[4] and s[3] < r[4]
-def covers(r, s): return r[1] <= s[1] and s[2] <= r[2] and r[3] <= s[3] and s[4] <= r[4]
+def meet(r, s): return r[1] < s[2] and s[1] < r[2] and r[3] < s[4] and s[3] < r[4] and not (r[5] == s[5] == 2 and (r[1] - s[1]) & 1)
+def covers(r, s): return r[1] <= s[1] and s[2] <= r[2] and r[3] <= s[3] and s[4] <= r[4] and (r[5] == 1 or r[1:] == s[1:])
 
 
 def order(calls):
@@ -68,50 +69,74 @@ def order(calls):
         d.pop(n, None)
         pre.append(d)
     N = len(calls)
-    post = [{} for c in calls]
-    for n, d in enumerate(pre):
-        for m, lag in d.items(): post[m][n] = lag
+    pre = [list(d.items()) for d in pre]
+    post = [[] for c in calls]
+    for n in range(N):
+        for m, lag in pre[n]: post[m].append((n, lag))
     cost = [min(x[1] for x in c[3].values()) for c in calls]
     tail = list(cost)
     for n in range(N - 1, -1, -1):
-        for m, lag in pre[n].items(): tail[m] = max(tail[m], cost[m] + lag + tail[n])
+        for m, lag in pre[n]: tail[m] = max(tail[m], cost[m] + lag + tail[n])
 
     def place(rank, queue, back):
-        taken, done, plan = {}, [0.0] * N, []
-        for n in sorted(range(N), key=lambda n: (-rank[n], -n if back else n)):
+        taken = {q: ([], []) for q in "vstgyx"}
+        done, start = [0.0] * N, [0.0] * N
+        for n in sorted(range(N - 1, -1, -1) if back else range(N), key=lambda n: -rank[n]):
             busy, until = calls[n][3][queue[n]]
-            t = max([done[m] + lag for m, lag in (post if back else pre)[n].items()], default=0.0) + (until - busy if back else 0)
-            L = taken.setdefault(queue[n], [])
-            lo, hi = 0, len(L)
+            t = 0.0
+            for m, lag in post[n] if back else pre[n]:
+                if done[m] + lag > t: t = done[m] + lag
+            if back: t += until - busy
+            begins, ends = taken[queue[n]]
+            lo, hi = 0, len(ends)
+            if hi and ends[-1] <= t: lo = hi
             while lo < hi:
-                if L[(lo + hi) // 2][1] <= t: lo = (lo + hi) // 2 + 1
-                else: hi = (lo + hi) // 2
-            while lo < len(L) and t + busy > L[lo][0]:
-                t = max(t, L[lo][1])
+                k = (lo + hi) >> 1
+                if ends[k] <= t: lo = k + 1
+                else: hi = k
+            while lo < len(ends) and t + busy > begins[lo]:
+                if ends[lo] > t: t = ends[lo]
                 lo += 1
-            L.insert(lo, (t, t + busy))
-            done[n] = t + (busy if back else until)
-            plan.append((t, n, queue[n]))
-        return done, plan
+            begins.insert(lo, t)
+            ends.insert(lo, t + busy)
+            start[n], done[n] = t, t + (busy if back else until)
+        return done, start
 
-    def both_ways(rank, queue, passes):
-        best = None
-        for k in range(passes):
-            done, plan = place(rank, queue, False)
-            if best is None or max(done) < best[0]: best = (max(done), plan, rank)
-            if k < passes - 1: rank = place(done, queue, True)[0]
-        return best
+    def both_ways(rank, queue):
+        done, start = place(rank, queue, False)
+        again = place(done, queue, True)[0]
+        done2, start2 = place(again, queue, False)
+        return (max(done), start, rank, queue) if max(done) <= max(done2) else (max(done2), start2, again, queue)
 
-    queue = [list(c[3])[-1] for c in calls]
-    best = both_ways(tail, queue, 4)
-    for least in (200, 200, 0, 200):
-        for n in sorted(range(N), key=lambda n: -tail[n]):
-            for q in calls[n][3]:
-                if q == queue[n] or cost[n] < least: continue
-                other = queue[:n] + [q] + queue[n + 1:]
-                b = both_ways(best[2], other, 2)
-                if b[0] < best[0] - 1: best, queue = b, other
-    return sorted(best[1])
+    queue = [c[6] if len(c) > 6 else "s" if len(c[3]) > 1 and c[3]["s"][0] > 200 else list(c[3])[-1] for c in calls]
+    now = both_ways(both_ways(tail, queue)[2], queue)
+    free = [n for n in range(N) if len(calls[n][3]) > 1]
+    for n in sorted(free, key=lambda n: -tail[n]):
+        for q in calls[n][3]:
+            if q != now[3][n] and cost[n] > 200: now = min(now, both_ways(now[2], now[3][:n] + [q] + now[3][n + 1:]), key=lambda x: x[0])
+    seed = [1]
+
+    def draw(k=1.0):
+        seed[0] = (seed[0] * 1103515245 + 12345) % 2 ** 31
+        return seed[0] / 2 ** 31 * k
+
+    best = now
+    for k in range(TRIES):
+        rank, queue = list(now[2]), list(now[3])
+        mid, width, size = draw(max(rank)), (1500, 4000, 8000)[int(draw(3))], (200, 600, 1500)[int(draw(3))]
+        near = [n for n in free if abs(rank[n] - mid) < width]
+        for _ in range(int(draw(4)) if near else 0):
+            n = near[int(draw(len(near)))]
+            queue[n] = list(calls[n][3])[int(draw(len(calls[n][3])))]
+        for n in range(N):
+            if abs(rank[n] - mid) < width: rank[n] += draw(size)
+        for n in range(N - 1, -1, -1):
+            for m, lag in pre[n]:
+                if rank[m] <= rank[n]: rank[m] = rank[n] + 0.001
+        other = both_ways(rank, queue)
+        if other[0] <= now[0] + draw(200 * (1 - k / TRIES)): now = other
+        if now[0] < best[0]: best = now
+    return sorted((best[1][n], n, best[3][n]) for n in range(N))
 
 
 def builder(g, T):
@@ -202,7 +227,7 @@ def rank_program(g, core, T, topo):
     def B(n, lo, cnt, st=1, p=128, p0=0):
         if n in ALIAS: n, lo = ALIAS[n][0], lo + ALIAS[n][1]
         hi = lo + (cnt - 1) * st + 1
-        return (T[n][p0:p, lo:hi] if st == 1 else T[n][p0:p, lo:hi:st], [(n, lo, hi, p0, p)], cnt, n)
+        return (T[n][p0:p, lo:hi] if st == 1 else T[n][p0:p, lo:hi:st], [(n, lo, hi, p0, p, st)], cnt, n)
 
     def like(n, o): return B(n, 0, o[2], 1, o[1][0][4], o[1][0][3])
     def ind(win, off): return (win[0].indirect(off[0]), win[1] + off[1], 16 * off[2], None)
@@ -232,7 +257,7 @@ def rank_program(g, core, T, topo):
         else: call("s", o[1] + acc[1], a[1], ns, lambda: g.scalar.activation(o[0], a[0], fn, accum_out=acc[0]))
 
     def iota(o, pat, base, cm):
-        call("g", o[1], [], 130 + 2 * CYCLE * o[2], lambda: g.iota(o[0], pat, base, cm, allow_small_or_imprecise_dtypes=True), o[1][0][3] > 0)
+        call("g", o[1], [], 130 + 2 * CYCLE * o[2] + (2 * WAKE if o[1][0][3] else 0), lambda: g.iota(o[0], pat, base, cm, allow_small_or_imprecise_dtypes=True), o[1][0][3] > 0)
 
     def asel(o, a, pat, op, base, cm, c=0.0): call("g", o[1], a[1], 170 + 2 * CYCLE * o[2], lambda: g.affine_select(o[0], a[0], pat, op, c, base, cm))
     def mark(o, a, pat, base, c): asel(o, a, pat, A.not_equal, base, 1, c)
@@ -250,7 +275,9 @@ def rank_program(g, core, T, topo):
         ways = [lambda: fill(o, c), lambda: act(o, like("ONE", o), c)]
         either(*(ways + [lambda: iota(o, [[0, o[2]]], int(c), 0)] * (c == int(c))))
 
-    def mm(o, l, r, start, stop): call("t", o[1], l[1] + r[1], CYCLE / 2 * max(min(64, l[2]), r[2]), lambda: g.tensor.matmul(o[0], l[0], r[0], start, stop))
+    def mm(o, l, r, start, stop):
+        ns = CYCLE / 2 * max(min(64, l[2]), r[2]) * (4 if SCRATCH[l[3]][2] == "float32" else 1)
+        call("t", o[1], l[1] + r[1], ns, lambda: g.tensor.matmul(o[0], l[0], r[0], start, stop))
 
     def one(k):
         L = calls[-k:]
@@ -305,17 +332,17 @@ def rank_program(g, core, T, topo):
 
     def loads():
         dma("s", B("VI", 0, 28), (T.val[:, :], []))
-        dma("y", B("GI", 0, V), (T.gl[:, :], []))
-        dma("y", B("NBI", 0, V), (T.nb[:, :], []), 2200, True)
-        dma("y", B("Z0", 16, M), (T.zl[:, :], []), 2400, True)
-        dma("y", B("THI", 0, M, 1, 8), (T.th[:, :], []), 2400, True)
-        dma("y", B("REC", 0, W), (T.rec[:, :], []), 5000, True)
+        dma("y", B("GI", 0, V), (T.gl[:, :], []), 2400)
+        dma("y", B("NBI", 0, V), (T.nb[:, :], []), 5000, True)
+        dma("y", B("Z0", 16, M), (T.zl[:, :], []), 5000, True)
+        dma("y", B("THI", 0, M, 1, 8), (T.th[:, :], []), 5000, True)
+        dma("y", B("REC", 0, W), (T.rec[:, :], []), 10000, True)
 
     def neighbours():
         cp(B("NBD", 0, V), B("NBI", 0, V))
         tt(B("NBD", V, V), B("NBI", 0, V), B("NBD", 0, V), A.subtract)
         for r in range(2):
-            dma("y", (T["NW"][r:r + 113:16, 0:2 * CELLS], [("NW", 0, 2 * CELLS, r, r + 1)]), B("NBD", r * V, V), 3000)
+            dma("y", (T["NW"][r:r + 113:16, 0:2 * CELLS], [("NW", 0, 2 * CELLS, r, r + 1, 1)]), B("NBD", r * V, V), 3000)
 
     def consts():
         fill(B("ONE", 0, V), 1.0)
@@ -348,8 +375,10 @@ def rank_program(g, core, T, topo):
         for n, a, b in (("28p", 28.0, 0.0), ("wk", 448.0, 448.0), ("p1", 1.0, 1.0), ("-p", -1.0, 0.0), ("lb", 1.0, 8.0)): lin(col(n), col("p"), a, b)
         for n, d, a in (("L07", 0, 1.0), ("L07", 7, 1.0), ("L64", 0, 64.0), ("LK", 0, col("wk")), ("LK1", 0, col("p1")), ("DP", 0, 1.0),
                         ("DP", 1, 1.0), ("DM", 0, -1.0), ("DM", 1, -1.0)): lin(lwc(n, d), G8, a)
-        for n, r, c in (("LE", 0, 2.0 ** 17), ("LE", 1, 256.0), ("LE", 2, 1.0), ("LO", 0, 1.0), ("LO", 1, 1.0), ("L3", 3, 1.0)):
-            mark(lwc(n), lwc(n), GROUP, -r, c)
+        lin(col("we0"), row(0), 2.0 ** 17, row(2))
+        lin(col("we"), row(1), 256.0, col("we0"))
+        lin(col("wo"), row(0), 1.0, row(1))
+        for n, a in (("LE", col("we")), ("LO", col("wo")), ("L3", row(3))): lin(lwc(n), G8, a)
         mark(sq("IDN"), B("ZR", 0, 128), [[-1, 128]], 0, 1.0)
         for n, c in (("P18", 2.0 ** 18), ("P13", 8192.0), ("P14", 16384.0), ("I16", 16.0), ("HLF", 0.5), ("N1K", -1024.0),
                      ("D00", 1616.0), ("D01", 592.0), ("D10", 1648.0), ("D11", 624.0)):
@@ -392,7 +421,6 @@ def rank_program(g, core, T, topo):
         lin(DB("ch"), DF("ch"), bias=col("28p"))
         for n, a, b in (("a37", 32.0, 16.0 * 37), ("a17", 2.0, 17.0), ("a613", 32.0, 16.0 * 613), ("spare", 1.0, 3616.0)): lin(DF(n), aD, a, b)
         cp(B("THB", 0, M, 1, 8), B("THI", 0, M, 1, 8))
-        tt(B("THB", M, M, 1, 8), B("THI", 0, M, 1, 8), B("THB", 0, M, 1, 8), A.subtract)
         ts(B("LPI", 0, 24), B("LPI", 0, 24), 1, A.arith_shift_right)
         cp(B("LP", 0, 24), B("LPI", 0, 24))
         ts(col("la"), col("p"), 8.0, A.is_ge, 16.0, A.mult)
@@ -400,11 +428,13 @@ def rank_program(g, core, T, topo):
         ts(B("PP", 0, 384), B("PP", 0, 384), 31, A.bitwise_and)
 
     def table0():
-        mm(B("Q", 0, V), sq("SLX", 64), B("CR", 0, V, 1, 64), True, False)
-        spread(own(0))
-        mm(B("Q", 0, V), lw("L07", 0), B("G0", 0, V), False, True)
-        lin(B("TN", 16, M, 2), B("Q", 0, M, 2), bias=row(0))
-        lin(B("TN", 17, M, 2), B("Q", 1, M, 2), col("odd"), col("-r0"))
+        for par, bank in enumerate(("Q", "PT")):
+            for p in range(16): mm(B(bank, 14 * p, 14), B("DA", 128 * p + 12, 128), half(own(0), par), p == 0, False)
+            one(16)
+            mm(B(bank, 0, M), sq("SLX", 64), B("CR", par, M, 2, 64), False, False)
+            mm(B(bank, 0, M), lw("L07", 0), B("G0", par, M, 2), False, True)
+        lin(B("TN", 16, M, 2), B("Q", 0, M), bias=row(0))
+        lin(B("TN", 17, M, 2), B("PT", 0, M), col("odd"), col("-r0"))
 
     def values(t):
         mm(B("Q", 0, V), sq("SLX", 96), B("CR", 0, V, 1, 96), True, False)
@@ -418,17 +448,19 @@ def rank_program(g, core, T, topo):
         if t == 0:
             mm(B("K1", 0, V), sq("SLX", 96), B("CR", 0, V, 1, 96), True, True)
             lin(B("VT", V + 16, V), B("K1", 0, V), bias=col("28r6"))
-        dma("y", (T["VT"][3:116:16, V + 16:2 * V + 16], [("VT", V + 16, 2 * V + 16, 0, 128)]), B("LG" if t == 0 else "GN%d" % (t - 1), 0, 28))
+        dma("y", (T["VT"][3:116:16, V + 16:2 * V + 16], [("VT", V + 16, 2 * V + 16, 0, 128, 1)]), B("LG" if t == 0 else "GN%d" % (t - 1), 0, 28), 3000)
 
     def gather(out, tab, off, lo, n, buf="KW"):
-        for c in range(0, n, 28): move(B(buf, out + 16 * c, V), ind(B(tab, 0, V + 16), B(off, lo + c, 28)))
+        for c in range(0, n, 28):
+            move(B(buf, out + 16 * c, V), ind(B(tab, 0, V + 16), B(off, lo + c, 28)))
+            if buf == "NW" and c % 56 == 0: calls[-1].append("v")
 
     def keys_e(bank, base, n, buf="KW"):
         for p in range(16): mm(B(bank, 0, n), lw("LE", p), B(buf, base + n * p, n), p == 0, p == 15)
 
     def winners(par, bank):
-        scan(B("SE", 0, M), B("RAP", 0, M), B(bank, 0, M), A.add, A.max)
-        ts(half(DN("key2"), par), B("SE", 15, 14, 16), 0.0, A.max)
+        scan(B("SE", M * par, M), B("RAP", 0, M), B(bank, 0, M), A.add, A.max)
+        ts(half(DN("key2"), par), B("SE", M * par + 15, 14, 16), 0.0, A.max)
 
     def elected(t):
         par, e = t & 1, DN("e")
@@ -450,10 +482,10 @@ def rank_program(g, core, T, topo):
         ts(DU("o"), B("PM", 32, 28), 16.0, A.add)
         lin(DF("s37"), B("PM", 32, 28), 32.0, 16.0 * 37)
         tt(DF("ob"), B("PM", 32, 28), DF("a17"), A.mult)
-        dist(B("PM", 96, 28), "LK1", "MAT", 0, 28, last=False)
-        mm(B("PM", 96, 28), sq("I16"), DB("e"), False, False)
-        mm(B("PM", 96, 28), sq("P13"), DB("no"), False, True)
-        tt(DN("ps"), B("PM", 96, 28), DF("spare"), A.min)
+        dist(B("K0", 0, 28), "LK1", "MAT", 0, 28, last=False)
+        mm(B("K0", 0, 28), sq("I16"), DB("e"), False, False)
+        mm(B("K0", 0, 28), sq("P13"), DB("no"), False, True)
+        tt(DN("ps"), B("K0", 0, 28), DF("spare"), A.min)
         cp(DU("ps"), DN("ps"))
 
     def place(u, x):
@@ -469,9 +501,9 @@ def rank_program(g, core, T, topo):
         tt(part(b, 0), d, DF("s"), A.mult)
         ts(pj, pj, 15, A.bitwise_and)
         for j in range(2): tt(part(b, j + 1), part(pj, j), DF("s"), A.mult)
+        for j in range(3): tt(part(b, j), part(b, j), DF("m"), A.add)
         cp(DB("p", 2), pj)
         tt(DF("q"), B("PD", 0, 28), DF("a37"), A.mult)
-        tt(DF("q"), DF("q"), DF("m"), A.add)
         for j in range(3): tt(part(DN("ix", 3), j), part(b, j), DF("q"), A.add)
         place(DU("ix", 3), DN("ix", 3))
         mm(B("PD", 64, 56), sq("IDN"), B("J16", 0, 56), True, False)
@@ -491,11 +523,11 @@ def rank_program(g, core, T, topo):
         tt(DN("x"), B("PN", 464, 28), DF("x"), A.min)
 
     def old_values(t):
-        st = 32 if t == 0 else 16
+        bank, src, st = ("Q", "KW", 16) if t else ("PT", "NW", 32)
         for h in range(2):
-            for k in range(16): mm(B("PT", 128 * h + k, 8, 16, 112), B("KW" if t else "NW", 112 * st * h + k, 112, st), B("SL2", 0, 8), h + k == 0, h + k == 16)
+            for k in range(16): mm(B(bank, 128 * h + k, 8, 16, 112), B(src, 112 * st * h + k, 112, st), B("SL2", 0, 8), h + k == 0, h + k == 16)
             one(16)
-        move(B("PA", 0, 256, 1, 112), B("PT", 0, 256, 1, 112))
+        move(B("PA", 0, 256, 1, 112), B(bank, 0, 256, 1, 112))
 
     def old_damage(t):
         move(B("VO", 0, V), ind(B("VT", 0, 2 * V + 16), DU("o")))
@@ -519,10 +551,10 @@ def rank_program(g, core, T, topo):
         tt(DB("dl"), DN("nd"), own(t), A.subtract)
         for h, bank in enumerate(("PT", "PS")):
             mm(B(bank, 0, M), sq("I567"), B("VO", M * h, M), True, False)
-            mm(B(bank, 0, M), lw("DM", 8), B("MO", M * h, M), False, False)
             for p in range(16): mm(B(bank, p, 14, 16), B("DA", 128 * p + 5, 128), part(DB("dl"), h, 14), False, False)
             one(16)
         for h, bank in enumerate(("PT", "PS")):
+            mm(B(bank, 0, M), lw("DM", 8), B("MO", M * h, M), False, False)
             mm(B(bank, 0, M), lw("DP", 8), B("MN", M * h, M), False, True)
             lin(B("T1", M * h, M), B(bank, 0, M), row(9))
             tt(B("PB", M * h, M), B(bank, 0, M), B("T1", M * h, M), A.subtract)
@@ -530,7 +562,7 @@ def rank_program(g, core, T, topo):
         call("v", o[1][:1], o[1][1:] + a[1], 50 + SCATTER * V, lambda: g.vector.tensor_copy(o[0], a[0]))
 
     def clear():
-        for j in range(4): dma("y", B("WD", 904 * j, 904), B("ZR", 0, 904), 4000)
+        for j in range(4): dma("y", B("WD", 904 * j, 904), B("ZR", 0, 904), 8000)
 
     def members(t): ts(B("GM", (t & 1) * M, M), gf(t), 16.0, A.add)
 
@@ -538,9 +570,8 @@ def rank_program(g, core, T, topo):
         for h in range(2):
             o = B("PN", 24 * h, 24, 1, 112)
             mm(o, B("THB", 112 * h, 112, 1, 8), B("THS", 0, 24, 1, 8), h == 0, False)
-            mm(o, B("THB", M + 112 * h, 112, 1, 8), B("THS", 0, 24, 1, 8), False, False)
             mm(o, B("G0", (t & 1) + M * h, 112, 2), B("S15", 0, 24), False, h == 1)
-        one(6)
+        one(4)
         lin(B("THC", 0, 48, 1, 112), B("PN", 0, 48, 1, 112), bias=col("c", 112))
 
     def count():
@@ -574,9 +605,10 @@ def rank_program(g, core, T, topo):
         K, o, x = "K%d" % h, B(("PD", "PM")[h], 256, 112), B("XI", 112 * h, 112)
         for k in range(16): mm(B(K, k, 32, 16, 112), B("WD", H * h + k + 17, 112, 16), B("SL1", 0, 32), k == 0, k == 15)
         one(16)
-        move(B("PA", 256 + 128 * h, 128, 1, 112), B(K, 384, 128, 1, 112))
         n = 384 if t < 2 else 256
-        scan(B("SC", 384 * h, n, 1, 112), B("RAK", 0, n, 1, 112), B(K, 0, n, 1, 112), A.add, A.max)
+        for j in (h, 1 - h):
+            if j: scan(B("SC", 384 * h, n, 1, 112), B("RAK", 0, n, 1, 112), B(K, 0, n, 1, 112), A.add, A.max)
+            else: move(B("PA", 256 + 128 * h, 128, 1, 112), B(K, 384, 128, 1, 112))
         times(o, 1, t, h, True)
         tt(x, o, B("CC", 112 * h, 112), A.add)
         ts(x, x, 4, A.arith_shift_right, W - 1 + 2 ** 18, A.bitwise_and)
@@ -636,8 +668,8 @@ def rank_program(g, core, T, topo):
         name(256, False)
         either(lambda: ts(B("A2", 0, M), B("K0", 256, M), col("p"), A.not_equal), lambda: act(B("A2", 0, M), B("K0", 256, M), bias=col("-p"), fn=F.Abs))
         mm(B("K1", 256, M), sq("N1K"), B("A2", 0, M), False, True)
-        tt(gf(t), B("K1", 256, M), gf(t), A.max)
-        if t < 2: either(lambda: ts(B("G0", t & 1, M, 2), gf(t), 0.0, A.is_ge), lambda: act(B("G0", t & 1, M, 2), gf(t), bias=1.0, fn=F.Sign))
+        tt(B("YL", t & 1, M, 2) if t else gf(t), B("K1", 256, M), gf(t), A.max)
+        if t == 0: either(lambda: ts(B("G0", 0, M, 2), gf(0), 0.0, A.is_ge), lambda: act(B("G0", 0, M, 2), gf(0), bias=1.0, fn=F.Sign))
 
     def levels(t):
         s = str(t)
@@ -651,9 +683,10 @@ def rank_program(g, core, T, topo):
 
     loads()
     consts()
-    ts(B("G0", 0, V), B("GI", 0, V), 0.0, A.is_ge)
     ts(B("GU", 0, V), B("GI", 0, V), 16.0, A.add)
-    for par in range(2): cp(gf(par), B("GI", par, M, 2))
+    for par in range(2):
+        ts(B("G0", par, M, 2), B("GI", par, M, 2), 0.0, A.is_ge)
+        cp(gf(par), B("GI", par, M, 2))
     cp(B("V0", 0, 28), B("VI", 0, 28))
     send(B("LG", 0, 32), B("V0", 0, 32), "rg", -1)
     table0()
@@ -670,11 +703,11 @@ def rank_program(g, core, T, topo):
     members(1)
     elected(0)
     for t in range(RO):
-        thresholds(t)
         values(t)
         if t: gather(0, "VT", "GM", (t & 1) * M, M)
         if t == 1: gather(CELLS, "VT", "GM", 0, M)
         trials(t)
+        thresholds(t)
         slot_bases(t)
         if t: old_values(t)
         old_damage(t)
@@ -682,8 +715,8 @@ def rank_program(g, core, T, topo):
         if t == 1:
             keys_e("K0", 0, M)
             winners(1, "K0")
-            keys_e("K1", CELLS, M)
-            winners(0, "K1")
+            keys_e("Q", CELLS, M)
+            winners(0, "Q")
         choose(t)
         keys(t, 0)
         keys(t, 1)
@@ -700,7 +733,6 @@ def rank_program(g, core, T, topo):
             count()
         levels(t)
         if t == 0: members(2)
-        if t > 0: move(B("YL", t & 1, M, 2), gf(t))
     dma("y", (T.yl[:, :], []), B("YL", 0, V))
     dma("y", (T.yd[:, :], []), B("LD2", 0, 28))
     dma("y", (T.yz[:, :], []), B("LZ2", 16, M))

from concourse.mybir import AluOpType, AxisListType, ActivationFunctionType

V, M, W, RO, CAP = 448, 224, 4096, 3, 44
CELLS = 16 * M
H = CELLS // 2
CYCLE, GATHER, SCATTER, WAKE = 0.9, 1.35, 3.2, 175
TRIES = 6000
ROUND = float(3 * 2 ** 22)


def bf(n, p=128): return ("sbuf", [p, n], "bfloat16")
def f4(n, p=128): return ("sbuf", [p, n], "float32")
def i4(n, p=128): return ("sbuf", [p, n], "int32")
def u2(n): return ("sbuf", [128, n], "uint16")


SHIFTED = ["L07", "LE", "L64", "LK", "LK1", "LO", "L3", "DP", "DM", "EE0", "EE1"]
SQUARE = ["SLX", "I567", "IDN", "P18", "P13", "P14", "I16", "HLF", "N1K", "BD", "B32", "R2B", "R5B", "EJ", "EB", "UPM", "C64",
          "D64", "D00", "D01", "D10", "D11", "K4"]
SCRATCH = {
    "GI": i4(V), "NBI": i4(V), "VI": i4(28), "THI": i4(M, 8), "Z0": bf(M + 16), "REC": bf(W + 16), "NW": bf(2 * CELLS), "KW": bf(2 * CELLS),
    "WR": bf(CELLS), "KT": bf(CELLS), "WD": bf(4096), "ZR": bf(904), "GF": f4(480), "YL": f4(V), "GU": u2(V), "GM": u2(2 * M), "G0": bf(V),
    "NBD": bf(2 * V), "THB": f4(M, 8), "TN": bf(V + 16), "PB": bf(V), "T1": bf(V), "VT": bf(2 * V + 16), "CR": bf(V),
    "ONE": bf(V), "LW": bf(144 * len(SHIFTED)), "SQ": bf(128 * len(SQUARE)), "DA": bf(2064), "KS": bf(512, 1),
    "SEL": bf(64), "THS": f4(24, 8), "G8": bf(8), "OH": f4(16), "IO": f4(16), "IOQ": i4(2), "COL": f4(24),
    "IOX": f4(V), "RAP": bf(V), "RAM": bf(V), "RAK": bf(384), "RM": bf(H // 2), "J16": bf(84), "PP": i4(384), "PC": bf(V),
    "LPI": i4(24), "LPC": u2(52), "SE": f4(2 * V), "SC": f4(768),
    "ZE": bf(V), "MAT": bf(V), "GD": bf(V), "OG": bf(V), "VO": bf(V), "MT": bf(3 * V), "MO": bf(V), "MN": bf(V),
    "PA": bf(512), "TI": i4(96), "THC": f4(48), "X": bf(64), "INJ": bf(64), "IB": bf(64), "TM": bf(64),
    "OHP": bf(384), "OHC": bf(V), "XT": bf(M), "EQ": bf(M), "A2": bf(M), "EM": bf(M), "CC": f4(M),
    "XI": i4(M), "ISL": u2(M), "CF": f4(16), "CI": i4(4), "SB": bf(32 * 6), "GN2": f4(28), "LD2": f4(28), "LG": bf(32),
    "DF": f4(28 * 24), "DN": i4(28 * 20), "DU": u2(28 * 14), "DB": bf(28 * 8),
}
PSUM = ["PT", "K0", "K1", "Q", "PS", "PD", "PM", "PN"]
for _n in PSUM: SCRATCH[_n] = ("psum", [128, 512], "float32")
for _t in range(RO):
    SCRATCH["LM%d" % _t] = bf(32)
    SCRATCH["LZ%d" % _t] = bf(M + 16)
    SCRATCH["ZB%d" % _t] = bf(M)
    if _t < 2: SCRATCH["LD%d" % _t] = bf(32)
SEMAPHORES = ["cv", "cs", "ct", "cg", "rg"] + ["dma%d" % k for k in range(32)] + ["ls%d" % k for k in range(10)] + \
    [a + str(k) for a in ("rm", "rd", "rz") for k in range(RO)]
ALIAS = {n: ("SQ", 128 * k) for k, n in enumerate(SQUARE)}
ALIAS.update({"V0": ("SB", 0), "MV0": ("SB", 32), "MV1": ("SB", 64), "MV2": ("SB", 96), "GN0": ("SB", 128), "GN1": ("SB", 160),
              "LP": ("LPC", 0), "LC": ("LPC", 24), "SL1": ("SEL", 0), "SL2": ("SEL", 32), "S15": ("SEL", 40)})
PLAN = []


def meet(r, s): return r[1] < s[2] and s[1] < r[2] and r[3] < s[4] and s[3] < r[4] and not (r[5] == s[5] == 2 and (r[1] - s[1]) & 1)
def covers(r, s): return r[1] <= s[1] and s[2] <= r[2] and r[3] <= s[3] and s[4] <= r[4] and (r[5] == 1 or r[1:] == s[1:])


def order(calls):
    log, pre = {}, []
    for n, c in enumerate(calls):
        d = dict(c[4])
        for regs, w in ((c[2], False), (c[1], True)):
            for r in regs:
                for s, sw, m in log.get(r[0], []):
                    if r[0] in PSUM or ((w or sw) and meet(r, s)):
                        same = c[0] == calls[m][0] and c[0] in ("v", "s", "t", "g")
                        d[m] = max(d.get(m, 0), 0 if same and (c[0] == "t" or not sw) else WAKE)
        for regs, w in ((c[2], False), (c[1], True)):
            for r in regs:
                L = log.setdefault(r[0], [])
                if r[0] in PSUM: L[:] = []
                elif w: L[:] = [x for x in L if not covers(r, x[0])]
                L.append((r, w, n))
        d.pop(n, None)
        pre.append(d)
    N = len(calls)
    pre = [list(d.items()) for d in pre]
    post = [[] for c in calls]
    for n in range(N):
        for m, lag in pre[n]: post[m].append((n, lag))
    cost = [min(x[1] for x in c[3].values()) for c in calls]
    tail = list(cost)
    for n in range(N - 1, -1, -1):
        for m, lag in pre[n]: tail[m] = max(tail[m], cost[m] + lag + tail[n])

    def place(rank, queue, back):
        taken = {q: ([], []) for q in "vstgyx"}
        done, start = [0.0] * N, [0.0] * N
        for n in sorted(range(N - 1, -1, -1) if back else range(N), key=lambda n: -rank[n]):
            busy, until = calls[n][3][queue[n]]
            t = 0.0
            for m, lag in post[n] if back else pre[n]:
                if done[m] + lag > t: t = done[m] + lag
            if back: t += until - busy
            begins, ends = taken[queue[n]]
            lo, hi = 0, len(ends)
            if hi and ends[-1] <= t: lo = hi
            while lo < hi:
                k = (lo + hi) >> 1
                if ends[k] <= t: lo = k + 1
                else: hi = k
            while lo < len(ends) and t + busy > begins[lo]:
                if ends[lo] > t: t = ends[lo]
                lo += 1
            begins.insert(lo, t)
            ends.insert(lo, t + busy)
            start[n], done[n] = t, t + (busy if back else until)
        return done, start

    def both_ways(rank, queue):
        done, start = place(rank, queue, False)
        again = place(done, queue, True)[0]
        done2, start2 = place(again, queue, False)
        return (max(done), start, rank, queue) if max(done) <= max(done2) else (max(done2), start2, again, queue)

    queue = [c[6] if len(c) > 6 else "s" if len(c[3]) > 1 and c[3]["s"][0] > 200 else list(c[3])[-1] for c in calls]
    now = both_ways(both_ways(tail, queue)[2], queue)
    free = [n for n in range(N) if len(calls[n][3]) > 1]
    for n in sorted(free, key=lambda n: -tail[n]):
        for q in calls[n][3]:
            if q != now[3][n] and cost[n] > 200: now = min(now, both_ways(now[2], now[3][:n] + [q] + now[3][n + 1:]), key=lambda x: x[0])
    seed = [1]

    def draw(k=1.0):
        seed[0] = (seed[0] * 1103515245 + 12345) % 2 ** 31
        return seed[0] / 2 ** 31 * k

    best = now
    for k in range(TRIES):
        rank, queue = list(now[2]), list(now[3])
        mid, width, size = draw(max(rank)), (1500, 4000, 8000)[int(draw(3))], (200, 600, 1500)[int(draw(3))]
        near = [n for n in free if abs(rank[n] - mid) < width]
        for _ in range(int(draw(4)) if near else 0):
            n = near[int(draw(len(near)))]
            queue[n] = list(calls[n][3])[int(draw(len(calls[n][3])))]
        for n in range(N):
            if abs(rank[n] - mid) < width: rank[n] += draw(size)
        for n in range(N - 1, -1, -1):
            for m, lag in pre[n]:
                if rank[m] <= rank[n]: rank[m] = rank[n] + 0.001
        other = both_ways(rank, queue)
        if other[0] <= now[0] + draw(200 * (1 - k / TRIES)): now = other
        if now[0] < best[0]: best = now
    return sorted((best[1][n], n, best[3][n]) for n in range(N))


def builder(g, T):
    eng = {"v": g.vector, "s": g.scalar, "t": g.tensor, "g": g, "y": g.sync}
    cnt = {"v": 0, "s": 0, "t": 0, "g": 0, "dma": 0, "ls": 0, "alone": False}
    known = {q: {} for q in eng}
    log = {}
    total = {}

    def wait(q, evs):
        k = known[q]
        top = {}
        for e in evs:
            if k.get(e[0], 0) < e[1] and (e[0] not in top or top[e[0]][1] < e[1]): top[e[0]] = e
        for e in sorted(top.values(), key=lambda e: -sum(e[2].values())):
            if k.get(e[0], 0) >= e[1]: continue
            eng[q].wait_ge(T.sem[e[0]], e[1])
            k[e[0]] = e[1]
            for s, n in e[2].items():
                if k.get(s, 0) < n: k[s] = n

    def deps(q, outs, ins, comp):
        evs = []
        for regs, w in ((ins, False), (outs, True)):
            for r in regs:
                for s, sw, sq, ev in log.get(r[0], []):
                    same = comp and sq == q
                    if r[0] in PSUM:
                        if not same or (q != "t" and (w or sw)): evs.append(ev)
                    elif (w or sw) and meet(r, s):
                        if same and (q == "t" or not sw): continue
                        evs.append(ev)
        return evs

    def note(q, outs, ins, ev):
        for regs, w in ((ins, False), (outs, True)):
            for r in regs:
                L = log.setdefault(r[0], [])
                if r[0] in PSUM: L[:] = [x for x in L if x[2] != q or x[1] != w]
                else: L[:] = [x for x in L if not (covers(r, x[0]) and (w or (not x[1] and x[2] == q and q in "vstg")))]
                L.append((r, w, q, ev))

    def emit(q, outs, ins, call, alone=False):
        wait(q, deps(q, outs, ins, True))
        if q == "g":
            if (alone or cnt["alone"]) and cnt[q]: wait(q, [("cg", cnt[q], {})])
            cnt["alone"] = alone
        cnt[q] += 1
        s = "c" + q
        call().then_inc(T.sem[s], 1)
        total[s] = cnt[q]
        note(q, outs, ins, (s, cnt[q], dict(known[q])))

    def dma(q, out, in_):
        wait(q, deps("d" + q, out[1], in_[1], False))
        s = "dma%d" % cnt["dma"]
        cnt["dma"] += 1
        eng[q].dma_start(out[0], in_[0]).then_inc(T.sem[s], 16)
        total[s] = 16
        note("d" + s, out[1], in_[1], (s, 16, dict(known[q])))

    def send(out, in_, sem, to):
        wait("g", deps("r", [], in_[1], False))
        s = "ls%d" % cnt["ls"]
        cnt["ls"] += 1
        g.remote_dma(out[0], in_[0], T.sem[sem], T.sem[s], to[1], to[0], to[2])
        total[s] = to[3]
        note("r" + s, [], in_[1], (s, to[3], dict(known["g"])))

    def arrive(view, sem, n):
        total[sem] = n
        for r in view[1]: log.setdefault(r[0], []).append((r, True, "x" + sem, (sem, n, {})))

    def finish():
        wait("y", [(s, n, {}) for s, n in sorted(total.items())])

    return emit, dma, send, arrive, finish


def rank_program(g, core, T, topo):
    rank = T.rank_of(core)
    if rank is None: return
    N = len(T.cores)
    A, F = AluOpType, ActivationFunctionType
    emit, dma_now, send_now, arrive, finish = builder(g, T)
    calls = []

    def B(n, lo, cnt, st=1, p=128, p0=0):
        if n in ALIAS: n, lo = ALIAS[n][0], lo + ALIAS[n][1]
        hi = lo + (cnt - 1) * st + 1
        return (T[n][p0:p, lo:hi] if st == 1 else T[n][p0:p, lo:hi:st], [(n, lo, hi, p0, p, st)], cnt, n)

    def like(n, o): return B(n, 0, o[2], 1, o[1][0][4], o[1][0][3])
    def ind(win, off): return (win[0].indirect(off[0]), win[1] + off[1], 16 * off[2], None)
    def num(s): return (s, []) if s is None or isinstance(s, (int, float)) else s
    def short(*x): return 0.5 if all(SCRATCH[a[3]][2] in ("bfloat16", "uint16") for a in x) else 1.0

    def call(q, outs, ins, ns, f, alone=False):
        calls.append([q, outs, ins, {q: (ns, ns)}, {}, lambda _: emit(q, outs, ins, f, alone)])

    def vec(o, a, ins, k, f): call("v", o[1], ins, 50 + GATHER * o[2] if a[3] is None else CYCLE * max(64, k * o[2]), f)
    def tt(o, a, b, op): vec(o, a, a[1] + b[1], 1 if a[3] in PSUM or b[3] in PSUM else 2, lambda: g.vector.tensor_tensor(o[0], a[0], b[0], op))
    def cp(o, a): vec(o, a, a[1], a[3] and short(o, a), lambda: g.vector.tensor_copy(o[0], a[0]))

    def ts(o, a, s1, op0, s2=None, op1=None):
        x, y = num(s1), num(s2)
        if op1 is None: vec(o, a, a[1] + x[1], short(o, a), lambda: g.vector.tensor_scalar(o[0], a[0], x[0], None, op0))
        else: vec(o, a, a[1] + x[1] + y[1], short(o, a), lambda: g.vector.tensor_scalar(o[0], a[0], x[0], y[0], op0, op1))

    def scan(o, a, b, op0, op1): vec(o, a, a[1] + b[1], short(o, a, b), lambda: g.vector.tensor_tensor_scan(o[0], a[0], b[0], 0.0, op0, op1))
    def fill(o, c): vec(o, o, [], short(o), lambda: g.vector.memset(o[0], c))

    def act(o, a, scale=1.0, bias=0.0, fn=None, acc=None):
        x, y = num(scale), num(bias)
        ns = 65 + GATHER * o[2] if a[3] is None else 60 + CYCLE * max(64, o[2])
        if fn is None: fn = F.Copy if not y[1] and y[0] == 0.0 else F.Identity
        if acc is None: call("s", o[1], a[1] + x[1] + y[1], ns, lambda: g.scalar.activation(o[0], a[0], fn, bias=y[0], scale=x[0]))
        else: call("s", o[1] + acc[1], a[1], ns, lambda: g.scalar.activation(o[0], a[0], fn, accum_out=acc[0]))

    def iota(o, pat, base, cm):
        call("g", o[1], [], 130 + 2 * CYCLE * o[2] + (2 * WAKE if o[1][0][3] else 0), lambda: g.iota(o[0], pat, base, cm, allow_small_or_imprecise_dtypes=True), o[1][0][3] > 0)

    def asel(o, a, pat, op, base, cm, c=0.0): call("g", o[1], a[1], 170 + 2 * CYCLE * o[2], lambda: g.affine_select(o[0], a[0], pat, op, c, base, cm))
    def mark(o, a, pat, base, c): asel(o, a, pat, A.not_equal, base, 1, c)

    def either(*ways):
        for f in ways: f()
        L = calls[-len(ways):]
        calls[-len(ways):] = [["any", L[0][1], sum((c[2] for c in L), []), {c[0]: c[3][c[0]] for c in L}, {},
                               lambda q: [c[5](q) for c in L if c[0] == q]]]

    def move(o, a): either(lambda: cp(o, a), lambda: act(o, a))
    def lin(o, a, scale=1.0, bias=0.0): either(lambda: ts(o, a, scale, A.mult, bias, A.add), lambda: act(o, a, scale, bias))

    def const(o, c):
        ways = [lambda: fill(o, c), lambda: act(o, like("ONE", o), c)]
        either(*(ways + [lambda: iota(o, [[0, o[2]]], int(c), 0)] * (c == int(c))))

    def mm(o, l, r, start, stop):
        ns = CYCLE / 2 * max(min(64, l[2]), r[2]) * (4 if SCRATCH[l[3]][2] == "float32" else 1)
        call("t", o[1], l[1] + r[1], ns, lambda: g.tensor.matmul(o[0], l[0], r[0], start, stop))

    def one(k):
        L = calls[-k:]
        ns = sum(c[3]["t"][0] for c in L)
        calls[-k:] = [["t", sum((c[1] for c in L), []), sum((c[2] for c in L), []), {"t": (ns, ns)}, {}, lambda q: [c[5](q) for c in L]]]

    def dma(q, o, a, ns=2000, behind=False):
        calls.append([q + "d", o[1], a[1], {q: (60, ns)}, {len(calls) - 1: 60 - calls[-1][3][q][1]} if behind else {}, lambda _: dma_now(q, o, a)])

    def send(land, a, sem, step):
        dst, src = T.cores[(rank + step) % N], T.cores[(rank - step) % N]
        rid, pid = topo.addr(dst, core)
        lanes = topo.engines(core, dst)[:8]
        calls.append(["gd", [], a[1], {"g": (600, 2000) if sem != "rg" else (2000, 3500)}, {}, lambda _: send_now(land, a, sem, (rid, pid, sum(1 << e for e in lanes), len(lanes)))])
        calls.append(["x", land[1], [], {"x": (0, 1)}, {len(calls) - 1: 0}, lambda _: arrive(land, sem, len(topo.engines(src, core)[:8]))])

    def sq(n, k=128, m=128): return B(n, 0, m, 1, k)
    def lw(n, p): return B("LW", 144 * SHIFTED.index(n) + 15 - p, 128)
    def lwc(n, d=0): return B("LW", 144 * SHIFTED.index(n) + 15 + d, 8, 16)
    def ks(j): return B("KS", 128 * j, 128, 1, 1)

    def dist(o, n, src, base, cols, first=True, last=True):
        for p in range(16): mm(o, lw(n, p), B(src, base + p, cols, 16), first and p == 0, last and p == 15)
        one(16)

    def spread(src, last=False):
        for p in range(16): mm(B("Q", 28 * p, 28), B("DA", 128 * p + 12, 128), src, False, last and p == 15)
        one(16)

    slots = {}

    def slot(buf):
        def f(name, n=1):
            if (buf, name) not in slots:
                slots[(buf, name)] = sum(x[1] for k, x in slots.items() if k[0] == buf), n
            return B(buf, slots[(buf, name)][0] * 28, 28 * n)
        return f

    DF, DN, DU, DB = slot("DF"), slot("DN"), slot("DU"), slot("DB")
    def part(v, j, n=28): return B(v[3], v[1][0][1] + n * j, n)
    def half(v, par): return B(v[3], v[1][0][1] + par, 14, 2)
    cols = {}
    def col(n, p=128): return B("COL", cols.setdefault(n, len(cols)), 1, 1, p)
    def row(r): return B("OH", r, 1)
    def own(t, n=28): return B("V0" if t == 0 else "LD%d" % (t - 1), 0, n)
    def zin(t, lo=16): return B("Z0" if t == 0 else "LZ%d" % (t - 1), lo, M + 16 - lo)
    def gf(t): return B("GF", 240 * (t & 1) + 16, M)
    REC = B("REC", 0, W + 16)
    G8 = B("G8", 0, 8)
    aD = DF("a")
    GROUP = [[-16, 8]]

    def loads():
        dma("s", B("VI", 0, 28), (T.val[:, :], []))
        dma("y", B("GI", 0, V), (T.gl[:, :], []), 2400)
        dma("y", B("NBI", 0, V), (T.nb[:, :], []), 5000, True)
        dma("y", B("Z0", 16, M), (T.zl[:, :], []), 5000, True)
        dma("y", B("THI", 0, M, 1, 8), (T.th[:, :], []), 5000, True)
        dma("y", B("REC", 0, W), (T.rec[:, :], []), 10000, True)

    def neighbours():
        cp(B("NBD", 0, V), B("NBI", 0, V))
        tt(B("NBD", V, V), B("NBI", 0, V), B("NBD", 0, V), A.subtract)
        for r in range(2):
            dma("y", (T["NW"][r:r + 113:16, 0:2 * CELLS], [("NW", 0, 2 * CELLS, r, r + 1, 1)]), B("NBD", r * V, V), 3000)

    def consts():
        fill(B("ONE", 0, V), 1.0)
        fill(B("ZR", 0, 904), 0.0)
        iota(B("IOQ", 0, 1), [[0, 1]], 0, 1)
        iota(B("IO", 0, 16), [[1, 16]], 0, 0)
        iota(B("CR", 0, V, 1, 32), [[0, 16], [1, 28]], 0, 0)
        iota(B("CR", 0, V, 1, 64, 32), [[1, M], [0, 2]], 1, 0)
        iota(B("CR", 0, V, 1, 96, 64), [[1, 16], [0, 28]], 0, 0)
        asel(G8, B("ONE", 0, 8), GROUP, A.is_ge, 0, 1)
        asel(G8, G8, [[16, 8]], A.is_ge, 15, -1)
        for k in range(0, len(SHIFTED), 3): const(B("LW", 144 * k, 144 * min(3, len(SHIFTED) - k)), 0.0)
        for k in range(4): fill(B("DA", 516 * k, 516), 0.0)
        asel(B("DA", 15, 128, 16), B("ONE", 0, 128), [[-1, 16], [-16, 8]], A.is_equal, 0, 1)
        const(B("SLX", 0, 256), 0.0)
        for r, p in ((1, 0), (6, 0), (2, 32), (5, 64)): const(B("SLX", r, 8, 16, p + 1, p), 1.0)
        for n in ("TN", "VT", "Z0", "LZ0", "LZ1"): const(B(n, 0, 16), 0.0)
        const(B("REC", W, 16), 0.0)
        const(B("SB", 0, 192), 0.0)
        const(B("GF", 15, 2, 240), -5.0)
        const(B("SEL", 0, 64), 0.0)
        for n in ("X", "INJ", "TM"): const(B(n, 0, 64), 0.0)
        for j, c in enumerate((-1.0, -0.25, 13.0, 15.0)): const(ks(j), c)
        const(col("c"), 4095.0)
        ts(B("IOQ", 1, 1), B("IOQ", 0, 1), 15, A.bitwise_and)
        cp(col("p"), B("IOQ", 1, 1))
        ts(B("OH", 0, 16), B("IO", 0, 16), col("p"), A.is_equal)
        for n, r, a, b in (("-r0", 0, -1.0, 0.0), ("odd", 3, 2.0, -1.0), ("28r6", 6, 28.0, 0.0), ("no7", 7, -1.0, 1.0), ("2r7", 7, 2.0, 0.0),
                           ("r07", 7, 2.0, row(0)), ("-64r0", 0, -64.0, 0.0)): lin(col(n), row(r), a, b)
        for n, a, b in (("28p", 28.0, 0.0), ("wk", 448.0, 448.0), ("p1", 1.0, 1.0), ("-p", -1.0, 0.0), ("lb", 1.0, 8.0)): lin(col(n), col("p"), a, b)
        for n, d, a in (("L07", 0, 1.0), ("L07", 7, 1.0), ("L64", 0, 64.0), ("LK", 0, col("wk")), ("LK1", 0, col("p1")), ("DP", 0, 1.0),
                        ("DP", 1, 1.0), ("DM", 0, -1.0), ("DM", 1, -1.0)): lin(lwc(n, d), G8, a)
        lin(col("we0"), row(0), 2.0 ** 17, row(2))
        lin(col("we"), row(1), 256.0, col("we0"))
        lin(col("wo"), row(0), 1.0, row(1))
        for n, a in (("LE", col("we")), ("LO", col("wo")), ("L3", row(3))): lin(lwc(n), G8, a)
        mark(sq("IDN"), B("ZR", 0, 128), [[-1, 128]], 0, 1.0)
        for n, c in (("P18", 2.0 ** 18), ("P13", 8192.0), ("P14", 16384.0), ("I16", 16.0), ("HLF", 0.5), ("N1K", -1024.0),
                     ("D00", 1616.0), ("D01", 592.0), ("D10", 1648.0), ("D11", 624.0)):
            either(lambda: ts(sq(n), sq("IDN"), c, A.mult), lambda: act(sq(n), sq("IDN"), c), lambda: mark(sq(n), B("ZR", 0, 128), [[-1, 128]], 0, c))
        mark(sq("K4", 64), B("ZR", 0, 128, 1, 64), [[0, 128]], -32, 4.0)
        iota(sq("D64"), [[0, 128]], 0, 64)
        asel(sq("D64"), sq("D64"), [[-1, 128]], A.is_equal, 0, 1)
        for r in (5, 6, 7): mark(B("I567", r, 8, 16), B("I567", r, 8, 16), GROUP, -r, 1.0)
        mark(sq("R2B"), B("ZR", 0, 128), GROUP + [[0, 16]], -3, 32.0)
        lin(sq("R5B"), sq("R2B"), 18.5)
        asel(sq("BD"), B("ONE", 0, 128), GROUP + [[0, 16]], A.is_ge, 0, 1)
        asel(sq("BD"), sq("BD"), [[16, 8], [0, 16]], A.is_ge, 15, -1)
        lin(sq("B32"), sq("BD"), 32.0)
        for r in (8, 9): mark(B("SL1", 0, 24), B("SL1", 0, 24), [[0, 3]] + GROUP, -r, 4096.0)
        mark(B("SL1", 0, 24), B("SL1", 0, 24), [[-1, 3]] + GROUP, -5, 1.0)
        for n, lo, r, c in (("SL1", 24, 10, 1.0), ("SL2", 0, 3, 1.0), ("S15", 16, 15, 2.0 ** 25)): mark(B(n, lo, 8), B(n, lo, 8), GROUP, -r, c)
        mark(B("THS", 0, 24, 1, 8), B("ZR", 0, 24, 1, 8), [[0, 3], [-1, 8]], 0, 4096.0)
        const(sq("C64"), -64.0)
        asel(sq("UPM", 128, 112), sq("C64", 128, 112), [[1, 112]], A.is_gt, 0, -1)
        mark(sq("UPM", 128, 112), sq("UPM", 128, 112), [[0, 112]], -112, 64.0 * CAP)
        mark(B("IB", 0, 64), B("ZR", 0, 64), [[0, 64]], -112, 1.0)
        for j in range(2):
            for b, c in ((0, 14.0), (1, 256.0), (2, 2.0 ** 17), (4, -2.0 ** 17), (5, 0.5 + 0.5 * j), (12, 0.5)):
                mark(lwc("EE%d" % j), lwc("EE%d" % j), [[-1, 8]], -8 * b, c)
        for n, first, b, c in (("EJ", "ZR", 0, 28.0), ("EJ", "EJ", 1, 1.0), ("EJ", "EJ", 4, 1.0), ("EB", "ZR", 9, 32.0)):
            mark(sq(n), B(first, 0, 128), [[-1, 8], [0, 16]], -8 * b, c)
        for n, w, a, b in (("RAP", V, 8192.0, -2.0 ** 23), ("RAM", V, -8192.0, 2.0 ** 23), ("RAK", 384, 256.0, 1.0 - 2 ** 24)):
            const(B(n, 0, w), a)
            const(B(n, 0, w // 16, 16), b)
        iota(B("RM", 0, H // 2), [[0, 56], [255, 16]], 0, 0)
        iota(DF("c"), [[1, 28]], 0, 0)
        iota(DF("ch"), [[2, 14], [0, 2]], -V, 0)
        iota(DB("cl"), [[0, 14], [1, 2]], 0, 0)
        iota(B("J16", 0, 84), [[16, 3], [0, 28]], 0, 0)
        iota(B("IOX", 0, V), [[1, 28], [28, 16]], 0, 0)
        iota(B("LPI", 0, 24), [[48, 2], [4, 4], [1, 3]], 0, 0)
        iota(B("PP", 0, 384), [[0, 8], [1, 48]], 0, 0)
        iota(B("PC", 0, V), [[1, 28], [0, 16]], 28, 0)
        lin(aD, DF("c"), bias=col("28p"))
        lin(DB("ch"), DF("ch"), bias=col("28p"))
        for n, a, b in (("a37", 32.0, 16.0 * 37), ("a17", 2.0, 17.0), ("a613", 32.0, 16.0 * 613), ("spare", 1.0, 3616.0)): lin(DF(n), aD, a, b)
        cp(B("THB", 0, M, 1, 8), B("THI", 0, M, 1, 8))
        ts(B("LPI", 0, 24), B("LPI", 0, 24), 1, A.arith_shift_right)
        cp(B("LP", 0, 24), B("LPI", 0, 24))
        ts(col("la"), col("p"), 8.0, A.is_ge, 16.0, A.mult)
        ts(B("LC", 0, 28), B("ONE", 0, 28), col("la"), A.mult, col("lb"), A.add)
        ts(B("PP", 0, 384), B("PP", 0, 384), 31, A.bitwise_and)

    def table0():
        for par, bank in enumerate(("Q", "PT")):
            for p in range(16): mm(B(bank, 14 * p, 14), B("DA", 128 * p + 12, 128), half(own(0), par), p == 0, False)
            one(16)
            mm(B(bank, 0, M), sq("SLX", 64), B("CR", par, M, 2, 64), False, False)
            mm(B(bank, 0, M), lw("L07", 0), B("G0", par, M, 2), False, True)
        lin(B("TN", 16, M, 2), B("Q", 0, M), bias=row(0))
        lin(B("TN", 17, M, 2), B("PT", 0, M), col("odd"), col("-r0"))

    def values(t):
        mm(B("Q", 0, V), sq("SLX", 96), B("CR", 0, V, 1, 96), True, False)
        if t < 2: mm(B("Q", 0, V), lw("L07", 0), B("G0", 0, V), False, False)
        spread(own(t), True)
        if t == 2: move(B("VT", 16, V), B("Q", 0, V))
        for par, a, b in (((0, col("no7"), 0.0), (1, 1.0, col("2r7"))), ((0, 1.0, col("r07")), (1, col("no7"), col("-64r0"))), ())[t]:
            lin(B("VT", 16 + par, M, 2), B("Q", par, M, 2), a, b)

    def ghosts(t):
        if t == 0:
            mm(B("K1", 0, V), sq("SLX", 96), B("CR", 0, V, 1, 96), True, True)
            lin(B("VT", V + 16, V), B("K1", 0, V), bias=col("28r6"))
        dma("y", (T["VT"][3:116:16, V + 16:2 * V + 16], [("VT", V + 16, 2 * V + 16, 0, 128, 1)]), B("LG" if t == 0 else "GN%d" % (t - 1), 0, 28), 3000)

    def gather(out, tab, off, lo, n, buf="KW"):
        for c in range(0, n, 28):
            move(B(buf, out + 16 * c, V), ind(B(tab, 0, V + 16), B(off, lo + c, 28)))
            if buf == "NW" and c % 56 == 0: calls[-1].append("v")

    def keys_e(bank, base, n, buf="KW"):
        for p in range(16): mm(B(bank, 0, n), lw("LE", p), B(buf, base + n * p, n), p == 0, p == 15)

    def winners(par, bank):
        scan(B("SE", M * par, M), B("RAP", 0, M), B(bank, 0, M), A.add, A.max)
        ts(half(DN("key2"), par), B("SE", M * par + 15, 14, 16), 0.0, A.max)

    def elected(t):
        par, e = t & 1, DN("e")
        ts(e, DN("key%d" % t), 255, A.bitwise_and)
        ts(DU("z"), e, 15.0, A.add)
        ts(DU("v"), e, 2.0, A.mult, par + 14.0, A.add)
        tt(B("MAT", 0, V), ind(B("GF", 240 * par, 240), DU("z")), B("IOX", 0, V), A.is_equal)
        mm(B("PM", 0, 28), sq("IDN"), DB("ch"), True, False)
        mm(B("PM", 0, 28), sq("IDN"), DB("cl"), False, False)
        dist(B("PM", 0, 28), "LK", "MAT", 0, 28, first=False)
        cp(DB("e"), e)
        lin(DF("u"), DB("e"), 4.0, 13.0 + 2 * par)
        lin(DF("s"), DB("e"), 64.0, 16.0 * (609 + 2 * par))
        tt(DF("m"), DF("u"), aD, A.mult)
        cp(DU("nk"), B("PM", 0, 28))
        ts(DB("no"), B("PM", 0, 28), 0.0, A.is_lt)
        move(B("OG", 0, V), ind(B("NW", 0, 2 * CELLS), DU("nk")))
        dist(B("PM", 32, 28), "LO", "OG", 0, 28)
        ts(DU("o"), B("PM", 32, 28), 16.0, A.add)
        lin(DF("s37"), B("PM", 32, 28), 32.0, 16.0 * 37)
        tt(DF("ob"), B("PM", 32, 28), DF("a17"), A.mult)
        dist(B("K0", 0, 28), "LK1", "MAT", 0, 28, last=False)
        mm(B("K0", 0, 28), sq("I16"), DB("e"), False, False)
        mm(B("K0", 0, 28), sq("P13"), DB("no"), False, True)
        tt(DN("ps"), B("K0", 0, 28), DF("spare"), A.min)
        cp(DU("ps"), DN("ps"))

    def place(u, x):
        ts(x, x, 4, A.arith_shift_right, W - 1, A.bitwise_and)
        cp(u, x)

    def trials(t):
        d, pj, b = own(t), DN("p", 2), DF("b", 3)
        move(B("GD", 0, V), ind(B("TN" if t == 0 else "VT", 0, V + 16), DU("v")))
        dist(B("PD", 0, 28), "L3", "GD", 0, 28)
        move(B("ZE", 0, V), ind(zin(t, 0), DU("z")))
        for j in range(2): ts(part(pj, j), d, j + 1.0, A.add)
        tt(part(b, 0), d, DF("s"), A.mult)
        ts(pj, pj, 15, A.bitwise_and)
        for j in range(2): tt(part(b, j + 1), part(pj, j), DF("s"), A.mult)
        for j in range(3): tt(part(b, j), part(b, j), DF("m"), A.add)
        cp(DB("p", 2), pj)
        tt(DF("q"), B("PD", 0, 28), DF("a37"), A.mult)
        for j in range(3): tt(part(DN("ix", 3), j), part(b, j), DF("q"), A.add)
        place(DU("ix", 3), DN("ix", 3))
        mm(B("PD", 64, 56), sq("IDN"), B("J16", 0, 56), True, False)
        mm(B("PD", 64, 28), sq("IDN"), d, False, False)
        mm(B("PD", 92, 28), sq("IDN"), part(DB("p", 2), 0), False, False)
        mm(B("PD", 92, 28), sq("P18"), DB("no"), False, False)
        one(4)
        mm(B("PN", 464, 28), sq("IDN"), B("J16", 56, 28), True, False)
        mm(B("PN", 464, 28), sq("IDN"), part(DB("p", 2), 1), False, False)
        mm(B("PN", 464, 28), sq("P18"), DB("no"), False, False)
        one(3)
        for j in range(3): tt(B("MT", j * V, V), ind(REC, part(DU("ix", 3), j)), B("ZE", 0, V), A.max)
        dist(B("PD", 64, 56), "L64", "MT", 0, 56, first=False)
        dist(B("PN", 464, 28), "L64", "MT", 2 * V, 28, first=False)
        cp(DF("x"), B("PD", 64, 28))
        tt(DF("x"), B("PD", 92, 28), DF("x"), A.min)
        tt(DN("x"), B("PN", 464, 28), DF("x"), A.min)

    def old_values(t):
        bank, src, st = ("Q", "KW", 16) if t else ("PT", "NW", 32)
        for h in range(2):
            for k in range(16): mm(B(bank, 128 * h + k, 8, 16, 112), B(src, 112 * st * h + k, 112, st), B("SL2", 0, 8), h + k == 0, h + k == 16)
            one(16)
        move(B("PA", 0, 256, 1, 112), B(bank, 0, 256, 1, 112))

    def old_damage(t):
        move(B("VO", 0, V), ind(B("VT", 0, 2 * V + 16), DU("o")))
        dist(B("PM", 64, 28), "L3", "VO", 0, 28)
        tt(DF("ot"), own(t), DF("s37"), A.mult)
        tt(DF("od"), B("PM", 64, 28), DF("a613"), A.mult)
        tt(DF("co"), DF("ob"), DF("od"), A.add)
        tt(DN("io"), DF("ot"), DF("co"), A.add)
        place(DU("io"), DN("io"))
        tt(B("MO", 0, V), ind(REC, DU("io")), B("ZE", 0, V), A.max)

    def choose(t):
        s = str(t)
        ts(DN("nd"), DN("x"), 15, A.bitwise_and)
        tt(DF("nt"), DN("nd"), DF("s37"), A.mult)
        cp(B("MV" + s, 0, 28), DN("nd"))
        tt(DN("in"), DF("nt"), DF("co"), A.add)
        place(DU("in"), DN("in"))
        tt(B("MN", 0, V), ind(REC, DU("in")), B("ZE", 0, V), A.max)
        send(B("LM" + s, 0, 32), B("MV" + s, 0, 32), "rm" + s, -1)
        tt(DB("dl"), DN("nd"), own(t), A.subtract)
        for h, bank in enumerate(("PT", "PS")):
            mm(B(bank, 0, M), sq("I567"), B("VO", M * h, M), True, False)
            for p in range(16): mm(B(bank, p, 14, 16), B("DA", 128 * p + 5, 128), part(DB("dl"), h, 14), False, False)
            one(16)
        for h, bank in enumerate(("PT", "PS")):
            mm(B(bank, 0, M), lw("DM", 8), B("MO", M * h, M), False, False)
            mm(B(bank, 0, M), lw("DP", 8), B("MN", M * h, M), False, True)
            lin(B("T1", M * h, M), B(bank, 0, M), row(9))
            tt(B("PB", M * h, M), B(bank, 0, M), B("T1", M * h, M), A.subtract)
        o, a = ind(B("WD", 0, 4096), DU("ps")), B("PB", 0, V)
        call("v", o[1][:1], o[1][1:] + a[1], 50 + SCATTER * V, lambda: g.vector.tensor_copy(o[0], a[0]))

    def clear():
        for j in range(4): dma("y", B("WD", 904 * j, 904), B("ZR", 0, 904), 8000)

    def members(t): ts(B("GM", (t & 1) * M, M), gf(t), 16.0, A.add)

    def thresholds(t):
        for h in range(2):
            o = B("PN", 24 * h, 24, 1, 112)
            mm(o, B("THB", 112 * h, 112, 1, 8), B("THS", 0, 24, 1, 8), h == 0, False)
            mm(o, B("G0", (t & 1) + M * h, 112, 2), B("S15", 0, 24), False, h == 1)
        one(4)
        lin(B("THC", 0, 48, 1, 112), B("PN", 0, 48, 1, 112), bias=col("c", 112))

    def count():
        for h in range(2): mm(B("PN", 160, 8), B("ONE", 0, 128, 1, 112), B("INJ", 24 * h, 8, 1, 112), h == 0, h == 1)
        act(B("CF", 8, 8), B("PN", 160, 8), acc=B("CF", 0, 1))
        cp(B("CI", 0, 1), B("CF", 0, 1))
        ts(B("CI", 1, 1), B("CI", 0, 1), 31, A.bitwise_and)
        ts(col("c"), B("CI", 1, 1), 4096.0, A.mult, 4095.0, A.add)

    def slot_bases(t):
        par, o, big = t & 1, B("PS", 256, M), -129.0 * 2 ** 15
        either(lambda: ts(B("EM", 0, M), gf(t), big, A.mult, 0.0, A.max), lambda: act(B("EM", 0, M), gf(t), big, fn=F.Relu))
        mm(o, sq("K4", 64), B("CR", par, M, 2, 64), True, False)
        mm(o, ks(2 + par), B("ONE", 0, M, 1, 1), False, False)
        mm(o, sq("R2B"), B("VT", 16 + par, M, 2), False, True)
        tt(B("CC", 0, M), o, gf(t), A.mult)

    def times(o, b, t, h, last):
        for j, n in enumerate(("D64", ("P13", "P14")[h], "D%d%d" % (t & 1, h))):
            mm(o, B("PA", 256 * b + 128 * h, 128, 1, 112), sq(n, 112, 112), False, last and j == 2)
        one(3)

    def slot_open(t):
        for h in range(2):
            o = B(("PD", "PM")[h], 256, 112)
            mm(o, sq("IDN"), B("EM", 112 * h, 112), True, False)
            mm(o, sq("R5B"), B("VT", 16 + (t & 1) + M * h, 112, 2), False, False)
            times(o, 0, t, h, False)

    def keys(t, h):
        K, o, x = "K%d" % h, B(("PD", "PM")[h], 256, 112), B("XI", 112 * h, 112)
        for k in range(16): mm(B(K, k, 32, 16, 112), B("WD", H * h + k + 17, 112, 16), B("SL1", 0, 32), k == 0, k == 15)
        one(16)
        n = 384 if t < 2 else 256
        for j in (h, 1 - h):
            if j: scan(B("SC", 384 * h, n, 1, 112), B("RAK", 0, n, 1, 112), B(K, 0, n, 1, 112), A.add, A.max)
            else: move(B("PA", 256 + 128 * h, 128, 1, 112), B(K, 384, 128, 1, 112))
        times(o, 1, t, h, True)
        tt(x, o, B("CC", 112 * h, 112), A.add)
        ts(x, x, 4, A.arith_shift_right, W - 1 + 2 ** 18, A.bitwise_and)
        ts(B("ISL", 112 * h, 112), x, float(W), A.min)

    def injured(t):
        top = B("SC", 15, 48, 16, 112)
        ts(B("TI", 0, 48, 1, 112), top, 0.0, A.max)
        tt(B("INJ", 0, 48, 1, 112), top, B("THC", 0, 48, 1, 112), A.is_gt)
        ts(B("TI", 48, 48, 1, 112), B("TI", 0, 48, 1, 112), 255, A.bitwise_and)
        tt(B("X", 0, 48, 1, 112), B("TI", 48, 48, 1, 112), B("INJ", 0, 48, 1, 112), A.mult)
        ts(B("IB", 0, 48, 1, 112), B("X", 0, 48, 1, 112), 28.0, A.is_ge)
        mm(B("PN", 64, 48, 1, 112), sq("UPM", 113, 112), B("IB", 0, 48, 1, 113), True, False)
        mm(B("PN", 88, 24, 1, 112), sq("C64", 112, 112), B("IB", 0, 24, 1, 112), False, True)
        one(2)
        tt(B("OHP", 0, 384), ind(B("X", 0, 64), B("LP", 0, 24)), B("PP", 0, 384), A.is_equal)
        tt(B("TM", 0, 48, 1, 112), B("PN", 64, 48, 1, 112), B("X", 0, 48, 1, 112), A.min)
        tt(B("OHC", 0, V), ind(B("TM", 0, 64), B("LC", 0, 28)), B("PC", 0, V), A.is_equal)

    def notices(t):
        s = str(t)
        for q in range(4):
            for j in range(4):
                gg, h = j >> 1, j & 1
                mm(B("PN", 128, 28, 1, 32 * q + 32, 32 * q), B("OHP", 48 * (4 * h + q) + 16 * gg, 32, 1, 112),
                   B("OHC", 8 * h + 2 * q + gg, 28, 16, 112), j == 0, j == 3)
        one(16)
        tt(DN("gn"), B("PN", 128, 28), B("LM" + s, 0, 28), A.add)
        ts(DN("gn"), DN("gn"), 15, A.bitwise_and)
        cp(B("GN" + s, 0, 28), DN("gn"))
        n = 32 if t < 2 else 28
        send(B("LD" + s, 0, n), B("GN" + s, 0, n), "rd" + s, 1)

    def turn(t):
        for h in range(2):
            for b, (n, lo) in enumerate((("X", 0), ("INJ", 0), ("IB", 0), ("X", 8))):
                mm(B("K0", 112 * h, 112, 1, 32 * b + 32, 32 * b), B(n, 24 * h + lo, 32, 1, 112), sq("IDN", 112, 112), True, True)
        one(8)
        move(B("XT", 0, M), B("K0", 0, M))

    def patch(t):
        par = t & 1
        for p in range(16): mm(B("PD", 192 + par, 14, 2), lw("EE%d" % t, p), B("XT", 14 * p, 14), p == 0, p == 15)
        one(16)
        k = half(DN("key%d" % (t + 1)), par)
        tt(k, B("PD", 192 + par, 14, 2), k, A.max)

    def joins(t):
        def name(lo, last):
            mm(B("K1", lo, M), sq("EJ"), B("XT", 0, M), True, False)
            mm(B("K1", lo, M), ks(0), B("ONE", 0, M, 1, 1), False, last)
        name(0, True)
        mm(B("K0", 256, M), sq("BD"), B("G0", t & 1, M, 2), True, False)
        mm(B("K0", 256, M), sq("EB"), B("XT", 0, M), False, False)
        tt(B("EQ", 0, M), B("K1", 0, M), gf(t), A.is_equal)
        mm(B("K0", 256, M), sq("B32"), B("EQ", 0, M), False, True)
        name(256, False)
        either(lambda: ts(B("A2", 0, M), B("K0", 256, M), col("p"), A.not_equal), lambda: act(B("A2", 0, M), B("K0", 256, M), bias=col("-p"), fn=F.Abs))
        mm(B("K1", 256, M), sq("N1K"), B("A2", 0, M), False, True)
        tt(B("YL", t & 1, M, 2) if t else gf(t), B("K1", 256, M), gf(t), A.max)
        if t == 0: either(lambda: ts(B("G0", 0, M, 2), gf(0), 0.0, A.is_ge), lambda: act(B("G0", 0, M, 2), gf(0), bias=1.0, fn=F.Sign))

    def levels(t):
        s = str(t)
        for c in range(0, M, 28): move(B("WR", 16 * c, V), ind(REC, B("ISL", c, 28)))
        for c in range(0, M, 56): scan(B("KT", 16 * c, 896), B("RM", 0, 896), B("WR", 16 * c, 896), A.min, A.max)
        mm(B("PS", 0, M), sq("HLF"), zin(t), True, False)
        mm(B("PS", 0, M), ks(1), B("ONE", 0, M, 1, 1), False, False)
        mm(B("PS", 0, M), sq("HLF"), B("KT", 15, M, 16), False, True)
        ts(B("ZB" + s, 0, M), B("PS", 0, M), ROUND, A.add, -ROUND, A.add)
        send(B("LZ" + s, 16, M), B("ZB" + s, 0, M), "rz" + s, 1 + t)

    loads()
    consts()
    ts(B("GU", 0, V), B("GI", 0, V), 16.0, A.add)
    for par in range(2):
        ts(B("G0", par, M, 2), B("GI", par, M, 2), 0.0, A.is_ge)
        cp(gf(par), B("GI", par, M, 2))
    cp(B("V0", 0, 28), B("VI", 0, 28))
    send(B("LG", 0, 32), B("V0", 0, 32), "rg", -1)
    table0()
    clear()
    ghosts(0)
    gather(0, "TN", "GU", 0, V, "NW")
    keys_e("K0", 0, V, "NW")
    old_values(0)
    neighbours()
    scan(B("SE", 0, V), B("RAP", 0, V), B("K0", 0, V), A.add, A.max)
    ts(DN("key0"), B("SE", 15, 28, 16), 0.0, A.max)
    scan(B("SE", V, V), B("RAM", 0, V), B("K0", 0, V), A.add, A.min)
    ts(DN("key1"), B("SE", V + 15, 28, 16), -1.0, A.mult, 0.0, A.max)
    members(1)
    elected(0)
    for t in range(RO):
        values(t)
        if t: gather(0, "VT", "GM", (t & 1) * M, M)
        if t == 1: gather(CELLS, "VT", "GM", 0, M)
        trials(t)
        thresholds(t)
        slot_bases(t)
        if t: old_values(t)
        old_damage(t)
        slot_open(t)
        if t == 1:
            keys_e("K0", 0, M)
            winners(1, "K0")
            keys_e("Q", CELLS, M)
            winners(0, "Q")
        choose(t)
        keys(t, 0)
        keys(t, 1)
        if t < 2: clear()
        injured(t)
        notices(t)
        turn(t)
        if t < 2:
            ghosts(t + 1)
            patch(t)
        joins(t)
        if t < 2:
            elected(t + 1)
            count()
        levels(t)
        if t == 0: members(2)
    dma("y", (T.yl[:, :], []), B("YL", 0, V))
    dma("y", (T.yd[:, :], []), B("LD2", 0, 28))
    dma("y", (T.yz[:, :], []), B("LZ2", 16, M))
    if not PLAN: PLAN.extend(order(calls))
    for _, n, q in PLAN: calls[n][5](q)
    finish()
